import numpy as np, ml_dtypes
CORES = [13,21,141,149]
N = 4
BF = ml_dtypes.bfloat16
def gentries(a):
    return np.ascontiguousarray(a.reshape(8, 16, -1).transpose(0, 2, 1)).reshape(8, -1)
def gtable(e):
    e = np.asarray(e); return np.ascontiguousarray(e.reshape(8, -1, 16).transpose(0, 2, 1)).reshape(128, -1).astype(np.int32)
V, G, BL, K, CAP, HO, RO = 1280, 512, 320, 1024, 256, 2, 2
W = V + G; CL = RO + 1; OWN = np.arange(V); LO = BL * (OWN // BL + 1)
def glists(a):
    return np.stack([gentries(x) for x in a]).astype(np.int64)
def pick(x, i):
    return np.take_along_axis(x, i[:, :, None, :], 3)
def reals(rng, top):
    return (0.5 + (top - 0.5) * rng.random((N, 8, 16, V))) * np.exp2(rng.integers(-1, 2, (N, 8, 1, V)))
def later(rng):
    r = rng.random((N, 8, V)); r = np.where(rng.random((N, 8, V)) < 0.5, r, r * r * r)
    return np.minimum(LO + ((W - LO) * r).astype(np.int64), W - 1)
def parts(rng):
    d = dict(a=rng.integers(-127, 128, (N, 8, 16, V)), b=rng.integers(-127, 128, (N, 8, 16, V)), h=reals(rng, 1.0), u=rng.integers(0, 256, (N, 8, 16, K)), v=rng.integers(0, 256, (N, 8, 16, K)))
    d["n0"] = later(rng); d["n1"] = later(rng); d["s"] = rng.integers(0, K, (N, 8, V))
    share = rng.permutation(np.array([0.1, 0.1, 0.2, 0.2, 0.35, 0.35, 0.5, 0.5])).reshape(1, 8, 1)
    d["f"] = np.where(rng.random((N, 8, K)) < share, rng.integers(V, W, (N, 8, K)), rng.integers(0, V, (N, 8, K)))
    d["th"] = rng.integers(60, 111, (N, 8, 1, RO)) + rng.integers(-15, 16, (N, 8, 16, RO))
    return d
def pack(d):
    o = {}
    for k, x, n in (("ta", "a", V), ("tb", "b", V), ("h0", "h", V), ("u0", "u", K), ("v0", "v", K)):
        o[k] = np.ascontiguousarray(d[x].reshape(N, 128, n)).astype(np.float32).astype(BF)
    for k, x in (("na", "n0"), ("nb", "n1"), ("sd", "s"), ("pf", "f")): o[k] = np.stack([gtable(e) for e in d[x]])
    o["th"] = np.ascontiguousarray(d["th"].reshape(N, 128, RO)).astype(np.int32)
    return o
def setup_inputs(rng):
    return pack(parts(rng))
def setup_inputs_spread(rng):
    d = parts(rng); d["h"] = reals(rng, 2.0)
    d["u"] = (256 * rng.random((N, 8, 16, K)) ** rng.integers(1, 5, (N, 8, 1, K))).astype(np.int64)
    d["u"] = np.minimum(d["u"], 255)
    d["th"] = np.clip(rng.choice(np.array([5, 40, 80, 120, 250]), (N, 8, 1, RO)) + rng.integers(-40, 41, (N, 8, 16, RO)), 0, 255)
    return pack(d)
def setup_inputs_ends(rng):
    d = parts(rng)
    def two(lo, hi, n):
        e = rng.integers(0, 2, (N, 8, 16, n)); r = rng.integers(0, 2, (N, 8, 1, n))
        return np.where(np.where(rng.random((N, 8, 1, n)) < 0.5, r, e) == 1, hi, lo)
    d["a"] = two(-127, 127, V); d["b"] = two(-127, 127, V); d["h"] = two(0.25, 4.0, V); d["u"] = two(0, 255, K); d["v"] = two(0, 255, K); d["th"] = two(0, 255, RO)
    for k in ("n0", "n1"): d[k] = np.where(rng.random((N, 8, V)) < 0.75, W - 1, LO)
    d["s"] = np.where(rng.random((N, 8, V)) < 0.5, 0, K - 1)
    d["f"] = np.where(rng.random((N, 8, K)) < 0.7, np.where(rng.random((N, 8, K)) < 0.5, 0, W - 1), rng.integers(0, W, (N, 8, K)))
    d["th"][:, 0] = 255; d["th"][:, 6:, :, 0] = 255
    for g, s, w in ((7, 127, 255), (6, -127, 0)):
        d["a"][:, g, :, 0] = s; d["a"][:, g, :, V - 1] = s; d["b"][:, g, :, 0] = s
        for p in (1, K - 1): d["u"][:, g, :, p] = w; d["v"][:, g, :, p] = 255; d["f"][:, g, p] = 0
    d["n1"][:, 6:, 0] = BL
    L = V - 1 - (V - RO) % CL; d["th"][:, 6:, :, RO - 1] = 255
    for g, s, w in ((7, 127, 255), (6, -127, 0)):
        d["a"][:, g, :, L] = 0; d["b"][:, g, :, L] = s
        d["u"][:, g, :, K - 2] = 255; d["v"][:, g, :, K - 2] = w; d["f"][:, g, K - 2] = L
    return pack(d)
def setup_inputs_corners(rng):
    d = parts(rng); rest = OWN[OWN % CL == RO]; far = V + np.arange(RO, G, CL)
    n = np.array([0, 1, CAP - 1, CAP, CAP + 1, K, RO * CAP - 1, CAP])
    for g in range(8):
        q = int(rng.integers(N))
        for r in range(N):
            k = int(n[g])
            if r != q: k = K if g == 6 else int(rng.choice(np.array([k, min(k + 1, K), K])))
            if g == 6: gh = rng.choice(far, k)
            else: gh = np.where(rng.random(k) < 0.5, rng.integers(V, W, k), rng.choice(np.array([V, W - 1]), k))
            d["f"][r, g] = rng.permutation(np.concatenate([gh, rng.choice(rest, K - k)]))
    d["s"][:, 2] = K - 1; d["s"][:, 4] = K - 1; d["s"][:, 4, 0] = 0; d["s"][:, 3] = rng.choice(np.array([0, 1, K - 2, K - 1]), (N, V))
    t = rng.integers(20, 101, (N, 8, 16, 1)); d["th"] = np.repeat(t, RO, axis=3)
    c = rng.choice(np.array([0, 1, 8, 9, 15, 16]), (N, 8, 1, V)); at = (np.argsort(rng.random((N, 8, 16, V)), axis=2) < c).astype(np.int64)
    e = t + 1 - at; x = pick(d["u"], d["s"]) - 128
    d["a"] = np.where(x - e >= -127, x - e, x + e)
    return pack(d)
def setup_inputs_calm(rng):
    d = parts(rng); rest = OWN[OWN % CL == RO]; far = V + np.arange(RO, G, CL)
    c = ((0, 1, 2, 3, 0, 0, 1, 2), (0, 0, 0, 0, 1, 2, 1, 1), (0, 1, 0, 0, 0, 1, 1, 0))
    d["f"][..., :16] = rng.choice(far, (N, 8, 16))
    for g in range(8):
        q = int(rng.integers(N)); w = rng.choice(rest, K); at = rng.permutation(K); j = c[0][g]
        w[at[:j]] = rng.choice(far, j)
        for t in range(1, RO):
            k = c[t][g]; e = rng.choice(OWN[OWN % CL == t], k); w[at[j:j + k]] = e; j += k
            d["n0"][q, g, e] = rng.choice(far, k); d["n1"][q, g, e] = rng.choice(far, k); d["th"][q, g, :, t] = 255
        d["f"][q, g] = w
    return pack(d)
def setup_inputs_chains(rng):
    d = parts(rng); nxt = LO + (OWN - LO) % CL
    d["n0"][:, :4] = nxt; d["n1"][:, 2:6] = nxt; d["th"][:, ::2] = 255; d["th"][:, 5] = 0
    d["f"] = np.where(rng.random((N, 8, K)) < 0.6, rng.integers(0, BL, (N, 8, K)), d["f"])
    z = rng.random((N, 8, 1, V)) < 0.33; d["a"] = np.where(z, 0, d["a"]); d["b"] = np.where(z, 0, d["b"])
    c = rng.choice(np.array([0, 8, 9, 16]), (N, 8, 1, K)); tie = (np.argsort(rng.random((N, 8, 16, K)), axis=2) < c).astype(np.int64)
    d["u"] = np.minimum(d["u"], 254); d["v"] = np.where(rng.random((N, 8, 1, K)) < 0.5, d["u"] + 1 - tie, d["v"])
    d["f"][:, 4] = 0; d["f"][:, 4, K - 1] = V - 1
    d["s"][:, 1] = 0; d["s"][:, 3] = K - 1; d["s"][:, 3, V - 1] = 0
    return pack(d)
def check_ranges(d):
    bad = []
    for k, lo, hi in (("ta", -127, 127), ("tb", -127, 127), ("u0", 0, 255), ("v0", 0, 255), ("na", BL, W - 1), ("nb", BL, W - 1), ("sd", 0, K - 1), ("pf", 0, W - 1), ("th", 0, 255)):
        x = np.asarray(d[k]).astype(np.float64)
        if not np.all((x >= lo) & (x <= hi) & (x == np.floor(x))): bad.append("range of " + k)
    y = np.asarray(d["h0"]).astype(np.float64)
    if not np.all((y >= 0.25) & (y <= 4)): bad.append("range of h0")
    for k in ("na", "nb"):
        if not np.all(glists(d[k]) >= LO): bad.append("blocks of " + k)
    return bad
def reference(ta, tb, h0, u0, v0, na, nb, sd, pf, th):
    a = ta.astype(np.float32).astype(np.int64).reshape(N, 8, 16, V); b = tb.astype(np.float32).astype(np.int64).reshape(N, 8, 16, V)
    u = u0.astype(np.float32).astype(np.int64).reshape(N, 8, 16, K); v = v0.astype(np.float32).astype(np.int64).reshape(N, 8, 16, K)
    h = h0.astype(np.float64).reshape(N, 8, 16, V); limit = th.astype(np.int64).reshape(N, 8, 16, RO)
    n0, n1, s, face = glists(na), glists(nb), glists(sd), glists(pf)
    dead = np.zeros((N, 8, W), bool); shift = np.zeros(8, np.int64)
    for t in range(RO):
        w = np.concatenate([h, np.roll(h, -1, axis=0)[..., :G]], axis=3)
        x = pick(u, (s + shift[None, :, None]) & (K - 1))
        count = np.add.reduce((np.abs(x - 128 - a) <= limit[..., t:t + 1]).astype(np.int64), axis=2)
        dead[..., :V] |= (OWN % CL == t) & (count >= 9)
        for hop in range(HO):
            go = np.take_along_axis(dead, face, 2); fi = np.minimum(face, V - 1)
            un = (u + pick(a, fi) * v) & 255; vn = (v + pick(b, fi) * un) & 255
            u = np.where(go[:, :, None, :], un, u); v = np.where(go[:, :, None, :], vn, v)
            count = np.add.reduce((u >= v).astype(np.int64), axis=2)
            to = np.where(count >= 9, np.take_along_axis(n0, fi, 2), np.take_along_axis(n1, fi, 2))
            face = np.where(go, to, face)
        on = face >= V
        m = np.minimum(np.min(np.add.reduce(on.astype(np.int64), axis=2), axis=0), CAP)
        nu, nv, nf = u.copy(), v.copy(), face.copy()
        for g in range(8):
            at = [np.flatnonzero(on[r, g])[:int(m[g])] for r in range(N)]
            for r in range(N):
                e = (r + 1) % N
                nu[e, g][:, at[e]] = u[r, g][:, at[r]]; nv[e, g][:, at[e]] = v[r, g][:, at[r]]; nf[e, g, at[e]] = face[r, g, at[r]] - V
        u, v, face = nu, nv, nf; shift = shift + m
        x = pick(u, (s + shift[None, :, None]) & (K - 1))
        w[..., :V] = 0.5 * (h + x * 0.015625 - 2.0)
        for k in range(V // BL - 1, -1, -1):
            c = slice(k * BL, (k + 1) * BL)
            y = (a[..., c] * pick(w, n0[..., c]) + b[..., c] * pick(w, n1[..., c])) * 0.00390625
            w[..., c] = np.where(dead[:, :, None, c], y, w[..., c])
        h = w[..., :V]
    z = ((u - 128) * (v - 128)) * 2.0 ** -13
    p = pick(w, face) * (0.5 * (1.0 + np.tanh(0.5 * z)))
    yh = np.add.reduce(h.reshape(N, 8, 16, V // BL, BL), axis=3)
    return {"yh": yh.reshape(N, 128, BL).astype(np.float32), "yw": (p[..., :K // 2] + p[..., K // 2:]).reshape(N, 128, K // 2).astype(np.float32)}

def check_inputs(d):
    bad = list(check_ranges(d))
    if not bad:
        for name, y in reference(**d).items():
            for q in range(N):
                v = np.abs(np.asarray(y[q], np.float64)); s = np.sqrt(np.mean(v * v))
                if v.max() > 8 * s or s < 2.0 ** -3: bad.append('%s of rank %d is uneven or too small' % (name, q))
    return bad

@@ -1,0 +1,752 @@
+from concourse.bass import DstId, RemoteDMATransfer
+from concourse.mybir import AluOpType as OP, AxisListType, ActivationFunctionType as AF
+
+NCORES = 256
+V, GH, BL, K, CAP = 1280, 512, 320, 1024, 256
+W = V + GH
+SUB = 432
+OFF = 131072.0
+BF, F32, I32, U16 = "bfloat16", "float32", "int32", "uint16"
+
+_SB = {
+    "li": (I32, 320), "lf": (F32, 244), "sall": (F32, 108), "si": (I32, 108), "sj": (I32, 108),
+    "so0": (U16, 108), "so1": (U16, 80), "su0": (U16, 28),
+    "du0": (U16, 56), "du1": (U16, 56), "gu": (U16, 128), "nsb": (F32, 112), "ab": (BF, 2048), "pq": (F32, 2048),
+    "dtmp": (F32, 56), "row48": (F32, 56),
+    "jrow": (F32, 272), "j3": (F32, 128), "jg": (F32, 128), "pi": (I32, 4), "col": (F32, 32), "tb7": (F32, 8),
+    "pm": (F32, 768), "bo": (BF, 128), "tri": (BF, 128), "idb": (BF, 128), "idn": (BF, 128), "id16": (BF, 128),
+    "idf": (F32, 128), "da": (BF, 128), "db": (BF, 128),
+    "z1": (BF, 144), "zm": (BF, 144), "zd": (BF, 144), "zl": (BF, 144), "c256": (BF, 64), "one": (F32, 80),
+    "rst": (BF, 1280), "klist": (F32, 16), "thf": (F32, 2),
+    "a": (BF, 1296), "b": (BF, 1296), "h": (BF, V), "u": (BF, 2560), "v": (BF, 2560),
+    "ae": (BF, W), "be": (BF, W), "ne": (BF, W), "tp": (BF, W),
+    "ga": (BF, SUB), "gb": (BF, SUB), "ns0": (BF, SUB), "ns1": (BF, SUB),
+    "cd": (F32, SUB), "ce": (BF, SUB), "cs": (BF, SUB), "live0": (BF, SUB), "live1": (BF, SUB),
+    "coff": (BF, 256), "idh": (BF, 128), "idg": (F32, 128), "xs": (BF, V), "zr": (F32, 256),
+    "t0": (F32, K), "t1": (F32, K), "r0": (F32, 512), "r1": (F32, 512),
+    "g0": (BF, 512), "g1": (BF, 512), "sg0": (BF, 512), "sg1": (BF, 512),
+    "ss": (F32, 64), "se": (F32, 64), "fl": (F32, 64), "fu": (U16, 64),
+    "on": (BF, 80), "ci": (F32, 80), "cb": (BF, 160), "key": (F32, 80), "keyon": (F32, 80), "key2": (F32, 64),
+    "kt": (F32, 64), "flm": (F32, 80), "flq": (F32, 64), "flg": (BF, 1280), "cq": (BF, 1280), "cu": (U16, 16),
+    "oh": (BF, 256), "atu": (U16, 16), "az": (F32, 16), "a2": (F32, 16), "a2u": (U16, 16),
+    "cn": (F32, 16), "mm": (F32, 2), "nf": (F32, 64), "pre": (F32, 64),
+    "sn0": (BF, 768), "sn1": (BF, 768), "rc0": (BF, 768), "rc1": (BF, 768),
+    "dd0": (BF, 2560), "dd1": (BF, 2560), "up0": (BF, K), "up1": (BF, 2560),
+    "hg": (BF, GH), "w0": (F32, W), "w1": (F32, W),
+    "zz": (F32, K), "sig": (F32, 2560), "plo": (F32, 512), "phi": (F32, 512),
+    "oh2": (F32, BL), "ow": (F32, 512),
+    "yb": (BF, 640), "yf": (F32, 136),
+}
+SCRATCH = {n: ("sbuf", [128, w], d) for n, (d, w) in _SB.items()}
+for _n in ("x0", "x1", "x2", "x3", "d0", "d1", "s0", "s1"):
+    SCRATCH[_n] = ("psum", [128, 512], F32)
+
+_LOADS = ["sd", "u0", "ta", "th", "pf", "na", "nb", "v0", "tb", "h0"]
+_MSGS = ["hs0", "ct0", "fm0", "uv0", "hs1", "ct1", "fm1", "uv1"]
+SEMAPHORES = (["ev", "es", "et", "eg", "sent"] + ["l_" + n for n in _LOADS] + ["st0", "st1", "st2"]
+              + ["y_" + m for m in _MSGS] + ["a_hs0", "a_hs1", "a_ct0", "a_ct1", "a_fm0", "a_fm1", "a_u0", "a_v0", "a_u1", "a_v1"])
+
+CY, PCY, GAT, SCA = 0.001, 0.0006, 1.55, 3.2
+LAT_X, LAT_S = 0.12, 0.08
+T_RELAY, T_CNT = 4.5, 4.0
+TRIES, SEED = 2500, 12345
+
+
+def _two(x):
+    return _SB.get(x[0], (F32,))[0] in (BF, U16)
+
+
+def _psum(x):
+    return x[0] not in _SB
+
+
+def _n(x):
+    if x[0] == "@":
+        return 16 * _n(x[2])
+    return len(range(x[1], x[2], x[3]))
+
+
+def R(name, a=0, b=None, s=1):
+    if b is None:
+        b = _SB[name][1] if name in _SB else 512
+    return (name, a, b, s)
+
+
+def C(name, c):
+    return (name, c, c + 1, 1)
+
+
+def IND(win, off):
+    return ("@", win, off)
+
+
+class Plan:
+    pass
+
+
+def build():
+    nodes = []
+    tag = [0]
+
+    def regs(xs):
+        o = []
+        for x in xs:
+            if isinstance(x, tuple):
+                o += [x[1], x[2]] if x[0] == "@" else [x]
+        return o
+
+    def add(eng, kind, args, out, ins, dur, lat=0.0, after=()):
+        rd = regs(ins)
+        wr = []
+        for x in out:
+            if x[0] == "@":
+                wr.append(x[1]); rd.append(x[2])
+            else:
+                wr.append(x)
+        nodes.append(dict(eng=eng, kind=kind, args=args, rd=rd, wr=wr, dur=dur, lat=lat, after=list(after), id=len(nodes),
+                          tag=tag[0]))
+        return len(nodes) - 1
+
+    def vdur(out, ins, per):
+        if out[0] == "@":
+            return 0.05 + CY * SCA * _n(out)
+        if ins[0][0] == "@":
+            return 0.05 + CY * GAT * _n(out)
+        return 0.02 + CY * max(64, per * _n(out))
+
+    def tt(out, x, y, op):
+        return add("v", "tt", (out, x, y, op), [out], [x, y], vdur(out, [x], 1 if x[0] == "@" or _psum(x) or _psum(y) else 2))
+
+    def ts(out, x, s1, op0, s2=None, op1=None):
+        per = 0.5 if x[0] != "@" and _two(x) and _two(out) else 1
+        return add("v", "ts", (out, x, s1, s2, op0, op1), [out], [x, s1, s2], vdur(out, [x], per))
+
+    def cp(out, x):
+        per = 0.5 if x[0] != "@" and out[0] != "@" and _two(x) and _two(out) else 1
+        return add("v", "cp", (out, x), [out], [x], vdur(out, [x], per))
+
+    def ms(out, c):
+        return add("v", "ms", (out, c), [out], [], vdur(out, [out], 0.5 if _two(out) else 1))
+
+    def scan(out, d0, d1, init):
+        per = 0.5 if _two(out) and _two(d0) and _two(d1) else 1
+        return add("v", "scan", (out, d0, d1, init), [out], [d0, d1], vdur(out, [d0], per))
+
+    def rmin(out, x):
+        return add("v", "rmin", (out, x), [out], [x], 0.09)
+
+    def act(out, x, f, bias=0.0, scale=1.0, extra=0.0):
+        d = 0.065 + CY * (GAT * _n(out) if x[0] == "@" else max(64, _n(out))) + extra
+        return add("s", "act", (out, x, f, bias, scale), [out], [x, bias, scale], d)
+
+    def mm(out, pairs, start=True, stop=True):
+        d = sum(PCY * max(64, _n(r)) * (1 if _two(r) else 4) for l, r in pairs) + 0.05
+        return add("t", "mm", (out, pairs, start, stop), [out], [x for p in pairs for x in p], d)
+
+    def ext(out, z, src, n, more=()):
+        return mm(out, [(R(z, 15 - i, 143 - i), R(src[0], src[1] + i, src[1] + 16 * n, 16)) for i in range(16)] + list(more))
+
+    def iota(out, pat, base, cm):
+        return add("g", "iota", (out, pat, base, cm), [out], [], 0.13 + 2 * CY * _n(out))
+
+    def load(q, name, out, kb):
+        return add(q, "load", (name, out), [out], [], 0.06, lat=1.9 + kb / 300.0)
+
+    def store(q, sem, name, a, b, src):
+        return add(q, "store", (sem, name, a, b, src), [], [src], 0.06, lat=2.2)
+
+    def send(msg, ins):
+        return add("g", "send", (msg,), [], ins, 0.6)
+
+    def arrive(sem, out, snd, lat):
+        return add("a", "arrive", (sem,), out, [], 0.0, lat=lat, after=[snd])
+
+    load("y", "sd", R("li", 0, 80), 40)
+    load("s", "ta", R("a", 0, V), 320)
+    load("y", "u0", R("u", 0, K), 300)
+    load("s", "th", R("li", 304, 306), 330)
+    load("y", "pf", R("li", 240, 304), 340)
+    load("y", "v0", R("v", 0, K), 600)
+    load("s", "na", R("li", 80, 160), 380)
+    load("s", "nb", R("li", 160, 240), 420)
+    load("y", "tb", R("b", 0, V), 900)
+    load("y", "h0", R("h"), 1200)
+
+    LANE, G16, Q3, PF, ODD, EVEN, WM, WD, MA, MB, L3, TMP = range(12)
+    iota(C("pi", 0), [[0, 1]], 0, 1)
+    iota(R("j3"), [[64, 8], [3, 16]], 0, 0)
+    iota(R("jg"), [[16, 8], [0, 16]], 0, 0)
+    iota(R("jrow"), [[1, 272]], 0, 0)
+    iota(R("row48", 0, 54), [[0, 2], [48, 27]], 0, 0)
+    ts(C("pi", 1), C("pi", 0), 15, OP.bitwise_and)
+    cp(C("col", LANE), C("pi", 1))
+    cp(C("col", PF), C("pi", 0))
+    tt(C("col", G16), C("col", PF), C("col", LANE), OP.subtract)
+    ts(C("col", Q3), C("col", G16), 4.0, OP.mult, C("col", LANE), OP.add)
+    for t in range(2):
+        for e in range(3):
+            ts(R("pm", 128 * (3 * t + e), 128 * (3 * t + e + 1)), R("j3"), C("col", Q3), OP.subtract, float(16 * e - t), OP.is_equal)
+    ts(R("bo"), R("jg"), C("col", G16), OP.is_equal)
+    tag[0] = -1
+    ts(C("pi", 2), C("pi", 0), 1, OP.bitwise_and)
+    cp(C("col", ODD), C("pi", 2))
+    ts(C("col", EVEN), C("col", ODD), -256.0, OP.mult, 256.0, OP.add)
+    ts(R("tb7"), R("jrow", 0, 8), C("col", EVEN), OP.mult)
+    for s in range(7):
+        act(R("tp", 256 * s, 256 * s + 256), R("jrow", 0, 256), AF.Identity, bias=C("tb7", s), scale=C("col", ODD))
+    tag[0] = 0
+    ts(C("col", MA), C("col", LANE), 2.0, OP.is_lt)
+    ts(C("col", WM), C("col", LANE), 4.0, OP.is_lt, 0.5, OP.mult)
+    tt(C("col", WD), C("col", MA), C("col", WM), OP.subtract)
+    ts(C("col", MB), C("col", WM), 2.0, OP.mult, C("col", MA), OP.subtract)
+    ts(C("col", L3), C("col", LANE), 3.0, OP.mult)
+    ts(R("idb"), R("jrow", 0, 128), C("col", PF), OP.is_equal)
+    ts(R("idf"), R("jrow", 0, 128), C("col", PF), OP.is_equal)
+    ts(R("idn"), R("idb"), -1.0, OP.mult)
+    ts(R("id16"), R("idb"), 16.0, OP.mult)
+    ts(R("da"), R("idb"), C("col", MA), OP.mult)
+    ts(R("db"), R("idb"), C("col", MB), OP.mult)
+    ts(R("z1"), R("jrow", 0, 144), C("col", G16), OP.subtract, 15.0, OP.is_equal)
+    ts(R("zm"), R("z1"), C("col", WM), OP.mult)
+    ts(R("zd"), R("z1"), C("col", WD), OP.mult)
+    ts(R("zl"), R("z1"), C("col", LANE), OP.mult)
+    add("g", "asel", (R("tri"), R("bo"), [[-1, 128]], OP.is_gt, 0.0, 0, 1), [R("tri")], [R("bo")], 0.43)
+    ts(R("klist"), R("jrow", 0, 16), 16.0, OP.mult, C("col", LANE), OP.add)
+    ms(R("coff"), OFF)
+    ts(R("idh"), R("idb"), 0.5, OP.mult)
+    ts(R("idg"), R("idf"), 0.5, OP.mult)
+    for k in range(4):
+        ms(R("ae", 448 * k, 448 * k + 448), 0.0)
+    for nme in ("be", "ne"):
+        for k in range(2):
+            iota(R(nme, 896 * k, 896 * k + 896), [[0, 896]], 0, 0)
+    ms(R("a", V, 1296), 0.0)
+    ms(R("b", V, 1296), 0.0)
+    ms(R("lf", 80, 243, 81), 0.0)
+    ms(R("u", K, V), 0.0)
+    ms(R("v", K, V), 0.0)
+    ms(R("on", 64, 80), 1.0)
+    ms(R("flm", 64, 80), 0.0)
+    ms(R("one"), 1.0)
+    ms(R("c256"), 256.0)
+    iota(R("rst"), [[0, 1280]], 1, 0)
+    ms(R("rst", 0, 1280, 80), 0.0)
+    iota(R("dd0", 0, K), [[0, K]], 0, 0)
+    iota(R("dd1", 0, K), [[0, K]], 0, 0)
+
+    def perm(out, t, a, b):
+        mm(out, [(R("pm", 128 * (3 * t + e), 128 * (3 * t + e + 1)), R("lf", a + e, b, 3)) for e in range(3)])
+
+    cp(R("lf", 0, 80), R("li", 0, 80))
+    perm(R("s0", 128, 155), 0, 0, 81)
+    cp(R("su0", 0, 27), R("s0", 128, 155))
+    ts(R("thf"), R("li", 304, 306), 0.5, OP.add)
+    cp(R("fu"), R("li", 240, 304))
+    cp(R("fl"), R("li", 240, 304))
+    cp(R("lf", 81, 161), R("li", 80, 160))
+    cp(R("lf", 162, 242), R("li", 160, 240))
+
+    def jr(t, b):
+        return -((t - BL * b) // 3), -((t - BL * (b + 1)) // 3)
+
+    def first(t, b):
+        return (jr(t, b)[0] // 16) * 16
+
+    ms(R("nsb", 27, 112, 28), 0.0)
+
+    def tables(t):
+        bank = "s%d" % t
+        perm(R(bank, 160, 214), t, 81, 243)
+        tt(R("dtmp", 0, 54), R(bank, 160, 214), R("row48", 0, 54), OP.subtract)
+        for k in range(2):
+            ts(R("du%d" % t, 28 * k, 28 * k + 27), R("dtmp", 27 * k, 27 * k + 27), C("col", L3), OP.subtract, float(-t), OP.add)
+        act(R("ga"), IND(R("tp"), R("du%d" % t, 0, 27)), AF.Copy)
+        act(R("gb"), IND(R("tp"), R("du%d" % t, 28, 55)), AF.Copy)
+        for k in range(2):
+            o = 56 * t + 28 * k
+            cp(R("nsb", o, o + 27), R(bank, 160 + 27 * k, 187 + 27 * k))
+            for b in range(4):
+                c0, g0 = o + first(t, b) // 16, 32 * b + 16 * t + 8 * k
+                ts(R("gu", g0, g0 + 8), R("nsb", c0, c0 + 8), float(-BL * (b + 1)), OP.add)
+        mm(R("d1", 0, SUB), [(R("da"), R("ga")), (R("db"), R("gb"))])
+        act(R("ns%d" % t), R("d1", 0, SUB), AF.Copy)
+
+    def sums():
+        for k in range(2):
+            for q in range(4):
+                mm(R("x%d" % q, 256 * k, 256 * k + 256), [(R("idb"), R("coff")), (R("idb"), R("uv"[k], 256 * q, 256 * q + 256))])
+
+    def collapse(t, off):
+        n = 427
+        tt(R("cd"), IND(R("u", 0, K), off), R("a", t, 1296, 3), OP.subtract)
+        act(R("ce"), R("cd"), AF.Abs, bias=-128.0)
+        act(R("cs"), R("ce"), AF.Sign, bias=C("thf", t), scale=-1.0)
+        mm(R("d0", 0, SUB), [(R("bo"), R("cs"))])
+        ts(R("d0", 0, SUB), R("d0", 0, SUB), 1.0, OP.is_ge)
+        tt(R("ae", t, V, 3), R("d0", 0, n), R("a", t, V, 3), OP.mult)
+        tt(R("be", t, V, 3), R("d0", 0, n), R("b", t, V, 3), OP.mult)
+        tt(R("ne", t, V, 3), R("d0", 0, n), R("ns%d" % t, 0, n), OP.mult)
+        act(R("live%d" % t), R("d0", 0, SUB), AF.Identity, bias=1.0, scale=-1.0)
+
+    def scaled(t):
+        for b in (3, 2, 1, 0):
+            for k in range(2):
+                o, f = 512 * b + 256 * t + 128 * k, 3 * first(t, b) + t
+                act(R("ab", o, o + 128), R(("ae", "be")[k], f, f + 384, 3), AF.Copy, scale=1.0 / 256)
+
+    def hop(c):
+        fu = R("fu", 32 * c, 32 * c + 32)
+        fl = R("fl", 32 * c, 32 * c + 32)
+        gg, sg, bank = R("g%d" % c), R("sg%d" % c), "s%d" % c
+        act(gg, IND(R("ne"), fu), AF.Copy)
+        ext(R(bank, 32, 64), "zd", gg, 32)
+        ext(R(bank, 64, 96), "zm", gg, 32, [(R("idf"), fl)])
+        for q in (2 * c, 2 * c + 1):
+            u, v = R("u", 256 * q, 256 * q + 256), R("v", 256 * q, 256 * q + 256)
+            o = 256 * (q % 2)
+            fq, r = R("fu", 16 * q, 16 * q + 16), R("r%d" % c, o, o + 256)
+            for tab, acc, mul, res, t in (("ae", R("x%d" % q, 0, 256), v, u, R("t0", 256 * q, 256 * q + 256)),
+                                          ("be", R("x%d" % q, 256, 512), u, v, R("t1", 256 * q, 256 * q + 256))):
+                tt(t, IND(R(tab), fq), mul, OP.mult)
+                tt(acc, t, acc, OP.add)
+                act(r, acc, AF.Identity, bias=2.0 ** 31 - 128, scale=1.0 + 2.0 ** -19)
+                act(r, r, AF.Identity, bias=-2.0 ** 31)
+                tt(res, acc, r, OP.subtract)
+            d = R("d%d" % (q % 2), 0, 256)
+            mm(d, [(R("idb"), u), (R("idn"), v)])
+            act(R("sg%d" % c, o, o + 256), d, AF.Sign, bias=0.5)
+        ext(R(bank, 0, 32), "z1", sg, 32)
+        ss, se = R("ss", 32 * c, 32 * c + 32), R("se", 32 * c, 32 * c + 32)
+        act(ss, R(bank, 0, 32), AF.Sign, bias=-1.0)
+        tt(se, ss, R(bank, 32, 64), OP.mult)
+        tt(fl, se, R(bank, 64, 96), OP.add)
+        return fu, fl
+
+    def leave(t):
+        sn = "sn%d" % t
+        ts(R("on", 0, 64), R("fl"), float(V), OP.is_ge)
+        mm(R("s0", 256, 336), [(R("bo"), R("on"))])
+        mm(R("s0", 336, 416), [(R("tri"), R("on"))])
+        scan(R("cb", 0, 80), R("one"), R("s0", 256, 336), 0.0)
+        scan(R("cb", 80, 160), R("one"), R("s0", 256, 336), -16.0)
+        scan(R("ci"), R("one"), R("s0", 256, 336), 0.0)
+        ts(C("cn", 8 * t + 3), C("ci", 63), float(CAP), OP.min)
+        s = send("ct%d" % t, [C("cn", 8 * t + 3)])
+        arrive("a_ct%d" % t, [R("cn", 8 * t + 4, 8 * t + 7)], s, T_CNT)
+        for j in range(8):
+            ts(R("flg", 160 * j, 160 * j + 160), R("cb"), C("col", LANE), OP.subtract, float(32 * j), OP.is_le)
+        scan(R("cq"), R("rst"), R("flg"), 0.0)
+        cp(R("cu"), R("cq", 79, 1280, 80))
+        tt(R("key"), R("ci"), R("s0", 336, 416), OP.subtract)
+        tt(R("keyon"), R("key"), R("on"), OP.mult)
+        ts(R("flm", 0, 64), R("fl"), -1536.0, OP.add)
+        tt(R("oh"), IND(R("keyon"), R("cu")), R("jrow", 1, 257), OP.is_equal)
+        ext(R("s1", 256, 272), "zl", R("oh"), 16, [(R("id16"), R("cq", 79, 1280, 80))])
+        tt(R(sn, 512, 768), IND(R("flm"), R("cu")), R("oh"), OP.mult)
+        s = send("fm%d" % t, [R(sn, 512, 768)])
+        arrive("a_fm%d" % t, [R("rc%d" % t, 512, 768)], s, T_RELAY)
+        cp(R("atu"), R("s1", 256, 272))
+        if t == 0:
+            act(R(sn, 0, 256), IND(R("u", 0, V), R("atu")), AF.Copy)
+            cp(R(sn, 256, 512), IND(R("v", 0, V), R("atu")))
+        else:
+            act(R(sn, 0, 256), IND(R("u", 0, V), R("atu")), AF.Identity, bias=-1.0, scale=1.0 / 128)
+            ts(R(sn, 256, 512), IND(R("v", 0, V), R("atu")), -128.0, OP.add, 1.0 / 64, OP.mult)
+        s = send("uv%d" % t, [R(sn, 0, 512)])
+        arrive("a_u%d" % t, [R("rc%d" % t, 0, 256)], s, T_RELAY)
+        arrive("a_v%d" % t, [R("rc%d" % t, 256, 512)], s, T_RELAY + 0.3)
+        ts(R("kt"), R("on", 0, 64), -2048.0, OP.mult, 2048.0, OP.add)
+        tt(R("key2"), R("kt"), R("keyon", 0, 64), OP.add)
+        ts(R("flq"), R("fl"), -256.0, OP.add)
+
+    def enter(t):
+        rc, m = "rc%d" % t, C("mm", t)
+        rmin(m, R("cn", 8 * t + 3, 8 * t + 7))
+        ts(R("az"), R("klist"), m, OP.is_ge, float(V), OP.mult)
+        tt(R("a2"), R("az"), R("s1", 256, 272), OP.add)
+        cp(R("a2u"), R("a2"))
+        if t == 0:
+            ts(R("si", 0, 107), R("sall", 0, 107), m, OP.add)
+            ts(R("sj", 0, 107), R("si", 0, 107), K - 1, OP.bitwise_and)
+            cp(R("so0", 0, 107), R("sj", 0, 107))
+        else:
+            ts(R("si", 0, 80), R("sall", 0, 80), C("mm", 0), OP.add, m, OP.add)
+            ts(R("sj", 0, 80), R("si", 0, 80), K - 1, OP.bitwise_and)
+            cp(R("so1"), R("sj", 0, 80))
+        ts(R("nf"), R("key2"), m, OP.is_gt)
+        tt(R("pre"), R("nf"), R("flq"), OP.mult)
+        cp(IND(R("u" if t == 0 else "up1"), R("a2u")), R(rc, 0, 256))
+        cp(IND(R("dd%d" % t), R("a2u")), R(rc, 512, 768))
+        if t == 0:
+            cp(IND(R("v"), R("a2u")), R(rc, 256, 512))
+        else:
+            act(R("d1", 0, 256), R(rc, 256, 512), AF.Copy)
+            tt(R("zr"), R("d1", 0, 256), R(rc, 0, 256), OP.mult)
+            add("s", "act", (IND(R("sig"), R("a2u")), R("zr"), AF.Sigmoid, None, None), [IND(R("sig"), R("a2u"))], [R("zr")],
+                0.065 + CY * SCA * 256)
+        ext(R("s0", 416, 480), "z1", R("dd%d" % t), 64, [(R("idb"), R("c256"))])
+        tt(R("fl"), R("pre"), R("s0", 416, 480), OP.add)
+        cp(R("fu"), R("fl"))
+
+    def followers(w, rho, b):
+        n = rho + 1
+        tt(R("pq", 512 * b, 512 * b + 256 * n), IND(R(w, BL * (b + 1), W), R("gu", 32 * b, 32 * b + 16 * n)),
+           R("ab", 512 * b, 512 * b + 256 * n), OP.mult)
+
+    def heights(rho):
+        w, up, so = "w%d" % rho, "up%d" % rho, "so%d" % rho
+        banks = ("d0", "d1")
+        res = range(rho + 1)
+        old, half = (("h", "idh"), ("w0", "idg"))[rho]
+        followers(w, rho, 3)
+        for b in (3, 2, 1, 0):
+            blk = (BL * b, BL * b + BL)
+            acc = R("x%d" % b, 0, BL)
+            mm(acc, [(R(half), R(old, *blk))], stop=False)
+            if rho == 1 and b == 2:
+                cp(R("xs", *blk), IND(R(up, 0, K), R(so, 20 * b, 20 * b + 20)))
+            else:
+                act(R("xs", *blk), IND(R(up, 0, K), R(so, 20 * b, 20 * b + 20)), AF.Copy)
+            mm(acc, [(R("idb"), R("xs", *blk))], start=False)
+            for t in res:
+                j0, j1 = jr(t, b)
+                tt(R(banks[t], j0, j1), R("x%d" % b, 3 * j0 + t - BL * b, BL, 3), R("live%d" % t, j0, j1), OP.mult)
+            act(R(w, *blk), acc, AF.Copy)
+        for b in (3, 2, 1, 0):
+            if b < 3:
+                followers(w, rho, b)
+            for t in res:
+                j0, j1 = jr(t, b)
+                o = 512 * b + 256 * t + j0 - first(t, b)
+                tt(R(banks[t], j0, j1), R(banks[t], j0, j1), R("pq", o, o + j1 - j0), OP.add)
+            for t in res:
+                j0, j1 = jr(t, b)
+                o = 512 * b + 256 * t + 128 + j0 - first(t, b)
+                tt(R(w, 3 * j0 + t, 3 * (j1 - 1) + t + 1, 3), R(banks[t], j0, j1), R("pq", o, o + j1 - j0), OP.add)
+
+    def hops():
+        for hp in range(2):
+            for c in range(2):
+                tag[0] += 1
+                fu, fl = hop(c)
+                if hp == 0:
+                    cp(fu, fl)
+        tag[0] += 1
+
+    tables(0)
+    s = send("hs0", [R("h", 0, GH)])
+    arrive("a_hs0", [R("hg")], s, T_RELAY + 3)
+    collapse(0, R("su0", 0, 27))
+    sums()
+    hops()
+    leave(0)
+    cp(R("sall", 0, 80), R("li", 0, 80))
+    perm(R("s1", 128, 155), 1, 0, 81)
+    cp(R("sall", 80, 107), R("s1", 128, 155))
+    tables(1)
+    scaled(0)
+    act(R("w0", V, W), R("hg"), AF.Copy)
+    enter(0)
+    collapse(1, R("so0", 80, 107))
+    sums()
+    for c in range(2):
+        act(R("up0", 512 * c, 512 * c + 512), R("u", 512 * c, 512 * c + 512), AF.Identity, bias=-1.0, scale=1.0 / 128)
+    scaled(1)
+    hops()
+    leave(1)
+    heights(0)
+    s = send("hs1", [R("w0", 0, GH)])
+    arrive("a_hs1", [R("w1", V, W)], s, T_RELAY + 1)
+    for c in range(2):
+        act(R("up1", 512 * c, 512 * c + 512), R("u", 512 * c, 512 * c + 512), AF.Identity, bias=-1.0, scale=1.0 / 128)
+        act(R("x%d" % c), R("v", 512 * c, 512 * c + 512), AF.Identity, bias=-2.0, scale=1.0 / 64)
+        tt(R("zz", 512 * c, 512 * c + 512), R("x%d" % c), R("up1", 512 * c, 512 * c + 512), OP.mult)
+        act(R("sig", 512 * c, 512 * c + 512), R("zz", 512 * c, 512 * c + 512), AF.Sigmoid, extra=1.3 if c == 0 else 0.0)
+    enter(1)
+    heights(1)
+    for b in (3, 2, 1, 0):
+        mm(R("x3", 0, BL), [(R("idf"), R("w1", BL * b, BL * b + BL))], start=b == 3, stop=b == 0)
+    act(R("oh2"), R("x3", 0, BL), AF.Copy)
+    store("y", "st0", "yh", 0, BL, R("oh2"))
+    for c in range(2):
+        tt(R("plo", 256 * c, 256 * c + 256), IND(R("w1"), R("fu", 16 * c, 16 * c + 16)), R("sig", 256 * c, 256 * c + 256), OP.mult)
+    for c in range(2):
+        act(R("x%d" % c, 0, 256), R("plo", 256 * c, 256 * c + 256), AF.Copy)
+    for c in range(2):
+        tt(R("phi", 256 * c, 256 * c + 256), IND(R("w1"), R("fu", 32 + 16 * c, 48 + 16 * c)), R("sig", 512 + 256 * c, 768 + 256 * c), OP.mult)
+        tt(R("ow", 256 * c, 256 * c + 256), R("x%d" % c, 0, 256), R("phi", 256 * c, 256 * c + 256), OP.add)
+        store("y", "st%d" % (1 + c), "yw", 256 * c, 256 * c + 256, R("ow", 256 * c, 256 * c + 256))
+    return nodes
+
+
+def _meet(x, y):
+    return x[0] == y[0] and x[1] < y[2] and y[1] < x[2]
+
+
+def schedule(nodes):
+    for n in nodes:
+        dep = {}
+        for m in nodes[:n["id"]]:
+            raw = any(_meet(x, y) for x in m["wr"] for y in n["rd"])
+            other = any(_meet(x, y) for x in m["wr"] + m["rd"] for y in n["wr"])
+            bank = m["eng"] != n["eng"] and any(_psum(x) and x[0] == y[0] for x in m["wr"] + m["rd"] for y in n["wr"] + n["rd"])
+            group = m["kind"] == n["kind"] == "mm" and not n["args"][2]
+            if raw or bank or (other and not group):
+                dep[m["id"]] = True
+            elif other:
+                dep[m["id"]] = False
+        for m in n["after"]:
+            dep[m] = False
+        n["dep"] = dep
+    lastq = {}
+    for n in nodes:
+        if n["kind"] in ("load", "send"):
+            if n["eng"] in lastq and lastq[n["eng"]] not in n["dep"]:
+                n["dep"][lastq[n["eng"]]] = False
+            lastq[n["eng"]] = n["id"]
+
+    def gap(m, n):
+        if not n["dep"][m["id"]]:
+            return m["dur"]
+        return m["dur"] + m["lat"] + (LAT_S if m["eng"] == n["eng"] else LAT_X)
+
+    for n in reversed(nodes):
+        n.setdefault("lvl", n["dur"] + n["lat"])
+        for i in n["dep"]:
+            m = nodes[i]
+            m["lvl"] = max(m.get("lvl", m["dur"] + m["lat"]), gap(m, n) + n["lvl"])
+    deps = [[(i, gap(nodes[i], n)) for i in n["dep"]] for n in nodes]
+    users = [[] for n in nodes]
+    for n in nodes:
+        for i in n["dep"]:
+            users[i].append(n["id"])
+
+    def place(prio):
+        busy, at = {}, [0.0] * len(nodes)
+        wait = [len(d) for d in deps]
+        ready = [i for i, c in enumerate(wait) if not c]
+        while ready:
+            k = max(ready, key=lambda i: (prio[i], -i))
+            ready.remove(k)
+            t, dur = max([at[i] + d for i, d in deps[k]] + [0.0]), nodes[k]["dur"]
+            if nodes[k]["eng"] != "a":
+                q = busy.setdefault(nodes[k]["eng"], [])
+                pos = len(q)
+                for j, (a, b) in enumerate(q):
+                    if t + dur <= a + 1e-9:
+                        pos = j
+                        break
+                    t = max(t, b)
+                q.insert(pos, (t, t + dur))
+            at[k] = t
+            for i in users[k]:
+                wait[i] -= 1
+                if not wait[i]:
+                    ready.append(i)
+        return max(at[i] + n["dur"] + n["lat"] for i, n in enumerate(nodes)), at
+
+    prio = [n["lvl"] + (15.0 if n["tag"] < 0 else 0.0) for n in nodes]
+    best, at = place(prio)
+    seed = SEED
+    tags = max(n["tag"] for n in nodes) + 1
+    for it in range(TRIES):
+        trial = list(prio)
+        seed = (seed * 1103515245 + 12345) % 2 ** 31
+        mid = best * seed / 2 ** 31
+        if it % 4 == 3:
+            seed = (seed * 1103515245 + 12345) % 2 ** 31
+            pick, step = (seed >> 8) % tags, ((seed >> 16) % 64 - 32) / 10.0
+            trial = [p + (step if n["tag"] == pick else 0.0) for p, n in zip(prio, nodes)]
+        else:
+            for i in range(len(nodes)):
+                if abs(at[i] - mid) < 3:
+                    seed = (seed * 1103515245 + 12345) % 2 ** 31
+                    if (seed >> 8) % 8 == 0:
+                        trial[i] += (seed / 2 ** 31 - 0.5) * (1.0, 3.0, 8.0)[it % 4]
+        span, got = place(trial)
+        if span <= best:
+            best, at, prio = span, got, trial
+    for n in nodes:
+        n["t"] = at[n["id"]]
+    return sorted(nodes, key=lambda x: (x["t"], x["id"]))
+
+
+_ORDER = []
+
+
+def _order():
+    if not _ORDER:
+        _ORDER.extend(schedule(build()))
+    return _ORDER
+
+
+def _mask(engines):
+    return sum(1 << e for e in engines)
+
+
+def routes(T, topo):
+    cores, n = T.cores, len(T.cores)
+    out = {}
+    for r, c in enumerate(cores):
+        nxt, prv = (r + 1) % n, (r - 1) % n
+        own = [x for x in topo.cores_of(c) if x != c and topo.may_write(x, cores[nxt]) and topo.may_write(x, cores[prv])]
+        near = [x for x in own if topo.die(x) == topo.die(c)]
+        far = [x for x in own if topo.die(x) != topo.die(c)]
+
+        def beside(d):
+            return [x for x in range(NCORES) if topo.mates(x, cores[d]) and topo.die(x) == topo.die(c)
+                    and topo.may_write(x, cores[d]) and topo.may_write(c, x)][0]
+
+        for t in range(2):
+            src, land, buf = (("h", ("hg", 0), "yb"), ("w0", ("w1", V), "yf"))[t]
+            out[r, "hs%d" % t] = [(x, R(src, 128 * k, 128 * k + 128), R(buf, 0, 128),
+                                   [(prv, R(land[0], land[1] + 128 * k, land[1] + 128 * k + 128), "a_hs%d" % t)])
+                                  for k, x in enumerate((beside(prv), near[0], near[1], far[0]))]
+            mine = C("cn", 8 * t + 3)
+            to = [(d, C("cn", 8 * t + 3 + (d - r) % n), "a_ct%d" % t) for d in range(n) if d != r]
+            out[r, "ct%d" % t] = ([(None, mine, None, [x]) for x in to if topo.may_write(c, cores[x[0]])]
+                                  + [(near[1], mine, C("yf", 128 + 4 * t), [x for x in to if not topo.may_write(c, cores[x[0]])])])
+            keep = R("yb", 128 + 256 * t, 384 + 256 * t)
+            out[r, "fm%d" % t] = [(beside(nxt), R("sn%d" % t, 512, 768), keep, [(nxt, R("rc%d" % t, 512, 768), "a_fm%d" % t)])]
+            out[r, "uv%d" % t] = [(near[0], R("sn%d" % t, 0, 256), keep, [(nxt, R("rc%d" % t, 0, 256), "a_u%d" % t)]),
+                                  (far[0], R("sn%d" % t, 256, 512), keep, [(nxt, R("rc%d" % t, 256, 512), "a_v%d" % t)])]
+    return out
+
+
+def _deal(src, dsts, topo):
+    can = [topo.engines(src, d) for d in dsts]
+    every = sorted(set(e for x in can for e in x))
+    share = 1
+    while share * 2 * len(dsts) <= len(every):
+        share *= 2
+    used, got = set(), [None] * len(dsts)
+    for i in sorted(range(len(dsts)), key=lambda i: len(can[i])):
+        got[i] = [e for e in can[i] if e not in used][:share]
+        used.update(got[i])
+    return got
+
+
+def _firsts(pieces, T):
+    return [x if x is not None else T.cores[to[0][0]] for x, s, k, to in pieces]
+
+
+def rank_program(g, core, T, topo):
+    order = _order()
+    msgs = [n["args"][0] for n in order if n["kind"] == "send"]
+    way = routes(T, topo)
+    cores = T.cores
+
+    def ap(x):
+        if not isinstance(x, tuple):
+            return x
+        if x[0] == "@":
+            return ap(x[1]).indirect(ap(x[2]))
+        return T[x[0]][:, x[1]:x[2]] if x[3] == 1 else T[x[0]][:, x[1]:x[2]:x[3]]
+
+    def did(dst):
+        rid, pid = topo.addr(dst, core)
+        return DstId(rid=rid, pnc=pid)
+
+    rank = T.rank_of(core)
+    if rank is None:
+        sent = 0
+        for msg in msgs:
+            for r in range(len(cores)):
+                pieces = way[r, msg]
+                for (x, src, keep, to), eng in zip(pieces, _deal(cores[r], _firsts(pieces, T), topo)):
+                    if x != core:
+                        continue
+                    g.wait_ge(T.sem["y_" + msg], len(eng))
+                    on = topo.engines(core, cores[to[0][0]])
+                    g.remote_dma_fused([RemoteDMATransfer(dst_ids=[did(cores[d]) for d, l, s in to], dma_engine_mask=_mask(on),
+                                                          remote_sem=T.sem[to[0][2]], srcs=[ap(keep)], dsts=[ap(l) for d, l, s in to])],
+                                       local_sem=T.sem.sent)
+                    sent += len(on)
+        if sent:
+            g.wait_ge(T.sem.sent, sent)
+        return
+
+    due = {}
+    for (r, msg), pieces in way.items():
+        for (x, src, keep, to), eng in zip(pieces, _deal(cores[r], _firsts(pieces, T), topo)):
+            for d, l, s in to:
+                if d == rank:
+                    due[s] = due.get(s, 0) + (len(eng) if x is None else len(topo.engines(x, core)))
+
+    queue = {"v": g.vector, "s": g.scalar, "t": g.tensor, "g": g, "y": g.sync}
+    count = {"v": 0, "s": 0, "t": 0, "g": 0}
+    known = {q: {} for q in queue}
+    mark, seen = {}, {}
+    tail, sent = [], 0
+    for n in order:
+        kind, a, e = n["kind"], n["args"], n["eng"]
+        if kind == "arrive":
+            mark[n["id"]] = (a[0], due[a[0]])
+            seen[n["id"]] = {}
+            continue
+        q, kn = queue[e], known[e]
+        need = sorted((i for i, hard in n["dep"].items() if hard and i in mark), key=lambda i: -mark[i][1])
+        for i in need:
+            s, val = mark[i]
+            if kn.get(s, 0) < val:
+                q.wait_ge(T.sem[s], val)
+                kn[s] = val
+                for s2, v2 in seen[i].items():
+                    kn[s2] = max(kn.get(s2, 0), v2)
+        seen[n["id"]] = dict(kn)
+        if kind == "load":
+            q.dma_start(ap(a[1]), T[a[0]][:]).then_inc(T.sem["l_" + a[0]], 16)
+            mark[n["id"]] = ("l_" + a[0], 16)
+            continue
+        if kind == "store":
+            q.dma_start(T[a[1]][:, a[2]:a[3]], ap(a[4])).then_inc(T.sem[a[0]], 16)
+            tail.append(a[0])
+            continue
+        if kind == "send":
+            pieces = way[rank, a[0]]
+            firsts = _firsts(pieces, T)
+            deal = _deal(core, firsts, topo)
+            g.remote_dma_fused([RemoteDMATransfer(dst_ids=[did(f)], dma_engine_mask=_mask(eng),
+                                                  remote_sem=T.sem[to[0][2] if x is None else "y_" + a[0]],
+                                                  src=ap(src), dst=ap(to[0][1] if x is None else keep))
+                                for (x, src, keep, to), f, eng in zip(pieces, firsts, deal)], local_sem=T.sem.sent)
+            sent += sum(len(x) for x in deal)
+            continue
+        if kind == "tt":
+            i = q.tensor_tensor(ap(a[0]), ap(a[1]), ap(a[2]), a[3])
+        elif kind == "ts":
+            if a[5] is None:
+                i = q.tensor_scalar(ap(a[0]), ap(a[1]), ap(a[2]), None, a[4])
+            else:
+                i = q.tensor_scalar(ap(a[0]), ap(a[1]), ap(a[2]), ap(a[3]), a[4], a[5])
+        elif kind == "cp":
+            i = q.tensor_copy(ap(a[0]), ap(a[1]))
+        elif kind == "ms":
+            i = q.memset(ap(a[0]), a[1])
+        elif kind == "scan":
+            i = q.tensor_tensor_scan(ap(a[0]), ap(a[1]), ap(a[2]), a[3], OP.mult, OP.add)
+        elif kind == "rmin":
+            i = q.tensor_reduce(ap(a[0]), ap(a[1]), AxisListType.X, OP.min)
+        elif kind == "act":
+            if a[3] is None:
+                i = q.activation(ap(a[0]), ap(a[1]), a[2])
+            else:
+                i = q.activation(ap(a[0]), ap(a[1]), a[2], bias=ap(a[3]), scale=ap(a[4]))
+        elif kind == "mm":
+            for k, (l, r) in enumerate(a[1]):
+                i = q.matmul(ap(a[0]), ap(l), ap(r), a[2] and k == 0, a[3] and k == len(a[1]) - 1)
+        elif kind == "iota":
+            if _SB[a[0][0]][0] == I32:
+                i = q.iota(ap(a[0]), a[1], a[2], a[3])
+            else:
+                i = q.iota(ap(a[0]), a[1], a[2], a[3], allow_small_or_imprecise_dtypes=True)
+        else:
+            i = q.affine_select(ap(a[0]), ap(a[1]), a[2], a[3], a[4], a[5], a[6])
+        count[e] += 1
+        i.then_inc(T.sem["e" + e], 1)
+        mark[n["id"]] = ("e" + e, count[e])
+    for s in tail:
+        g.sync.wait_ge(T.sem[s], 16)
+    for e, c in count.items():
+        g.sync.wait_ge(T.sem["e" + e], c)
+    g.wait_ge(T.sem.sent, sent)

@@ -9,34 +9,40 @@ OFF = 131072.0
 BF, F32, I32, U16 = "bfloat16", "float32", "int32", "uint16"
 
 _SB = {
-    "li": (I32, 320), "lf": (F32, 244), "sall": (F32, 108), "si": (I32, 108), "sj": (I32, 108),
+    "li": (I32, 320), "lf": (F32, 252), "sall": (F32, 108), "si": (I32, 108), "sj": (I32, 108),
     "so0": (U16, 108), "so1": (U16, 80), "su0": (U16, 28),
-    "du0": (U16, 56), "du1": (U16, 56), "gu": (U16, 128), "nsb": (F32, 112), "ab": (BF, 2048), "pq": (F32, 2048),
-    "dtmp": (F32, 56), "row48": (F32, 56),
-    "jrow": (F32, 272), "j3": (F32, 128), "jg": (F32, 128), "pi": (I32, 4), "col": (F32, 32), "tb7": (F32, 8),
-    "pm": (F32, 768), "bo": (BF, 128), "tri": (BF, 128), "idb": (BF, 128), "idn": (BF, 128), "id16": (BF, 128),
-    "idf": (F32, 128), "da": (BF, 128), "db": (BF, 128),
-    "z1": (BF, 144), "zm": (BF, 144), "zd": (BF, 144), "zl": (BF, 144), "c256": (BF, 64), "one": (F32, 80),
-    "rst": (BF, 1280), "klist": (F32, 16), "thf": (F32, 2),
-    "a": (BF, 1296), "b": (BF, 1296), "h": (BF, V), "u": (BF, 2560), "v": (BF, 2560),
-    "ae": (BF, W), "be": (BF, W), "ne": (BF, W), "tp": (BF, W),
-    "ga": (BF, SUB), "gb": (BF, SUB), "ns0": (BF, SUB), "ns1": (BF, SUB),
-    "cd": (F32, SUB), "ce": (BF, SUB), "cs": (BF, SUB), "live0": (BF, SUB), "live1": (BF, SUB),
-    "coff": (BF, 256), "idh": (BF, 128), "idg": (F32, 128), "xs": (BF, V), "zr": (F32, 256),
-    "t0": (F32, K), "t1": (F32, K), "r0": (F32, 512), "r1": (F32, 512),
-    "g0": (BF, 512), "g1": (BF, 512), "sg0": (BF, 512), "sg1": (BF, 512),
-    "ss": (F32, 64), "se": (F32, 64), "fl": (F32, 64), "fu": (U16, 64),
-    "on": (BF, 80), "ci": (F32, 80), "cb": (BF, 160), "key": (F32, 80), "keyon": (F32, 80), "key2": (F32, 64),
-    "kt": (F32, 64), "flm": (F32, 80), "flq": (F32, 64), "flg": (BF, 1280), "cq": (BF, 1280), "cu": (U16, 16),
-    "oh": (BF, 256), "atu": (U16, 16), "az": (F32, 16), "a2": (F32, 16), "a2u": (U16, 16),
-    "cn": (F32, 16), "mm": (F32, 2), "nf": (F32, 64), "pre": (F32, 64),
-    "sn0": (BF, 768), "sn1": (BF, 768), "rc0": (BF, 768), "rc1": (BF, 768),
-    "dd0": (BF, 2560), "dd1": (BF, 2560), "up0": (BF, K), "up1": (BF, 2560),
-    "hg": (BF, GH), "w0": (F32, W), "w1": (F32, W),
-    "zz": (F32, K), "sig": (F32, 2560), "plo": (F32, 512), "phi": (F32, 512),
+    "du": (U16, 56), "gu": (U16, 128), "go": (U16, 8), "gf": (F32, 128), "grow": (F32, 128), "gcol": (F32, 8),
+    "nsb": (F32, 112), "ab": (BF, 2048), "pq": (F32, 2048), "dtmp": (F32, 56), "row48": (F32, 56),
+    "jrow": (F32, 256), "krow": (F32, 256), "j3": (F32, 128), "jg": (F32, 128), "pi": (I32, 4), "col": (F32, 32), "colb": (BF, 8),
+    "under": (F32, 16), "ca": (BF, 16), "tb7": (F32, 8), "pm": (F32, 768), "bo": (BF, 128), "tri": (BF, 128), "idb": (BF, 128), "idn": (BF, 128),
+    "id16": (BF, 128), "idf": (F32, 128), "da": (BF, 128), "db": (BF, 128), "i256": (BF, 128), "m256": (BF, 128),
+    "z1": (BF, 144), "zm": (BF, 144), "zd": (BF, 144), "zl": (BF, 144), "c256": (BF, 64), "one": (F32, 32),
+    "rst": (BF, 512), "klist": (F32, 80), "coff": (BF, 256), "ch": (BF, 256), "idh": (BF, 128), "idg": (F32, 128),
+    "a": (BF, 1296), "b": (BF, 1296), "h": (BF, 1296), "u": (BF, V), "v": (BF, V), "ub": (BF, K), "vb": (BF, K),
+    "ua": (BF, K), "lw": (BF, V), "kw": (BF, 256), "zk": (BF, 144),
+    "ae": (BF, W), "be": (BF, W), "ne": (BF, W), "tp": (BF, W), "lv": (BF, 1296),
+    "ga": (BF, 2 * SUB), "ns": (BF, 2 * SUB), "ac": (BF, 2 * SUB), "bs": (BF, 2 * SUB),
+    "cd": (BF, SUB), "c1": (BF, SUB), "c2": (BF, SUB), "xs": (BF, 1296), "zr": (F32, 256),
+    "t0": (F32, K), "t1": (F32, K), "r0": (F32, K), "r1": (F32, K), "ki": (I32, K), "gg": (BF, K), "sg": (BF, K),
+    "fs": (F32, 128), "dz": (F32, 128), "dm": (F32, 128), "fu": (U16, 64),
+    "on": (BF, 64), "ci": (F32, 64), "cc": (F32, 4), "cb": (BF, 256), "key": (F32, 64), "flm": (F32, 64), "flq": (F32, 64),
+    "flg": (BF, K), "cq": (BF, K), "cs": (BF, 16), "cu": (U16, 16),
+    "oh": (BF, 256), "atu": (U16, 16), "az": (F32, 48), "a2u": (U16, 16),
+    "cn": (F32, 16), "mm": (F32, 4), "nf": (F32, 384), "loc": (U16, 64),
+    "sn0": (BF, 768), "sn1": (BF, 768), "rc": (BF, 768),
+    "dd": (BF, K + 2 * CAP), "up": (BF, 16 + V),
+    "hg": (BF, GH), "w0": (F32, W), "w1": (F32, W), "wl": (F32, V), "c3": (F32, BL),
+    "zz": (F32, K), "sig": (F32, V), "plo": (F32, 512), "phi": (F32, 512),
     "oh2": (F32, BL), "ow": (F32, 512),
     "yb": (BF, 640), "yf": (F32, 136),
 }
+_AT = {}
+for _n, (_d, _w) in list(_SB.items()):
+    if _w <= 144 and _n != "yf":
+        _used = _SB.get("all_" + _d, (_d, 0))[1]
+        _AT[_n] = ("all_" + _d, _used, _w)
+        _SB["all_" + _d] = (_d, _used + -(-_w // 32) * 32)
+        del _SB[_n]
 SCRATCH = {n: ("sbuf", [128, w], d) for n, (d, w) in _SB.items()}
 for _n in ("x0", "x1", "x2", "x3", "d0", "d1", "s0", "s1"):
     SCRATCH[_n] = ("psum", [128, 512], F32)
@@ -46,10 +52,15 @@ _MSGS = ["hs0", "ct0", "fm0", "uv0", "hs1", "ct1", "fm1", "uv1"]
 SEMAPHORES = (["ev", "es", "et", "eg", "sent"] + ["l_" + n for n in _LOADS] + ["st0", "st1", "st2"]
               + ["y_" + m for m in _MSGS] + ["a_hs0", "a_hs1", "a_ct0", "a_ct1", "a_fm0", "a_fm1", "a_u0", "a_v0", "a_u1", "a_v1"])
 
-CY, PCY, GAT, SCA = 0.001, 0.0006, 1.55, 3.2
-LAT_X, LAT_S = 0.12, 0.08
-T_RELAY, T_CNT = 4.5, 4.0
-TRIES, SEED = 2500, 12345
+COSTS = ((0.001, 0.0005, 1.55, 3.2, 4.0, 3.5, 1.4, 0.12, 0.08),
+         (0.0009, 0.00045, 1.2, 2.2, 5.5, 5.0, 2.0, 0.2, 0.1),
+         (0.0012, 0.0007, 1.9, 4.8, 4.0, 3.5, 1.4, 0.12, 0.08))
+TRIES, SEED = 3000, 12345
+REMAP, WIDE, ASIDE = True, False, False
+SHEAR = [("ts", "vs"), ("tv", "vs"), ("ts", "vs"), ("tv", "vs")]
+EARLY = {"chunk0": 0.5, "chunk2": 0.5, "half0": 2.0, "hs1": 5.0, "count": 4.0}
+SLACK, PASSES = 0.1, 2
+PARTS = ((0, 14), (14, 27))
 
 
 def _two(x):
@@ -67,26 +78,29 @@ def _n(x):
 
 
 def R(name, a=0, b=None, s=1):
+    if name in _AT:
+        buf, at, w = _AT[name]
+        return (buf, at + a, at + (w if b is None else b), s)
     if b is None:
         b = _SB[name][1] if name in _SB else 512
     return (name, a, b, s)
 
 
 def C(name, c):
-    return (name, c, c + 1, 1)
+    return R(name, c, c + 1)
 
 
 def IND(win, off):
     return ("@", win, off)
 
 
-class Plan:
-    pass
+LAND = {"u0": R("u", K, K + CAP) if REMAP else R("rc", 0, CAP), "v0": R("v", K, K + CAP), "fm0": R("dd", K, K + CAP),
+        "u1": R("rc", CAP, 2 * CAP), "v1": R("rc", 2 * CAP, 3 * CAP), "fm1": R("dd", K + CAP, K + 2 * CAP)}
 
 
-def build():
+def build(costs=COSTS[0]):
+    CY, PCY, GAT, SCA, T_RELAY, T_CNT, T_DMA = costs[:7]
     nodes = []
-    tag = [0]
 
     def regs(xs):
         o = []
@@ -104,8 +118,11 @@ def build():
             else:
                 wr.append(x)
         nodes.append(dict(eng=eng, kind=kind, args=args, rd=rd, wr=wr, dur=dur, lat=lat, after=list(after), id=len(nodes),
-                          tag=tag[0]))
+                          tag=""))
         return len(nodes) - 1
+
+    def early(name):
+        nodes[-1]["tag"] = name
 
     def vdur(out, ins, per):
         if out[0] == "@":
@@ -118,7 +135,8 @@ def build():
         return add("v", "tt", (out, x, y, op), [out], [x, y], vdur(out, [x], 1 if x[0] == "@" or _psum(x) or _psum(y) else 2))
 
     def ts(out, x, s1, op0, s2=None, op1=None):
-        per = 0.5 if x[0] != "@" and _two(x) and _two(out) else 1
+        wide = [s for s in (s1, s2) if isinstance(s, tuple) and not _two(s)]
+        per = 0.5 if x[0] != "@" and _two(x) and _two(out) and not wide else 1
         return add("v", "ts", (out, x, s1, s2, op0, op1), [out], [x, s1, s2], vdur(out, [x], per))
 
     def cp(out, x):
@@ -130,30 +148,33 @@ def build():
 
     def scan(out, d0, d1, init):
         per = 0.5 if _two(out) and _two(d0) and _two(d1) else 1
-        return add("v", "scan", (out, d0, d1, init), [out], [d0, d1], vdur(out, [d0], per))
+        return add("v", "scan", (out, d0, d1, init), [out], [d0, d1, init], vdur(out, [d0], per))
 
     def rmin(out, x):
         return add("v", "rmin", (out, x), [out], [x], 0.09)
 
-    def act(out, x, f, bias=0.0, scale=1.0, extra=0.0):
+    def act(out, x, f=AF.Identity, bias=0.0, scale=1.0, extra=0.0):
         d = 0.065 + CY * (GAT * _n(out) if x[0] == "@" else max(64, _n(out))) + extra
         return add("s", "act", (out, x, f, bias, scale), [out], [x, bias, scale], d)
 
     def mm(out, pairs, start=True, stop=True):
         d = sum(PCY * max(64, _n(r)) * (1 if _two(r) else 4) for l, r in pairs) + 0.05
-        return add("t", "mm", (out, pairs, start, stop), [out], [x for p in pairs for x in p], d)
+        return add("t", "mm", (out, pairs, start, stop), [out], [x for p in pairs for x in p] + ([] if start else [out]), d)
 
-    def ext(out, z, src, n, more=()):
-        return mm(out, [(R(z, 15 - i, 143 - i), R(src[0], src[1] + i, src[1] + 16 * n, 16)) for i in range(16)] + list(more))
+    def ext(out, z, src, n, more=(), start=True):
+        return mm(out, [(R(z, 15 - i, 143 - i), R(src[0], src[1] + i, src[1] + 16 * n, 16)) for i in range(16)] + list(more), start)
 
     def iota(out, pat, base, cm):
         return add("g", "iota", (out, pat, base, cm), [out], [], 0.13 + 2 * CY * _n(out))
 
+    def asel(out, x, pat, op, fill, base, cm):
+        return add("g", "asel", (out, x, pat, op, fill, base, cm), [out], [x], 0.17 + 2 * CY * _n(out))
+
     def load(q, name, out, kb):
-        return add(q, "load", (name, out), [out], [], 0.06, lat=1.9 + kb / 300.0)
+        return add(q, "load", (name, out), [out], [], 0.06, lat=T_DMA + kb / 300.0)
 
     def store(q, sem, name, a, b, src):
-        return add(q, "store", (sem, name, a, b, src), [], [src], 0.06, lat=2.2)
+        return add(q, "store", (sem, name, a, b, src), [], [src], 0.06, lat=T_DMA + 0.4)
 
     def send(msg, ins):
         return add("g", "send", (msg,), [], ins, 0.6)
@@ -161,90 +182,97 @@ def build():
     def arrive(sem, out, snd, lat):
         return add("a", "arrive", (sem,), out, [], 0.0, lat=lat, after=[snd])
 
+    def fl(c0=0, c1=64):
+        return R("fs", 2 * c0 + 1, 2 * c1, 2)
+
     load("y", "sd", R("li", 0, 80), 40)
     load("s", "ta", R("a", 0, V), 320)
-    load("y", "u0", R("u", 0, K), 300)
+    load("y", "u0", R("u", 0, K), 500)
     load("s", "th", R("li", 304, 306), 330)
-    load("y", "pf", R("li", 240, 304), 340)
-    load("y", "v0", R("v", 0, K), 600)
+    load("y", "pf", R("li", 240, 304), 600)
+    load("y", "v0", R("v", 0, K), 800)
     load("s", "na", R("li", 80, 160), 380)
     load("s", "nb", R("li", 160, 240), 420)
-    load("y", "tb", R("b", 0, V), 900)
-    load("y", "h0", R("h"), 1200)
+    load("y", "tb", R("b", 0, V), 1100)
+    load("y", "h0", R("h", 0, V), 1400)
 
-    LANE, G16, Q3, PF, ODD, EVEN, WM, WD, MA, MB, L3, TMP = range(12)
+    LANE, G16, Q3, PF, ODD, EVEN, WM, WD, MA, MB, L3, GL, E0, E1, WR = range(15)
     iota(C("pi", 0), [[0, 1]], 0, 1)
     iota(R("j3"), [[64, 8], [3, 16]], 0, 0)
     iota(R("jg"), [[16, 8], [0, 16]], 0, 0)
-    iota(R("jrow"), [[1, 272]], 0, 0)
-    iota(R("row48", 0, 54), [[0, 2], [48, 27]], 0, 0)
+    iota(R("jrow"), [[1, 256]], 0, 0)
+    iota(R("row48"), [[0, 2], [48, 28]], 0, 0)
+    iota(C("col", PF), [[0, 1]], 0, 1)
     ts(C("pi", 1), C("pi", 0), 15, OP.bitwise_and)
     cp(C("col", LANE), C("pi", 1))
-    cp(C("col", PF), C("pi", 0))
     tt(C("col", G16), C("col", PF), C("col", LANE), OP.subtract)
     ts(C("col", Q3), C("col", G16), 4.0, OP.mult, C("col", LANE), OP.add)
-    for t in range(2):
-        for e in range(3):
-            ts(R("pm", 128 * (3 * t + e), 128 * (3 * t + e + 1)), R("j3"), C("col", Q3), OP.subtract, float(16 * e - t), OP.is_equal)
+
+    for e in range(3):
+        ts(R("pm", 128 * e, 128 * e + 128), R("j3"), C("col", Q3), OP.subtract, float(16 * e), OP.is_equal)
     ts(R("bo"), R("jg"), C("col", G16), OP.is_equal)
-    tag[0] = -1
     ts(C("pi", 2), C("pi", 0), 1, OP.bitwise_and)
     cp(C("col", ODD), C("pi", 2))
-    ts(C("col", EVEN), C("col", ODD), -256.0, OP.mult, 256.0, OP.add)
-    ts(R("tb7"), R("jrow", 0, 8), C("col", EVEN), OP.mult)
+    act(C("col", EVEN), C("col", ODD), bias=256.0, scale=-256.0)
+    act(R("tb7"), R("jrow", 0, 8), scale=C("col", EVEN))
     for s in range(7):
-        act(R("tp", 256 * s, 256 * s + 256), R("jrow", 0, 256), AF.Identity, bias=C("tb7", s), scale=C("col", ODD))
-    tag[0] = 0
-    ts(C("col", MA), C("col", LANE), 2.0, OP.is_lt)
-    ts(C("col", WM), C("col", LANE), 4.0, OP.is_lt, 0.5, OP.mult)
-    tt(C("col", WD), C("col", MA), C("col", WM), OP.subtract)
-    ts(C("col", MB), C("col", WM), 2.0, OP.mult, C("col", MA), OP.subtract)
-    ts(C("col", L3), C("col", LANE), 3.0, OP.mult)
+        act(R("tp", 256 * s, 256 * s + 256), R("jrow"), bias=C("tb7", s), scale=C("col", ODD))
+    ts(R("under"), R("jrow", 0, 16), C("col", LANE), OP.is_gt)
+    act(C("col", MB), C("under", 2), bias=C("under", 4), scale=-1.0)
+    act(C("col", WM), C("col", MB), scale=256.0)
+    act(C("col", L3), C("col", MB), scale=-256.0)
+    act(C("col", WD), C("under", 2), bias=C("col", L3), scale=256.0)
+    act(C("col", MA), C("col", LANE), scale=3.0)
+    act(R("row48"), R("row48"), bias=C("col", MA))
+    act(C("colb", 0), C("col", LANE))
     ts(R("idb"), R("jrow", 0, 128), C("col", PF), OP.is_equal)
-    ts(R("idf"), R("jrow", 0, 128), C("col", PF), OP.is_equal)
-    ts(R("idn"), R("idb"), -1.0, OP.mult)
-    ts(R("id16"), R("idb"), 16.0, OP.mult)
-    ts(R("da"), R("idb"), C("col", MA), OP.mult)
-    ts(R("db"), R("idb"), C("col", MB), OP.mult)
-    ts(R("z1"), R("jrow", 0, 144), C("col", G16), OP.subtract, 15.0, OP.is_equal)
-    ts(R("zm"), R("z1"), C("col", WM), OP.mult)
-    ts(R("zd"), R("z1"), C("col", WD), OP.mult)
-    ts(R("zl"), R("z1"), C("col", LANE), OP.mult)
-    add("g", "asel", (R("tri"), R("bo"), [[-1, 128]], OP.is_gt, 0.0, 0, 1), [R("tri")], [R("bo")], 0.43)
-    ts(R("klist"), R("jrow", 0, 16), 16.0, OP.mult, C("col", LANE), OP.add)
+    for name, f in (("i256", 1.0 / 256), ("da", C("under", 2)), ("db", C("col", MB)), ("idf", 1.0), ("idn", -1.0), ("m256", 256.0),
+                    ("id16", 16.0), ("idh", 0.5), ("idg", 0.5)):
+        act(R(name), R("idb"), scale=f)
+    iota(R("z1"), [[0, 144]], 0, 0)
+    act(R("z1", 15, 143, 16), R("bo", 0, 128, 16))
+    for name, c in (("zm", WM), ("zd", WD), ("zl", LANE)):
+        act(R(name), R("z1"), scale=C("col", c))
+    ms(R("lf"), 0.0)
     ms(R("coff"), OFF)
-    ts(R("idh"), R("idb"), 0.5, OP.mult)
-    ts(R("idg"), R("idf"), 0.5, OP.mult)
-    for k in range(4):
-        ms(R("ae", 448 * k, 448 * k + 448), 0.0)
-    for nme in ("be", "ne"):
-        for k in range(2):
-            iota(R(nme, 896 * k, 896 * k + 896), [[0, 896]], 0, 0)
+    for k in range(2):
+        ms(R("ae", 896 * k, 896 * k + 896), 0.0)
+    for name in ("be", "ne"):
+        for k in range(4):
+            iota(R(name, 448 * k, 448 * k + 448), [[0, 448]], 0, 0)
     ms(R("a", V, 1296), 0.0)
-    ms(R("b", V, 1296), 0.0)
-    ms(R("lf", 80, 243, 81), 0.0)
-    ms(R("u", K, V), 0.0)
-    ms(R("v", K, V), 0.0)
-    ms(R("on", 64, 80), 1.0)
-    ms(R("flm", 64, 80), 0.0)
-    ms(R("one"), 1.0)
-    ms(R("c256"), 256.0)
-    iota(R("rst"), [[0, 1280]], 1, 0)
-    ms(R("rst", 0, 1280, 80), 0.0)
-    iota(R("dd0", 0, K), [[0, K]], 0, 0)
-    iota(R("dd1", 0, K), [[0, K]], 0, 0)
+    iota(R("b", V, 1296), [[0, 16]], 0, 0)
+    iota(R("dz"), [[0, 128]], 0, 0)
+    for k in range(3):
+        iota(R("lv", 432 * k, 432 * k + 432), [[0, 432]], 1, 0)
+    asel(R("tri"), R("bo"), [[-1, 128]], OP.is_gt, 0.0, 0, 1)
+    asel(R("tri"), R("tri"), [[-1, 128]], OP.not_equal, 2048.0, 0, 1)
+    for e in range(3):
+        asel(R("pm", 128 * e + 384, 128 * e + 512), R("bo"), [[16, 8], [3, 16]], OP.is_equal, 0.0, 1 - 16 * e, -1)
+    iota(R("one"), [[0, 32]], 1, 0)
+    iota(R("krow"), [[1, 256]], -2047, 0)
+    iota(R("rst"), [[0, 512]], 1, 0)
+    asel(R("rst"), R("rst"), [[0, 16], [1, 32]], OP.is_gt, 0.0, 0, 0)
+    iota(R("klist"), [[16, 80]], 0, 0)
+    act(R("klist"), R("klist"), bias=C("col", LANE))
+    iota(R("c256"), [[0, 64]], 256, 0)
+    for k in range(2):
+        iota(R("dd", 512 * k, 512 * k + 512), [[0, 512]], 0, 0)
 
     def perm(out, t, a, b):
         mm(out, [(R("pm", 128 * (3 * t + e), 128 * (3 * t + e + 1)), R("lf", a + e, b, 3)) for e in range(3)])
 
     cp(R("lf", 0, 80), R("li", 0, 80))
-    perm(R("s0", 128, 155), 0, 0, 81)
-    cp(R("su0", 0, 27), R("s0", 128, 155))
-    ts(R("thf"), R("li", 304, 306), 0.5, OP.add)
+    perm(R("s0", 128, 156), 0, 0, 84)
+    cp(R("su0"), R("s0", 128, 156))
+    UNIT = (1.0, 1.0 / 256)
+    for k in range(2):
+        ts(R("colb", 2 + 2 * k, 4 + 2 * k), R("li", 304, 306), 1.0 - 2 * k, OP.mult)
+    act(R("colb", 3, 6, 2), R("colb", 3, 6, 2), scale=UNIT[1])
     cp(R("fu"), R("li", 240, 304))
-    cp(R("fl"), R("li", 240, 304))
-    cp(R("lf", 81, 161), R("li", 80, 160))
-    cp(R("lf", 162, 242), R("li", 160, 240))
+    cp(fl(), R("li", 240, 304))
+    cp(R("lf", 84, 164), R("li", 80, 160))
+    cp(R("lf", 168, 248), R("li", 160, 240))
 
     def jr(t, b):
         return -((t - BL * b) // 3), -((t - BL * (b + 1)) // 3)
@@ -252,235 +280,337 @@ def build():
     def first(t, b):
         return (jr(t, b)[0] // 16) * 16
 
-    ms(R("nsb", 27, 112, 28), 0.0)
-
     def tables(t):
-        bank = "s%d" % t
-        perm(R(bank, 160, 214), t, 81, 243)
-        tt(R("dtmp", 0, 54), R(bank, 160, 214), R("row48", 0, 54), OP.subtract)
+        mine = (SUB * t, SUB * t + SUB)
+        act(R("ac", *mine), R("a", t, 1296, 3), bias=128.0 * UNIT[t], scale=UNIT[t])
+        act(R("bs", *mine), R("b", t, 1296, 3), scale=65536.0)
+        both = R(("s1", "d1")[t], 160, 216)
+        perm(both, t, 84, 252)
+        tt(R("dtmp"), both, R("row48"), OP.subtract)
+        act(R("nsb", 56 * t, 56 * t + 56), both)
+        ts(R("du"), R("dtmp"), float(-t), OP.add)
         for k in range(2):
-            ts(R("du%d" % t, 28 * k, 28 * k + 27), R("dtmp", 27 * k, 27 * k + 27), C("col", L3), OP.subtract, float(-t), OP.add)
-        act(R("ga"), IND(R("tp"), R("du%d" % t, 0, 27)), AF.Copy)
-        act(R("gb"), IND(R("tp"), R("du%d" % t, 28, 55)), AF.Copy)
-        for k in range(2):
-            o = 56 * t + 28 * k
-            cp(R("nsb", o, o + 27), R(bank, 160 + 27 * k, 187 + 27 * k))
-            for b in range(4):
-                c0, g0 = o + first(t, b) // 16, 32 * b + 16 * t + 8 * k
-                ts(R("gu", g0, g0 + 8), R("nsb", c0, c0 + 8), float(-BL * (b + 1)), OP.add)
-        mm(R("d1", 0, SUB), [(R("da"), R("ga")), (R("db"), R("gb"))])
-        act(R("ns%d" % t), R("d1", 0, SUB), AF.Copy)
+            act(R("ga", SUB * k, SUB * k + SUB), IND(R("tp"), R("du", 28 * k, 28 * k + 27)), AF.Copy)
+        both = R(("s0", "d0")[t], 0, SUB)
+        mm(both, [(R("da"), R("ga", 0, SUB)), (R("db"), R("ga", SUB))])
+        act(R("ns", *mine), both, AF.Copy)
 
-    def sums():
-        for k in range(2):
-            for q in range(4):
-                mm(R("x%d" % q, 256 * k, 256 * k + 256), [(R("idb"), R("coff")), (R("idb"), R("uv"[k], 256 * q, 256 * q + 256))])
+    def collapse(t, win, off):
+        for i, (c0, c1) in enumerate(PARTS):
+            p, bank = (16 * c0, 16 * c1), "d%d" % (1 - i)
+            tt(R("cd", *p), IND(win, R(off[0], off[1] + c0, off[1] + c1)), R("ac", SUB * t + p[0], SUB * t + p[1]), OP.subtract)
+            ts(R("c1", *p), R("cd", *p), C("colb", 4 + t), OP.is_ge)
+            ts(R("c2", *p), R("cd", *p), C("colb", 2 + t), OP.is_le)
+            mm(R(bank, *p), [(R("bo"), R("c1", *p)), (R("bo"), R("c2", *p))])
+            ts(R(bank, *p), R(bank, *p), 24.5, OP.is_ge, 1.0 / 256, OP.mult)
+        for tab, src in (("ae", "a"), ("be", "bs"), ("ne", "ns")):
+            for i, (c0, c1) in enumerate(PARTS):
+                j0, j1 = 16 * c0, min(16 * c1, 427)
+                f = (3 * j0 + t, 3 * (j1 - 1) + t + 1, 3)
+                tt(R(tab, *f), R("d%d" % (1 - i), j0, j1), R(src, *f) if src == "a" else R(src, SUB * t + j0, SUB * t + j1), OP.mult)
+        for i, (c0, c1) in enumerate(PARTS):
+            j0, j1 = 16 * c0, min(16 * c1, 427)
+            act(R("lv", 3 * j0 + t, 3 * (j1 - 1) + t + 1, 3), R("d%d" % (1 - i), j0, j1), bias=1.0, scale=-256.0)
 
-    def collapse(t, off):
-        n = 427
-        tt(R("cd"), IND(R("u", 0, K), off), R("a", t, 1296, 3), OP.subtract)
-        act(R("ce"), R("cd"), AF.Abs, bias=-128.0)
-        act(R("cs"), R("ce"), AF.Sign, bias=C("thf", t), scale=-1.0)
-        mm(R("d0", 0, SUB), [(R("bo"), R("cs"))])
-        ts(R("d0", 0, SUB), R("d0", 0, SUB), 1.0, OP.is_ge)
-        tt(R("ae", t, V, 3), R("d0", 0, n), R("a", t, V, 3), OP.mult)
-        tt(R("be", t, V, 3), R("d0", 0, n), R("b", t, V, 3), OP.mult)
-        tt(R("ne", t, V, 3), R("d0", 0, n), R("ns%d" % t, 0, n), OP.mult)
-        act(R("live%d" % t), R("d0", 0, SUB), AF.Identity, bias=1.0, scale=-1.0)
-
-    def scaled(t):
+    def factors(t):
         for b in (3, 2, 1, 0):
-            for k in range(2):
-                o, f = 512 * b + 256 * t + 128 * k, 3 * first(t, b) + t
-                act(R("ab", o, o + 128), R(("ae", "be")[k], f, f + 384, 3), AF.Copy, scale=1.0 / 256)
+            o, f = 512 * b + 256 * t, 3 * first(t, b) + t
+            asel(R("ab", o, o + 128), R("ae", f, f + 384, 3), [[0, 128]], OP.is_ge, 0.0, 0, 0)
+            act(R("ab", o + 128, o + 256), R("be", f, f + 384, 3), scale=1.0 / 65536)
 
-    def hop(c):
-        fu = R("fu", 32 * c, 32 * c + 32)
-        fl = R("fl", 32 * c, 32 * c + 32)
-        gg, sg, bank = R("g%d" % c), R("sg%d" % c), "s%d" % c
-        act(gg, IND(R("ne"), fu), AF.Copy)
-        ext(R(bank, 32, 64), "zd", gg, 32)
-        ext(R(bank, 64, 96), "zm", gg, 32, [(R("idf"), fl)])
-        for q in (2 * c, 2 * c + 1):
-            u, v = R("u", 256 * q, 256 * q + 256), R("v", 256 * q, 256 * q + 256)
-            o = 256 * (q % 2)
-            fq, r = R("fu", 16 * q, 16 * q + 16), R("r%d" % c, o, o + 256)
-            for tab, acc, mul, res, t in (("ae", R("x%d" % q, 0, 256), v, u, R("t0", 256 * q, 256 * q + 256)),
-                                          ("be", R("x%d" % q, 256, 512), u, v, R("t1", 256 * q, 256 * q + 256))):
-                tt(t, IND(R(tab), fq), mul, OP.mult)
-                tt(acc, t, acc, OP.add)
-                act(r, acc, AF.Identity, bias=2.0 ** 31 - 128, scale=1.0 + 2.0 ** -19)
-                act(r, r, AF.Identity, bias=-2.0 ** 31)
-                tt(res, acc, r, OP.subtract)
-            d = R("d%d" % (q % 2), 0, 256)
-            mm(d, [(R("idb"), u), (R("idn"), v)])
-            act(R("sg%d" % c, o, o + 256), d, AF.Sign, bias=0.5)
-        ext(R(bank, 0, 32), "z1", sg, 32)
-        ss, se = R("ss", 32 * c, 32 * c + 32), R("se", 32 * c, 32 * c + 32)
-        act(ss, R(bank, 0, 32), AF.Sign, bias=-1.0)
-        tt(se, ss, R(bank, 32, 64), OP.mult)
-        tt(fl, se, R(bank, 64, 96), OP.add)
-        return fu, fl
+    def shear(how, acc, tab, fq, mul, res, t, r, p, old, big):
+        if tab:
+            tt(t, IND(R(tab), fq), mul, OP.mult)
+        if how[0] == "t":
+            mm(acc, old + [(R("idf"), t)])
+        else:
+            if old:
+                mm(acc, old)
+            tt(acc, t, acc, OP.add)
+        if how[1] == "v":
+            r = R("ki", *p)
+            ts(r, acc, -127.5 / 256, OP.add)
+        else:
+            act(r, acc, bias=big - big / 2 ** 24, scale=1.0 + 2.0 ** -19)
+            act(r, r, bias=-big)
+        tt(res, acc, r, OP.subtract)
 
-    def leave(t):
+    def steps():
+        for h in range(2):
+            act(R("gg", 512 * h, 512 * h + 512), IND(R("ne"), R("fu", 32 * h, 32 * h + 32)), AF.Copy)
+        ext(R("s1", 160, 224), "zd", R("gg"), 64)
+        ext(R("s1", 224, 288), "zm", R("gg"), 64, [(R("idf"), fl())])
+        act(R("dz", 1, 128, 2), R("s1", 160, 224))
+        act(R("dm", 1, 128, 2), R("s1", 224, 288))
+
+    def hop(h, hp, ui, unit, uo, v):
+        if WIDE:
+            p = (512 * h, 512 * h + 512)
+            tt(R("t0", *p), IND(R("ae"), R("fu", 32 * h, 32 * h + 32)), R(v, *p), OP.mult)
+        for q in (2 * h, 2 * h + 1):
+            p, (hu, hv) = (256 * q, 256 * q + 256), SHEAR[q]
+            fq, au, av = R("fu", 16 * q, 16 * q + 16), R("x%d" % q, 0, 256), R("x%d" % q, 256, 512)
+            old = [(R("i256"), R("coff"))] * (hu[1] == "s") + [(R(unit), R(ui, *p))]
+            shear(hu, au, None if WIDE else "ae", fq, R(v, *p), R(uo, *p), R("t0", *p), R("r0", *p), p, old, 2.0 ** 23)
+            old = [(R("idb"), R("coff")), (R("idb"), R(v, *p))] * (hv[0] == "t" or hp == 0)
+            shear(hv, av, "be", fq, R(uo, *p), R(v, *p), R("t1", *p), R("r1", *p), p, old, 2.0 ** 31)
+            mm(au, [(R("m256"), R(uo, *p)), (R("idn"), R(v, *p))])
+            act(R("sg", *p), au, AF.Sign, bias=0.5)
+            early("chunk%d" % q)
+        cnt = R("s%d" % h, 0, 32)
+        ext(cnt, "z1", R("sg", 512 * h), 32)
+        ts(R("dm", 64 * h, 64 * h + 64, 2), cnt, 1.0, OP.is_ge)
+        scan(R("fs", 64 * h, 64 * h + 64), R("dz", 64 * h, 64 * h + 64), R("dm", 64 * h, 64 * h + 64), 0.0)
+        early("half%d" % h)
+
+    def search(h):
+        c, bank = (32 * h, 32 * h + 32), "s%d" % h
+        tot = R(bank, 32, 64)
+        ts(R("on", *c), fl(*c), float(V), OP.is_ge)
+        mm(tot, [(R("bo"), R("on", *c))])
+        mm(R(bank, 64, 96), [(R("tri"), R("on", *c))])
+        scan(R("ci", *c), R("one"), tot, C("cc", 0) if h else 0.0)
+        for e in range(4):
+            if h or not ASIDE:
+                scan(R("cb", 128 * h + 32 * e, 128 * h + 32 * e + 32), R("one"), tot, C("cc", e) if h else -16.0 * e)
+            else:
+                act(R("cb", 32 * e, 32 * e + 32), R("ci", *c), bias=-16.0 * e)
+        if h == 0:
+            act(R("cc"), R("jrow", 0, 4), bias=C("ci", 31), scale=-16.0)
+        for j in range(4):
+            o = 512 * h + 128 * j
+            ts(R("flg", o, o + 128), R("cb", 128 * h, 128 * h + 128), C("colb", 0), OP.subtract, float(64 * j), OP.is_le)
+        scan(R("cq", 512 * h, 512 * h + 512), R("rst"), R("flg", 512 * h, 512 * h + 512), 0.0)
+        tt(R("key", *c), R("ci", *c), R(bank, 64, 96), OP.subtract)
+        act(R("flm", *c), fl(*c), bias=-1536.0)
+
+    def hops(ui, unit, uo, v):
+        steps()
+        for h in range(2):
+            hop(h, 0, ui, unit, uo, v)
+            cp(R("fu", 32 * h, 32 * h + 32), fl(32 * h, 32 * h + 32))
+        steps()
+        for h in range(2):
+            hop(h, 1, uo, "idb", uo, v)
+            search(h)
+
+    NF, KK, PK, PRE, L1, L2 = (R("nf", 64 * k, 64 * k + 64) for k in range(6))
+
+    def leave(t, uo, v):
         sn = "sn%d" % t
-        ts(R("on", 0, 64), R("fl"), float(V), OP.is_ge)
-        mm(R("s0", 256, 336), [(R("bo"), R("on"))])
-        mm(R("s0", 336, 416), [(R("tri"), R("on"))])
-        scan(R("cb", 0, 80), R("one"), R("s0", 256, 336), 0.0)
-        scan(R("cb", 80, 160), R("one"), R("s0", 256, 336), -16.0)
-        scan(R("ci"), R("one"), R("s0", 256, 336), 0.0)
         ts(C("cn", 8 * t + 3), C("ci", 63), float(CAP), OP.min)
         s = send("ct%d" % t, [C("cn", 8 * t + 3)])
+        early("count")
         arrive("a_ct%d" % t, [R("cn", 8 * t + 4, 8 * t + 7)], s, T_CNT)
-        for j in range(8):
-            ts(R("flg", 160 * j, 160 * j + 160), R("cb"), C("col", LANE), OP.subtract, float(32 * j), OP.is_le)
-        scan(R("cq"), R("rst"), R("flg"), 0.0)
-        cp(R("cu"), R("cq", 79, 1280, 80))
-        tt(R("key"), R("ci"), R("s0", 336, 416), OP.subtract)
-        tt(R("keyon"), R("key"), R("on"), OP.mult)
-        ts(R("flm", 0, 64), R("fl"), -1536.0, OP.add)
-        tt(R("oh"), IND(R("keyon"), R("cu")), R("jrow", 1, 257), OP.is_equal)
-        ext(R("s1", 256, 272), "zl", R("oh"), 16, [(R("id16"), R("cq", 79, 1280, 80))])
+        tt(R("cs"), R("cq", 31, 512, 32), R("cq", 543, K, 32), OP.add)
+        ts(R("cu"), R("cs"), 63.0, OP.min)
+        tt(R("oh"), IND(R("key"), R("cu")), R("krow"), OP.is_equal)
+        ext(R("s0", 256, 272), "zl", R("oh"), 16, [(R("id16"), R("cs"))])
         tt(R(sn, 512, 768), IND(R("flm"), R("cu")), R("oh"), OP.mult)
         s = send("fm%d" % t, [R(sn, 512, 768)])
-        arrive("a_fm%d" % t, [R("rc%d" % t, 512, 768)], s, T_RELAY)
-        cp(R("atu"), R("s1", 256, 272))
+        arrive("a_fm%d" % t, [LAND["fm%d" % t]], s, T_RELAY)
+        ts(R("atu"), R("s0", 256, 272), float(K - 1), OP.min)
         if t == 0:
-            act(R(sn, 0, 256), IND(R("u", 0, V), R("atu")), AF.Copy)
-            cp(R(sn, 256, 512), IND(R("v", 0, V), R("atu")))
+            act(R(sn, 0, 256), IND(R(uo, 0, K), R("atu")), AF.Copy)
+            cp(R(sn, 256, 512), IND(R(v, 0, K), R("atu")))
         else:
-            act(R(sn, 0, 256), IND(R("u", 0, V), R("atu")), AF.Identity, bias=-1.0, scale=1.0 / 128)
-            ts(R(sn, 256, 512), IND(R("v", 0, V), R("atu")), -128.0, OP.add, 1.0 / 64, OP.mult)
+            act(R(sn, 0, 256), IND(R(uo, 0, K), R("atu")), bias=-1.0, scale=2.0)
+            ts(R(sn, 256, 512), IND(R(v, 0, K), R("atu")), -128.0, OP.add, 1.0 / 64, OP.mult)
         s = send("uv%d" % t, [R(sn, 0, 512)])
-        arrive("a_u%d" % t, [R("rc%d" % t, 0, 256)], s, T_RELAY)
-        arrive("a_v%d" % t, [R("rc%d" % t, 256, 512)], s, T_RELAY + 0.3)
-        ts(R("kt"), R("on", 0, 64), -2048.0, OP.mult, 2048.0, OP.add)
-        tt(R("key2"), R("kt"), R("keyon", 0, 64), OP.add)
-        ts(R("flq"), R("fl"), -256.0, OP.add)
+        arrive("a_u%d" % t, [LAND["u%d" % t]], s, T_RELAY)
+        arrive("a_v%d" % t, [LAND["v%d" % t]], s, T_RELAY + 0.3)
+        act(R("flq"), fl(), bias=-256.0)
+        act(KK, R("key"), bias=2047.0 + LAND["fm%d" % t][1])
+        tt(PK, R("klist", 0, 64), KK, OP.subtract)
 
-    def enter(t):
-        rc, m = "rc%d" % t, C("mm", t)
+    def least(t):
+        m = C("mm", t)
         rmin(m, R("cn", 8 * t + 3, 8 * t + 7))
-        ts(R("az"), R("klist"), m, OP.is_ge, float(V), OP.mult)
-        tt(R("a2"), R("az"), R("s1", 256, 272), OP.add)
-        cp(R("a2u"), R("a2"))
-        if t == 0:
-            ts(R("si", 0, 107), R("sall", 0, 107), m, OP.add)
-            ts(R("sj", 0, 107), R("si", 0, 107), K - 1, OP.bitwise_and)
-            cp(R("so0", 0, 107), R("sj", 0, 107))
-        else:
-            ts(R("si", 0, 80), R("sall", 0, 80), C("mm", 0), OP.add, m, OP.add)
-            ts(R("sj", 0, 80), R("si", 0, 80), K - 1, OP.bitwise_and)
-            cp(R("so1"), R("sj", 0, 80))
-        ts(R("nf"), R("key2"), m, OP.is_gt)
-        tt(R("pre"), R("nf"), R("flq"), OP.mult)
-        cp(IND(R("u" if t == 0 else "up1"), R("a2u")), R(rc, 0, 256))
-        cp(IND(R("dd%d" % t), R("a2u")), R(rc, 512, 768))
-        if t == 0:
-            cp(IND(R("v"), R("a2u")), R(rc, 256, 512))
-        else:
-            act(R("d1", 0, 256), R(rc, 256, 512), AF.Copy)
-            tt(R("zr"), R("d1", 0, 256), R(rc, 0, 256), OP.mult)
-            add("s", "act", (IND(R("sig"), R("a2u")), R("zr"), AF.Sigmoid, None, None), [IND(R("sig"), R("a2u"))], [R("zr")],
-                0.065 + CY * SCA * 256)
-        ext(R("s0", 416, 480), "z1", R("dd%d" % t), 64, [(R("idb"), R("c256"))])
-        tt(R("fl"), R("pre"), R("s0", 416, 480), OP.add)
-        cp(R("fu"), R("fl"))
+        ts(R("az", 0, 16), R("klist", 0, 16), m, OP.is_ge)
+        tt(R("az", 16, 32), R("az", 0, 16), R("klist", 64, 80), OP.mult)
+        tt(R("az", 32, 48), R("az", 16, 32), R("s0", 256, 272), OP.max)
+        cp(R("a2u"), R("az", 32, 48))
+        ts(NF, R("key"), m, OP.subtract, -2048.0, OP.is_gt)
+        tt(PRE, NF, R("flq"), OP.mult)
+        tt(L1, NF, PK, OP.mult)
+        tt(L2, L1, KK, OP.add)
+        cp(R("loc"), L2)
 
-    def followers(w, rho, b):
-        n = rho + 1
-        tt(R("pq", 512 * b, 512 * b + 256 * n), IND(R(w, BL * (b + 1), W), R("gu", 32 * b, 32 * b + 16 * n)),
-           R("ab", 512 * b, 512 * b + 256 * n), OP.mult)
+    def faces(t):
+        for h in range(2):
+            act(R("gg", 512 * h, 512 * h + 512), IND(R("dd", 0, LAND["fm%d" % t][2]), R("loc", 32 * h, 32 * h + 32)), AF.Copy)
+        ext(R("s0", 416, 480), "z1", R("gg"), 64, [(R("idb"), R("c256"))])
+        tt(fl(), PRE, R("s0", 416, 480), OP.add)
+        cp(R("fu"), fl())
 
-    def heights(rho):
-        w, up, so = "w%d" % rho, "up%d" % rho, "so%d" % rho
-        banks = ("d0", "d1")
-        res = range(rho + 1)
-        old, half = (("h", "idh"), ("w0", "idg"))[rho]
-        followers(w, rho, 3)
-        for b in (3, 2, 1, 0):
-            blk = (BL * b, BL * b + BL)
-            acc = R("x%d" % b, 0, BL)
-            mm(acc, [(R(half), R(old, *blk))], stop=False)
-            if rho == 1 and b == 2:
-                cp(R("xs", *blk), IND(R(up, 0, K), R(so, 20 * b, 20 * b + 20)))
+    def followers(w, b, ts_):
+        for t in ts_:
+            o = 512 * b + 256 * t
+            tt(R("pq", o, o + 256), IND(R(w, BL * (b + 1), W), R("gu", o // 16, o // 16 + 16)), R("ab", o, o + 256), OP.mult)
+
+    def parts(t, b):
+        j0, j1 = jr(t, b)
+        o = 512 * b + 256 * t + j0 - first(t, b)
+        return j0, j1, R("pq", o, o + j1 - j0), R("pq", o + 128, o + 128 + j1 - j0)
+
+    def heights0():
+        for c in range(2):
+            act(R("xs", 640 * c, 640 * c + 640), IND(R(UA, 0, K), R("so0", 40 * c, 40 * c + 40)), bias=-1.0, scale=2.0)
+        for t in (0, 2, 1):
+            n = len(range(t, V, 3))
+            acc = R("d%d" % min(t, 1), 0, n)
+            mm(acc, [(R("idh"), R("h", t, V, 3)), (R("idb"), R("xs", t, V, 3))])
+            if t:
+                act(R("w0", t, V, 3), acc)
+            if t == 0:
+                tt(acc, acc, R("lv", 0, V, 3), OP.mult)
+                act(R("wl", 0, V, 3), acc)
+            elif t == 1:
+                tt(R("wl", 1, V, 3), acc, R("lv", 1, V, 3), OP.mult)
             else:
-                act(R("xs", *blk), IND(R(up, 0, K), R(so, 20 * b, 20 * b + 20)), AF.Copy)
-            mm(acc, [(R("idb"), R("xs", *blk))], start=False)
-            for t in res:
-                j0, j1 = jr(t, b)
-                tt(R(banks[t], j0, j1), R("x%d" % b, 3 * j0 + t - BL * b, BL, 3), R("live%d" % t, j0, j1), OP.mult)
-            act(R(w, *blk), acc, AF.Copy)
+                asel(R("wl", 2, V, 3), R("w0", 2, V, 3), [[0, n]], OP.is_ge, 0.0, 0, 0)
         for b in (3, 2, 1, 0):
-            if b < 3:
-                followers(w, rho, b)
-            for t in res:
-                j0, j1 = jr(t, b)
-                o = 512 * b + 256 * t + j0 - first(t, b)
-                tt(R(banks[t], j0, j1), R(banks[t], j0, j1), R("pq", o, o + j1 - j0), OP.add)
-            for t in res:
-                j0, j1 = jr(t, b)
-                o = 512 * b + 256 * t + 128 + j0 - first(t, b)
-                tt(R(w, 3 * j0 + t, 3 * (j1 - 1) + t + 1, 3), R(banks[t], j0, j1), R("pq", o, o + j1 - j0), OP.add)
+            followers("w0", b, [0])
+            j0, j1, p1, p2 = parts(0, b)
+            tt(R("d0", j0, j1), R("d0", j0, j1), p1, OP.add)
+            tt(R("w0", 3 * j0, 3 * j1 - 2, 3), R("d0", j0, j1), p2, OP.add)
 
-    def hops():
-        for hp in range(2):
-            for c in range(2):
-                tag[0] += 1
-                fu, fl = hop(c)
-                if hp == 0:
-                    cp(fu, fl)
-        tag[0] += 1
+    def own(t, b):
+        j0, j1 = jr(t, b)
+        return 3 * j0 + t, 3 * (j1 - 1) + t + 1, 3
+
+    def local(name, t, b):
+        f = own(t, b)
+        return R(name, f[0] - BL * b, f[1] - BL * b, 3)
+
+    def halves():
+        for b in (3, 2, 1, 0):
+            mm(R("x%d" % b, 0, BL), [(R("idg"), R("wl", BL * b, BL * b + BL))])
+        followers("w1", 3, [0, 1])
+        act(local("c3", 2, 3), local("x3", 2, 3))
+        for t in range(2):
+            tt(local("x3", t, 3), local("x3", t, 3), parts(t, 3)[2], OP.add)
+        for t in range(2):
+            tt(local("c3", t, 3), local("x3", t, 3), parts(t, 3)[3], OP.add)
+
+    def heights1():
+        win = R("up", 0, 16 + K)
+        tt(R("w1", 3 * BL, V), IND(win, R("so1", 60, 80)), R("c3"), OP.add)
+        for b in (2, 1, 0):
+            blk = (BL * b, BL * b + BL)
+            act(R("xs", *blk), IND(win, R("so1", 20 * b, 20 * b + 20)), AF.Copy)
+            mm(R("x%d" % b, 0, BL), [(R("idb"), R("xs", *blk))], start=False)
+            act(R("w1", *own(2, b)), local("x%d" % b, 2, b))
+        for b in (2, 1, 0):
+            followers("w1", b, [0, 1])
+            for t in range(2):
+                tt(local("x%d" % b, t, b), local("x%d" % b, t, b), parts(t, b)[2], OP.add)
+            for t in range(2):
+                tt(R("w1", *own(t, b)), local("x%d" % b, t, b), parts(t, b)[3], OP.add)
 
     tables(0)
     s = send("hs0", [R("h", 0, GH)])
     arrive("a_hs0", [R("hg")], s, T_RELAY + 3)
-    collapse(0, R("su0", 0, 27))
-    sums()
-    hops()
-    leave(0)
-    cp(R("sall", 0, 80), R("li", 0, 80))
-    perm(R("s1", 128, 155), 1, 0, 81)
-    cp(R("sall", 80, 107), R("s1", 128, 155))
+    UA = "ua" if REMAP else "u"
+    collapse(0, R("u", 0, K), ("su0", 0))
+    act(R("sall", 0, 80), R("lf", 0, 80))
+    perm(R("d1", 128, 156), 1, 0, 84)
+    act(R("sall", 80, 108), R("d1", 128, 156))
     tables(1)
-    scaled(0)
+    hops("u", "i256", "u", "v")
+    leave(0, "u", "v")
+    factors(0)
+    iota(R("gcol", 0, 2), [[56, 2]], 0, 0)
+    iota(R("gcol", 2, 8), [[7, 3], [56, 2]], 6, 0)
+    iota(R("grow"), [[BL, 4], [0, 32]], BL, 0)
+    iota(R("up", 0, 16), [[0, 16]], 0, 0)
+    iota(R("ch"), [[0, 256]], -128, 0)
+    act(C("col", GL), C("under", 8), bias=20.0, scale=-20.0)
+    ts(R("go"), R("gcol"), C("col", GL), OP.add, C("col", LANE), OP.add)
+    tt(R("gf"), IND(R("nsb"), R("go")), R("grow"), OP.subtract)
+    cp(R("gu"), R("gf"))
     act(R("w0", V, W), R("hg"), AF.Copy)
-    enter(0)
-    collapse(1, R("so0", 80, 107))
-    sums()
-    for c in range(2):
-        act(R("up0", 512 * c, 512 * c + 512), R("u", 512 * c, 512 * c + 512), AF.Identity, bias=-1.0, scale=1.0 / 128)
-    scaled(1)
-    hops()
-    leave(1)
-    heights(0)
+    least(0)
+    ts(R("si"), R("sall"), C("mm", 0), OP.add)
+    ts(R("sj"), R("si"), K - 1, OP.bitwise_and)
+    cp(R("so0"), R("sj"))
+    faces(0)
+    if REMAP:
+        for k in range(2):
+            iota(R("lw", 512 * k, 512 * k + 512), [[0, 512]], 0, 0)
+        act(C("col", E1), C("under", 1), bias=C("under", 2), scale=-1.0)
+        act(C("col", WR), C("col", E1), bias=C("under", 1), scale=float(K))
+        act(R("zk"), R("z1"), scale=C("col", WR))
+        act(R("kw"), R("jrow"), bias=C("col", E1), scale=C("under", 1))
+        cp(IND(R("lw"), R("a2u")), R("kw"))
+        act(R("ga", 0, SUB), IND(R("lw", 0, K), R("so0", 80, 107)), AF.Copy)
+        ext(R("s1", 0, 27), "zk", R("ga"), 27)
+        tt(R("si", 80, 107), R("s1", 0, 27), R("sj", 80, 107), OP.max)
+        cp(R("su0", 0, 27), R("si", 80, 107))
+    else:
+        cp(IND(R("u"), R("a2u")), LAND["u0"])
+    for q in range(4):
+        for old, new in (("v", "vb"), ("u", "ua"))[:1 + REMAP]:
+            act(R(new, 256 * q, 256 * q + 256), IND(R(old), R("loc", 16 * q, 16 * q + 16)), AF.Copy)
+    if REMAP:
+        collapse(1, R("u"), ("su0", 0))
+    else:
+        collapse(1, R("u", 0, K), ("so0", 80))
+    factors(1)
+    heights0()
     s = send("hs1", [R("w0", 0, GH)])
+    early("hs1")
     arrive("a_hs1", [R("w1", V, W)], s, T_RELAY + 1)
+    ext(R("d0", SUB), "z1", R("lv"), 80)
+    hops(UA, "idb", "ub", "vb")
+    leave(1, "ub", "vb")
     for c in range(2):
-        act(R("up1", 512 * c, 512 * c + 512), R("u", 512 * c, 512 * c + 512), AF.Identity, bias=-1.0, scale=1.0 / 128)
-        act(R("x%d" % c), R("v", 512 * c, 512 * c + 512), AF.Identity, bias=-2.0, scale=1.0 / 64)
-        tt(R("zz", 512 * c, 512 * c + 512), R("x%d" % c), R("up1", 512 * c, 512 * c + 512), OP.mult)
-        act(R("sig", 512 * c, 512 * c + 512), R("zz", 512 * c, 512 * c + 512), AF.Sigmoid, extra=1.3 if c == 0 else 0.0)
-    enter(1)
-    heights(1)
+        act(R("up", 16 + 512 * c, 528 + 512 * c), R("ub", 512 * c, 512 * c + 512), bias=-1.0, scale=2.0)
+    for q in range(4):
+        p, av = (256 * q, 256 * q + 256), R("x%d" % q, 256, 512)
+        mm(av, [(R("idb"), R("ch")), (R("idb"), R("vb", *p))])
+        tt(R("zz", *p), av, R("up", 16 + p[0], 16 + p[1]), OP.mult)
+    for c in range(2):
+        act(R("sig", 512 * c, 512 * c + 512), R("zz", 512 * c, 512 * c + 512), AF.Sigmoid, scale=1.0 / 64, extra=1.3 if c == 0 else 0.0)
+    halves()
+    least(1)
+    ts(R("si", 0, 80), R("sall", 0, 80), C("mm", 0), OP.add, C("mm", 1), OP.add)
+    ts(R("sj", 0, 80), R("si", 0, 80), K - 1, OP.bitwise_and)
+    ts(R("gf", 0, 80), R("sj", 0, 80), 1.0 / 16, OP.mult, 1.0, OP.add)
+    tt(R("gf", 0, 80), R("gf", 0, 80), R("d0", SUB), OP.mult)
+    cp(R("so1"), R("gf", 0, 80))
+    cp(IND(R("up", 16), R("a2u")), LAND["u1"])
+    act(R("s1", 0, 256), LAND["v1"], AF.Copy)
+    tt(R("zr"), R("s1", 0, 256), LAND["u1"], OP.mult)
+    add("s", "act", (IND(R("sig"), R("a2u")), R("zr"), AF.Sigmoid, None, None), [IND(R("sig"), R("a2u"))], [R("zr")],
+        0.065 + CY * SCA * 256)
+    faces(1)
+    heights1()
     for b in (3, 2, 1, 0):
-        mm(R("x3", 0, BL), [(R("idf"), R("w1", BL * b, BL * b + BL))], start=b == 3, stop=b == 0)
-    act(R("oh2"), R("x3", 0, BL), AF.Copy)
-    store("y", "st0", "yh", 0, BL, R("oh2"))
+        mm(R("d0", 0, BL), [(R("idf"), R("w1", BL * b, BL * b + BL))], start=b == 3)
+    act(R("d1"), R("sig", 512, K), AF.Copy)
     for c in range(2):
-        tt(R("plo", 256 * c, 256 * c + 256), IND(R("w1"), R("fu", 16 * c, 16 * c + 16)), R("sig", 256 * c, 256 * c + 256), OP.mult)
-    for c in range(2):
-        act(R("x%d" % c, 0, 256), R("plo", 256 * c, 256 * c + 256), AF.Copy)
-    for c in range(2):
-        tt(R("phi", 256 * c, 256 * c + 256), IND(R("w1"), R("fu", 32 + 16 * c, 48 + 16 * c)), R("sig", 512 + 256 * c, 768 + 256 * c), OP.mult)
-        tt(R("ow", 256 * c, 256 * c + 256), R("x%d" % c, 0, 256), R("phi", 256 * c, 256 * c + 256), OP.add)
-        store("y", "st%d" % (1 + c), "yw", 256 * c, 256 * c + 256, R("ow", 256 * c, 256 * c + 256))
+        p = (256 * c, 256 * c + 256)
+        tt(R("plo", *p), IND(R("w1"), R("fu", 16 * c, 16 * c + 16)), R("sig", *p), OP.mult)
+        act(R("phi", *p), IND(R("w1"), R("fu", 32 + 16 * c, 48 + 16 * c)), AF.Copy)
+        tt(R("d1", *p), R("d1", *p), R("phi", *p), OP.mult)
+        tt(R("ow", *p), R("d1", *p), R("plo", *p), OP.add)
+        store("y", "st%d" % (1 + c), "yw", p[0], p[1], R("ow", *p))
+    act(R("oh2"), R("d0", 0, BL), AF.Copy)
+    store("s", "st0", "yh", 0, BL, R("oh2"))
+    goes_on = {}
+    for n in reversed(nodes):
+        if n["kind"] == "mm":
+            out, pairs, start, stop = n["args"]
+            n["args"] = (out, pairs, start, not goes_on.get(out[0], False))
+            goes_on[out[0]] = not start
     return nodes
 
 
 def _meet(x, y):
-    return x[0] == y[0] and x[1] < y[2] and y[1] < x[2]
+    if x[0] != y[0] or x[1] >= y[2] or y[1] >= x[2]:
+        return False
+    return x[3] != y[3] or (x[1] - y[1]) % x[3] == 0
 
 
 def schedule(nodes):
@@ -489,83 +619,124 @@ def schedule(nodes):
         for m in nodes[:n["id"]]:
             raw = any(_meet(x, y) for x in m["wr"] for y in n["rd"])
             other = any(_meet(x, y) for x in m["wr"] + m["rd"] for y in n["wr"])
-            bank = m["eng"] != n["eng"] and any(_psum(x) and x[0] == y[0] for x in m["wr"] + m["rd"] for y in n["wr"] + n["rd"])
-            group = m["kind"] == n["kind"] == "mm" and not n["args"][2]
-            if raw or bank or (other and not group):
+            bank = any(_psum(x) and x[0] == y[0] for x in m["wr"] + m["rd"] for y in n["wr"] + n["rd"])
+            if raw or other or (bank and m["eng"] != n["eng"]):
                 dep[m["id"]] = True
-            elif other:
+            elif bank and n["kind"] == "mm":
                 dep[m["id"]] = False
         for m in n["after"]:
             dep[m] = False
         n["dep"] = dep
     lastq = {}
     for n in nodes:
-        if n["kind"] in ("load", "send"):
+        if n["kind"] == "load":
             if n["eng"] in lastq and lastq[n["eng"]] not in n["dep"]:
                 n["dep"][lastq[n["eng"]]] = False
             lastq[n["eng"]] = n["id"]
 
-    def gap(m, n):
-        if not n["dep"][m["id"]]:
-            return m["dur"]
-        return m["dur"] + m["lat"] + (LAT_S if m["eng"] == n["eng"] else LAT_X)
-
-    for n in reversed(nodes):
-        n.setdefault("lvl", n["dur"] + n["lat"])
-        for i in n["dep"]:
-            m = nodes[i]
-            m["lvl"] = max(m.get("lvl", m["dur"] + m["lat"]), gap(m, n) + n["lvl"])
-    deps = [[(i, gap(nodes[i], n)) for i in n["dep"]] for n in nodes]
-    users = [[] for n in nodes]
+    above = []
     for n in nodes:
-        for i in n["dep"]:
-            users[i].append(n["id"])
+        far = 0
+        for i, hard in n["dep"].items():
+            if hard and nodes[i]["kind"] != "send":
+                far |= above[i]
+        n["dep"] = {i: hard for i, hard in n["dep"].items() if not far >> i & 1}
+        for i, hard in n["dep"].items():
+            if hard and nodes[i]["kind"] != "send":
+                far |= 1 << i
+        above.append(far)
 
-    def place(prio):
-        busy, at = {}, [0.0] * len(nodes)
-        wait = [len(d) for d in deps]
+    def gaps(same, costs):
+        return [[(i, same[i]["dur"] + (same[i]["lat"] + costs[7 + (nodes[i]["eng"] == n["eng"])] if hard else 0.0))
+                 for i, hard in n["dep"].items()] for n in nodes]
+
+    before = gaps(nodes, COSTS[0])
+    others = [(same, gaps(same, costs)) for same, costs in [(nodes, COSTS[0])] + [(build(c), c) for c in COSTS[1:]]]
+    after = [[] for n in nodes]
+    for n in nodes:
+        for i, d in before[n["id"]]:
+            after[i].append((n["id"], d))
+    chain = [0.0] * len(nodes)
+    for n in reversed(nodes):
+        k = n["id"]
+        chain[k] = max([d + chain[i] for i, d in after[k]] + [n["dur"] + n["lat"]]) + EARLY.get(n["tag"], 0.0)
+
+    def flow():
+        at, free, wait = [0.0] * len(nodes), {"a": 0.0}, [len(x) for x in before]
+        ready = {i: 0.0 for i, c in enumerate(wait) if not c}
+        while ready:
+            can = {i: max(t, free.get(nodes[i]["eng"], 0.0)) for i, t in ready.items()}
+            k = min(can, key=lambda i: (can[i], -chain[i], i))
+            k = max((i for i in can if nodes[i]["eng"] == nodes[k]["eng"] and can[i] <= can[k] + SLACK), key=lambda i: (chain[i], -i))
+            at[k] = can[k]
+            del ready[k]
+            if nodes[k]["eng"] != "a":
+                free[nodes[k]["eng"]] = at[k] + nodes[k]["dur"]
+            for i, d in after[k]:
+                wait[i] -= 1
+                if not wait[i]:
+                    ready[i] = max(at[j] + d for j, d in before[i])
+        return at
+
+    def pack(at, back):
+        need, frees = (after, before) if back else (before, after)
+        busy, new, wait = {}, [0.0] * len(nodes), [len(x) for x in need]
         ready = [i for i, c in enumerate(wait) if not c]
         while ready:
-            k = max(ready, key=lambda i: (prio[i], -i))
+            k = min(ready, key=lambda i: (-at[i] - nodes[i]["dur"], -i) if back else (at[i], i))
             ready.remove(k)
-            t, dur = max([at[i] + d for i, d in deps[k]] + [0.0]), nodes[k]["dur"]
+            dur = nodes[k]["dur"]
+            if back:
+                t = max([d - new[i] for i, d in need[k]] + [dur + nodes[k]["lat"]]) - dur
+            else:
+                t = max([new[i] + d for i, d in need[k]] + [0.0])
             if nodes[k]["eng"] != "a":
                 q = busy.setdefault(nodes[k]["eng"], [])
                 pos = len(q)
-                for j, (a, b) in enumerate(q):
-                    if t + dur <= a + 1e-9:
-                        pos = j
-                        break
-                    t = max(t, b)
+                while pos and q[pos - 1][1] > t:
+                    pos -= 1
+                while pos < len(q) and t + dur > q[pos][0] + 1e-9:
+                    t = max(t, q[pos][1])
+                    pos += 1
                 q.insert(pos, (t, t + dur))
-            at[k] = t
-            for i in users[k]:
+            new[k] = -t - dur if back else t
+            for i, d in frees[k]:
                 wait[i] -= 1
                 if not wait[i]:
                     ready.append(i)
-        return max(at[i] + n["dur"] + n["lat"] for i, n in enumerate(nodes)), at
+        return new
 
-    prio = [n["lvl"] + (15.0 if n["tag"] < 0 else 0.0) for n in nodes]
-    best, at = place(prio)
-    seed = SEED
-    tags = max(n["tag"] for n in nodes) + 1
+    def spans(at):
+        order, out = sorted(range(len(nodes)), key=lambda i: (at[i], i)), []
+        for same, need in others:
+            t, free = [0.0] * len(nodes), {}
+            for k in order:
+                e = nodes[k]["eng"]
+                t[k] = max([t[i] + d for i, d in need[k]] + [free.get(e, 0.0)])
+                if e != "a":
+                    free[e] = t[k] + same[k]["dur"]
+            out.append(max(t[k] + same[k]["dur"] + same[k]["lat"] for k in order))
+        return out
+
+    at = flow()
+    for it in range(PASSES):
+        at = pack(pack(at, True), False)
+    best, seed = sum(spans(at)), SEED
     for it in range(TRIES):
-        trial = list(prio)
         seed = (seed * 1103515245 + 12345) % 2 ** 31
-        mid = best * seed / 2 ** 31
-        if it % 4 == 3:
-            seed = (seed * 1103515245 + 12345) % 2 ** 31
-            pick, step = (seed >> 8) % tags, ((seed >> 16) % 64 - 32) / 10.0
-            trial = [p + (step if n["tag"] == pick else 0.0) for p, n in zip(prio, nodes)]
-        else:
-            for i in range(len(nodes)):
-                if abs(at[i] - mid) < 3:
-                    seed = (seed * 1103515245 + 12345) % 2 ** 31
-                    if (seed >> 8) % 8 == 0:
-                        trial[i] += (seed / 2 ** 31 - 0.5) * (1.0, 3.0, 8.0)[it % 4]
-        span, got = place(trial)
-        if span <= best:
-            best, at, prio = span, got, trial
+        mid, trial = max(at) * seed / 2 ** 31, list(at)
+        for i in range(len(nodes)):
+            if abs(at[i] - mid) < 3:
+                seed = (seed * 1103515245 + 12345) % 2 ** 31
+                if (seed >> 8) % 7 == 0:
+                    trial[i] += (seed / 2 ** 31 - 0.5) * (1.0, 2.0, 4.0)[it % 3]
+        trial = pack(trial, False)
+        if it % 2:
+            trial = pack(pack(trial, True), False)
+        total = sum(spans(trial))
+        if total <= best:
+            best, at = total, trial
+    nodes[0]["spans"] = spans(at)
     for n in nodes:
         n["t"] = at[n["id"]]
     return sorted(nodes, key=lambda x: (x["t"], x["id"]))
@@ -607,9 +778,9 @@ def routes(T, topo):
             out[r, "ct%d" % t] = ([(None, mine, None, [x]) for x in to if topo.may_write(c, cores[x[0]])]
                                   + [(near[1], mine, C("yf", 128 + 4 * t), [x for x in to if not topo.may_write(c, cores[x[0]])])])
             keep = R("yb", 128 + 256 * t, 384 + 256 * t)
-            out[r, "fm%d" % t] = [(beside(nxt), R("sn%d" % t, 512, 768), keep, [(nxt, R("rc%d" % t, 512, 768), "a_fm%d" % t)])]
-            out[r, "uv%d" % t] = [(near[0], R("sn%d" % t, 0, 256), keep, [(nxt, R("rc%d" % t, 0, 256), "a_u%d" % t)]),
-                                  (far[0], R("sn%d" % t, 256, 512), keep, [(nxt, R("rc%d" % t, 256, 512), "a_v%d" % t)])]
+            out[r, "fm%d" % t] = [(beside(nxt), R("sn%d" % t, 512, 768), keep, [(nxt, LAND["fm%d" % t], "a_fm%d" % t)])]
+            out[r, "uv%d" % t] = [(near[0], R("sn%d" % t, 0, 256), keep, [(nxt, LAND["u%d" % t], "a_u%d" % t)]),
+                                  (far[0], R("sn%d" % t, 256, 512), keep, [(nxt, LAND["v%d" % t], "a_v%d" % t)])]
     return out
 
 
@@ -724,7 +895,7 @@ def rank_program(g, core, T, topo):
         elif kind == "ms":
             i = q.memset(ap(a[0]), a[1])
         elif kind == "scan":
-            i = q.tensor_tensor_scan(ap(a[0]), ap(a[1]), ap(a[2]), a[3], OP.mult, OP.add)
+            i = q.tensor_tensor_scan(ap(a[0]), ap(a[1]), ap(a[2]), ap(a[3]), OP.mult, OP.add)
         elif kind == "rmin":
             i = q.tensor_reduce(ap(a[0]), ap(a[1]), AxisListType.X, OP.min)
         elif kind == "act":

@@ -1,3 +1,4 @@
+import math
 from concourse.bass import DstId, RemoteDMATransfer
 from concourse.mybir import AluOpType as OP, AxisListType, ActivationFunctionType as AF
 
@@ -6,6 +7,7 @@ V, GH, BL, K, CAP = 1280, 512, 320, 1024, 256
 W = V + GH
 SUB = 432
 OFF = 131072.0
+LOW = 128.0
 BF, F32, I32, U16 = "bfloat16", "float32", "int32", "uint16"
 
 _SB = {
@@ -18,10 +20,10 @@ _SB = {
     "id16": (BF, 128), "idf": (F32, 128), "da": (BF, 128), "db": (BF, 128), "i256": (BF, 128), "m256": (BF, 128),
     "z1": (BF, 144), "zm": (BF, 144), "zd": (BF, 144), "zl": (BF, 144), "c256": (BF, 64), "one": (F32, 32),
     "rst": (BF, 512), "klist": (F32, 80), "coff": (BF, 256), "ch": (BF, 256), "idh": (BF, 128), "idg": (F32, 128),
-    "a": (BF, 1296), "b": (BF, 1296), "h": (BF, 1296), "u": (BF, V), "v": (BF, V), "ub": (BF, K), "vb": (BF, K),
-    "ua": (BF, K), "lw": (BF, V), "kw": (BF, 256), "zk": (BF, 144),
+    "a": (BF, 1296), "b": (BF, 1296), "h": (BF, 1296), "u": (BF, V), "v": (BF, V), "ub": (BF, K), "vb": (BF, V),
+    "ua": (BF, V), "d2": (BF, V), "lw": (BF, V), "kw": (BF, 256), "zk": (BF, 144),
     "ae": (BF, W), "be": (BF, W), "ne": (BF, W), "tp": (BF, W), "lv": (BF, 1296),
-    "ga": (BF, 2 * SUB), "ns": (BF, 2 * SUB), "ac": (BF, 2 * SUB), "bs": (BF, 2 * SUB),
+    "ga": (BF, 2 * SUB), "ns": (BF, 2 * SUB), "ac": (BF, 2 * SUB), "aq": (BF, 2 * SUB), "f256": (F32, 128),
     "cd": (BF, SUB), "c1": (BF, SUB), "c2": (BF, SUB), "xs": (BF, 1296), "zr": (F32, 256),
     "t0": (F32, K), "t1": (F32, K), "r0": (F32, K), "r1": (F32, K), "ki": (I32, K), "gg": (BF, K), "sg": (BF, K),
     "fs": (F32, 128), "dz": (F32, 128), "dm": (F32, 128), "fu": (U16, 64),
@@ -34,7 +36,7 @@ _SB = {
     "hg": (BF, GH), "w0": (F32, W), "w1": (F32, W), "wl": (F32, V), "c3": (F32, BL),
     "zz": (F32, K), "sig": (F32, V), "plo": (F32, 512), "phi": (F32, 512),
     "oh2": (F32, BL), "ow": (F32, 512),
-    "yb": (BF, 640), "yf": (F32, 136),
+    "yb": (BF, 640), "yf": (F32, 400), "zq": (F32, 256),
 }
 _AT = {}
 for _n, (_d, _w) in list(_SB.items()):
@@ -48,17 +50,19 @@ for _n in ("x0", "x1", "x2", "x3", "d0", "d1", "s0", "s1"):
     SCRATCH[_n] = ("psum", [128, 512], F32)
 
 _LOADS = ["sd", "u0", "ta", "th", "pf", "na", "nb", "v0", "tb", "h0"]
-_MSGS = ["hs0", "ct0", "fm0", "uv0", "hs1", "ct1", "fm1", "uv1"]
-SEMAPHORES = (["ev", "es", "et", "eg", "sent"] + ["l_" + n for n in _LOADS] + ["st0", "st1", "st2"]
+_MSGS = ["hs0", "ct0", "fm0", "u0", "v0", "hs1", "ct1", "fm1", "u1", "v1"]
+SEMAPHORES = (["ev", "es", "et", "eg", "sent"] + ["l_" + n for n in _LOADS] + ["st0", "st1", "st2"] + ["m%d" % k for k in range(12)]
               + ["y_" + m for m in _MSGS] + ["a_hs0", "a_hs1", "a_ct0", "a_ct1", "a_fm0", "a_fm1", "a_u0", "a_v0", "a_u1", "a_v1"])
 
-COSTS = ((0.001, 0.0005, 1.55, 3.2, 4.0, 3.5, 1.4, 0.12, 0.08),
-         (0.0009, 0.00045, 1.2, 2.2, 5.5, 5.0, 2.0, 0.2, 0.1),
-         (0.0012, 0.0007, 1.9, 4.8, 4.0, 3.5, 1.4, 0.12, 0.08))
-TRIES, SEED = 3000, 12345
-REMAP, WIDE, ASIDE = True, False, False
-SHEAR = [("ts", "vs"), ("tv", "vs"), ("ts", "vs"), ("tv", "vs")]
-EARLY = {"chunk0": 0.5, "chunk2": 0.5, "half0": 2.0, "hs1": 5.0, "count": 4.0}
+COSTS = ((0.001, 0.0005, 1.55, 3.2, 4.0, 3.5, 1.2, 0.12, 0.08, 0.2, 0.6),
+         (0.0009, 0.00045, 1.2, 2.2, 5.0, 4.5, 1.6, 0.2, 0.1, 0.45, 1.2),
+         (0.0012, 0.0007, 1.9, 4.8, 4.0, 3.5, 1.2, 0.12, 0.08, 0.2, 0.4))
+ZV, FUSE, LAST = (4, 1, 2), True, ((0, 20), (20, 32))
+TRIES, HEAT, SEED = 160000, 0.7, 22
+REMAP, AHEAD, GG = True, True, 16
+SCAT, REMAP1 = (True, False, True), False
+SHEAR = [[("ts", "vs"), ("ts", "vv"), ("ts", "vs"), ("ts", "vv")]] * 4
+EARLY = {"chunk0": 0.5, "chunk2": 0.5, "half0": 2.0, "hs1": 5.0, "count": 4.0, "tp": 6.0}
 SLACK, PASSES = 0.1, 2
 PARTS = ((0, 14), (14, 27))
 
@@ -95,12 +99,13 @@ def IND(win, off):
 
 
 LAND = {"u0": R("u", K, K + CAP) if REMAP else R("rc", 0, CAP), "v0": R("v", K, K + CAP), "fm0": R("dd", K, K + CAP),
-        "u1": R("rc", CAP, 2 * CAP), "v1": R("rc", 2 * CAP, 3 * CAP), "fm1": R("dd", K + CAP, K + 2 * CAP)}
+        "u1": R("up", 16 + K, 16 + V) if REMAP1 else R("rc", CAP, 2 * CAP), "v1": R("zq"), "fm1": R("dd", K + CAP, K + 2 * CAP)}
 
 
 def build(costs=COSTS[0]):
     CY, PCY, GAT, SCA, T_RELAY, T_CNT, T_DMA = costs[:7]
-    nodes = []
+    T_ROWS, T_SEND = costs[9:]
+    nodes, queued = [], [0.0]
 
     def regs(xs):
         o = []
@@ -161,8 +166,10 @@ def build(costs=COSTS[0]):
         d = sum(PCY * max(64, _n(r)) * (1 if _two(r) else 4) for l, r in pairs) + 0.05
         return add("t", "mm", (out, pairs, start, stop), [out], [x for p in pairs for x in p] + ([] if start else [out]), d)
 
-    def ext(out, z, src, n, more=(), start=True):
-        return mm(out, [(R(z, 15 - i, 143 - i), R(src[0], src[1] + i, src[1] + 16 * n, 16)) for i in range(16)] + list(more), start)
+    def ext(out, z, src, n, more=()):
+        if more:
+            mm(out, list(more))
+        return mm(out, [(R(z, 15 - i, 143 - i), R(src[0], src[1] + i, src[1] + 16 * n, 16)) for i in range(16)], not more)
 
     def iota(out, pat, base, cm):
         return add("g", "iota", (out, pat, base, cm), [out], [], 0.13 + 2 * CY * _n(out))
@@ -170,14 +177,26 @@ def build(costs=COSTS[0]):
     def asel(out, x, pat, op, fill, base, cm):
         return add("g", "asel", (out, x, pat, op, fill, base, cm), [out], [x], 0.17 + 2 * CY * _n(out))
 
+    def move(out, x, us=0.6):
+        sem = "m%d" % sum(n["kind"] == "move" for n in nodes)
+        return add("y", "move", (sem, out, x), [out], [x], 0.06, lat=T_DMA + us)
+
+    def zeros(name):
+        for k in range(2):
+            move(R(name, GH * k, GH * k + GH), R("be", V, W))
+
+    def gcopy(out, x):
+        return asel(out, x, [[0, _n(out)]], OP.is_ge, 0.0, 0, 0)
+
     def load(q, name, out, kb):
-        return add(q, "load", (name, out), [out], [], 0.06, lat=T_DMA + kb / 300.0)
+        queued[0] += kb / 600.0 + T_ROWS
+        return add(q, "load", (name, out), [out], [], 0.06, lat=T_DMA + queued[0])
 
     def store(q, sem, name, a, b, src):
         return add(q, "store", (sem, name, a, b, src), [], [src], 0.06, lat=T_DMA + 0.4)
 
     def send(msg, ins):
-        return add("g", "send", (msg,), [], ins, 0.6)
+        return add("g", "send", (msg,), [], ins, T_SEND)
 
     def arrive(sem, out, snd, lat):
         return add("a", "arrive", (sem,), out, [], 0.0, lat=lat, after=[snd])
@@ -187,14 +206,13 @@ def build(costs=COSTS[0]):
 
     load("y", "sd", R("li", 0, 80), 40)
     load("s", "ta", R("a", 0, V), 320)
-    load("y", "u0", R("u", 0, K), 500)
-    load("s", "th", R("li", 304, 306), 330)
-    load("y", "pf", R("li", 240, 304), 600)
-    load("y", "v0", R("v", 0, K), 800)
-    load("s", "na", R("li", 80, 160), 380)
-    load("s", "nb", R("li", 160, 240), 420)
-    load("y", "tb", R("b", 0, V), 1100)
-    load("y", "h0", R("h", 0, V), 1400)
+    load("y", "u0", R("u", 0, K), 256)
+    load("s", "th", R("li", 304, 306), 1)
+    load("y", "na", R("li", 80, 160), 40)
+    load("s", "nb", R("li", 160, 240), 40)
+    load("y", "pf", R("li", 240, 304), 32)
+    load("y", "v0", R("v", 0, K), 256)
+    load("y", "tb", R("b", 0, V), 320)
 
     LANE, G16, Q3, PF, ODD, EVEN, WM, WD, MA, MB, L3, GL, E0, E1, WR = range(15)
     iota(C("pi", 0), [[0, 1]], 0, 1)
@@ -217,31 +235,34 @@ def build(costs=COSTS[0]):
     act(R("tb7"), R("jrow", 0, 8), scale=C("col", EVEN))
     for s in range(7):
         act(R("tp", 256 * s, 256 * s + 256), R("jrow"), bias=C("tb7", s), scale=C("col", ODD))
+        early("tp")
     ts(R("under"), R("jrow", 0, 16), C("col", LANE), OP.is_gt)
     act(C("col", MB), C("under", 2), bias=C("under", 4), scale=-1.0)
-    act(C("col", WM), C("col", MB), scale=256.0)
-    act(C("col", L3), C("col", MB), scale=-256.0)
-    act(C("col", WD), C("under", 2), bias=C("col", L3), scale=256.0)
+    act(C("col", WD), C("col", MB), bias=C("under", 2), scale=-1.0)
     act(C("col", MA), C("col", LANE), scale=3.0)
     act(R("row48"), R("row48"), bias=C("col", MA))
     act(C("colb", 0), C("col", LANE))
     ts(R("idb"), R("jrow", 0, 128), C("col", PF), OP.is_equal)
-    for name, f in (("i256", 1.0 / 256), ("da", C("under", 2)), ("db", C("col", MB)), ("idf", 1.0), ("idn", -1.0), ("m256", 256.0),
-                    ("id16", 16.0), ("idh", 0.5), ("idg", 0.5)):
+    for name, f in (("da", C("under", 2)), ("db", C("col", MB))):
         act(R(name), R("idb"), scale=f)
     iota(R("z1"), [[0, 144]], 0, 0)
     act(R("z1", 15, 143, 16), R("bo", 0, 128, 16))
-    for name, c in (("zm", WM), ("zd", WD), ("zl", LANE)):
+    for name, c in (("zm", MB), ("zd", WD), ("zl", LANE)):
         act(R(name), R("z1"), scale=C("col", c))
-    ms(R("lf"), 0.0)
-    ms(R("coff"), OFF)
-    for k in range(2):
-        ms(R("ae", 896 * k, 896 * k + 896), 0.0)
-    for name in ("be", "ne"):
-        for k in range(4):
-            iota(R(name, 448 * k, 448 * k + 448), [[0, 448]], 0, 0)
-    ms(R("a", V, 1296), 0.0)
-    iota(R("b", V, 1296), [[0, 16]], 0, 0)
+    for k in range(3):
+        iota(R("lf", 84 * k + 80, 84 * k + 84), [[0, 4]], 0, 0)
+    iota(R("coff"), [[0, 256]], int(OFF), 0)
+    for k in range(4):
+        for name, on_vector in zip(("ae", "be", "ne"), ZV):
+            if k < on_vector:
+                ms(R(name, 448 * k, 448 * k + 448), 0.0)
+            else:
+                iota(R(name, 448 * k, 448 * k + 448), [[0, 448]], 0, 0)
+    load("y", "h0", R("h", 0, V), 320)
+    for name, f in (("i256", 1.0 / 256), ("f256", 1.0 / 256), ("idf", 1.0), ("idn", -1.0), ("id16", 16.0), ("idh", 0.5),
+                    ("idg", 0.5)):
+        asel(R(name), R("be", W - 128, W), [[-1, 128]], OP.not_equal, f, 0, 1)
+    iota(R("a", V, 1296), [[0, 16]], 0, 0)
     iota(R("dz"), [[0, 128]], 0, 0)
     for k in range(3):
         iota(R("lv", 432 * k, 432 * k + 432), [[0, 432]], 1, 0)
@@ -250,14 +271,13 @@ def build(costs=COSTS[0]):
     for e in range(3):
         asel(R("pm", 128 * e + 384, 128 * e + 512), R("bo"), [[16, 8], [3, 16]], OP.is_equal, 0.0, 1 - 16 * e, -1)
     iota(R("one"), [[0, 32]], 1, 0)
-    iota(R("krow"), [[1, 256]], -2047, 0)
+    iota(R("krow"), [[1, 256]], -2047 - int(LOW), 0)
     iota(R("rst"), [[0, 512]], 1, 0)
     asel(R("rst"), R("rst"), [[0, 16], [1, 32]], OP.is_gt, 0.0, 0, 0)
     iota(R("klist"), [[16, 80]], 0, 0)
     act(R("klist"), R("klist"), bias=C("col", LANE))
     iota(R("c256"), [[0, 64]], 256, 0)
-    for k in range(2):
-        iota(R("dd", 512 * k, 512 * k + 512), [[0, 512]], 0, 0)
+    zeros("dd")
 
     def perm(out, t, a, b):
         mm(out, [(R("pm", 128 * (3 * t + e), 128 * (3 * t + e + 1)), R("lf", a + e, b, 3)) for e in range(3)])
@@ -280,10 +300,11 @@ def build(costs=COSTS[0]):
     def first(t, b):
         return (jr(t, b)[0] // 16) * 16
 
+    SPAN = [max(-(-(jr(t, b)[1] - first(t, b)) // 16) for t in range(2)) for b in range(4)]
+
     def tables(t):
         mine = (SUB * t, SUB * t + SUB)
         act(R("ac", *mine), R("a", t, 1296, 3), bias=128.0 * UNIT[t], scale=UNIT[t])
-        act(R("bs", *mine), R("b", t, 1296, 3), scale=65536.0)
         both = R(("s1", "d1")[t], 160, 216)
         perm(both, t, 84, 252)
         tt(R("dtmp"), both, R("row48"), OP.subtract)
@@ -301,31 +322,33 @@ def build(costs=COSTS[0]):
             tt(R("cd", *p), IND(win, R(off[0], off[1] + c0, off[1] + c1)), R("ac", SUB * t + p[0], SUB * t + p[1]), OP.subtract)
             ts(R("c1", *p), R("cd", *p), C("colb", 4 + t), OP.is_ge)
             ts(R("c2", *p), R("cd", *p), C("colb", 2 + t), OP.is_le)
-            mm(R(bank, *p), [(R("bo"), R("c1", *p)), (R("bo"), R("c2", *p))])
-            ts(R(bank, *p), R(bank, *p), 24.5, OP.is_ge, 1.0 / 256, OP.mult)
-        for tab, src in (("ae", "a"), ("be", "bs"), ("ne", "ns")):
+            mm(R(bank, *p), [(R("bo"), R("c1", *p))])
+            mm(R(bank, *p), [(R("bo"), R("c2", *p))], start=False)
+            ts(R(bank, *p), R(bank, *p), 24.5, OP.is_ge)
+        for tab, src in (("ae", "a"), ("be", "b"), ("ne", "ns")):
             for i, (c0, c1) in enumerate(PARTS):
                 j0, j1 = 16 * c0, min(16 * c1, 427)
                 f = (3 * j0 + t, 3 * (j1 - 1) + t + 1, 3)
-                tt(R(tab, *f), R("d%d" % (1 - i), j0, j1), R(src, *f) if src == "a" else R(src, SUB * t + j0, SUB * t + j1), OP.mult)
+                tt(R(tab, *f), R("d%d" % (1 - i), j0, j1), R(src, *f) if src != "ns" else R(src, SUB * t + j0, SUB * t + j1), OP.mult)
         for i, (c0, c1) in enumerate(PARTS):
             j0, j1 = 16 * c0, min(16 * c1, 427)
-            act(R("lv", 3 * j0 + t, 3 * (j1 - 1) + t + 1, 3), R("d%d" % (1 - i), j0, j1), bias=1.0, scale=-256.0)
+            act(R("lv", 3 * j0 + t, 3 * (j1 - 1) + t + 1, 3), R("d%d" % (1 - i), j0, j1), bias=1.0, scale=-1.0)
 
     def factors(t):
+        for k in range(2):
+            act(R("aq", SUB * k, SUB * k + SUB), R(("ae", "be")[k], t, t + 3 * SUB, 3), scale=1.0 / 256)
         for b in (3, 2, 1, 0):
-            o, f = 512 * b + 256 * t, 3 * first(t, b) + t
-            asel(R("ab", o, o + 128), R("ae", f, f + 384, 3), [[0, 128]], OP.is_ge, 0.0, 0, 0)
-            act(R("ab", o + 128, o + 256), R("be", f, f + 384, 3), scale=1.0 / 65536)
+            o, f, n = 512 * b + 256 * t, first(t, b), 16 * SPAN[b]
+            for k in range(2):
+                gcopy(R("ab", o + n * k, o + n * k + n), R("aq", SUB * k + f, SUB * k + f + n))
 
-    def shear(how, acc, tab, fq, mul, res, t, r, p, old, big):
-        if tab:
-            tt(t, IND(R(tab), fq), mul, OP.mult)
+    def shear(how, acc, tab, fq, mul, res, t, r, p, old, big, unit="idf"):
+        if old:
+            mm(acc, old)
+        tt(t, IND(R(tab), fq), mul, OP.mult)
         if how[0] == "t":
-            mm(acc, old + [(R("idf"), t)])
+            mm(acc, [(R(unit), t)], start=False)
         else:
-            if old:
-                mm(acc, old)
             tt(acc, t, acc, OP.add)
         if how[1] == "v":
             r = R("ki", *p)
@@ -336,32 +359,39 @@ def build(costs=COSTS[0]):
         tt(res, acc, r, OP.subtract)
 
     def steps():
-        for h in range(2):
-            act(R("gg", 512 * h, 512 * h + 512), IND(R("ne"), R("fu", 32 * h, 32 * h + 32)), AF.Copy)
+        for c in range(0, 64, GG):
+            act(R("gg", 16 * c, 16 * (c + GG)), IND(R("ne"), R("fu", c, c + GG)), AF.Copy)
         ext(R("s1", 160, 224), "zd", R("gg"), 64)
         ext(R("s1", 224, 288), "zm", R("gg"), 64, [(R("idf"), fl())])
         act(R("dz", 1, 128, 2), R("s1", 160, 224))
         act(R("dm", 1, 128, 2), R("s1", 224, 288))
 
     def hop(h, hp, ui, unit, uo, v):
-        if WIDE:
-            p = (512 * h, 512 * h + 512)
-            tt(R("t0", *p), IND(R("ae"), R("fu", 32 * h, 32 * h + 32)), R(v, *p), OP.mult)
         for q in (2 * h, 2 * h + 1):
-            p, (hu, hv) = (256 * q, 256 * q + 256), SHEAR[q]
+            n = 2 * (v == "vb") + hp
+            p, (hu, hv), raw = (256 * q, 256 * q + 256), SHEAR[n][q], unit == "i256"
             fq, au, av = R("fu", 16 * q, 16 * q + 16), R("x%d" % q, 0, 256), R("x%d" % q, 256, 512)
+            off = hv[1] == "s" or (hp == 0 and SHEAR[n + 1][q][1] == "vs")
+            oldv = ([(R("i256"), R("coff"))] * off + [(R(unit), R(v, *p))]) * (hv[0] == "t" or hp == 0)
+            if oldv and hv[0] == "v":
+                mm(av, oldv)
+                oldv = []
             old = [(R("i256"), R("coff"))] * (hu[1] == "s") + [(R(unit), R(ui, *p))]
-            shear(hu, au, None if WIDE else "ae", fq, R(v, *p), R(uo, *p), R("t0", *p), R("r0", *p), p, old, 2.0 ** 23)
-            old = [(R("idb"), R("coff")), (R("idb"), R(v, *p))] * (hv[0] == "t" or hp == 0)
-            shear(hv, av, "be", fq, R(uo, *p), R(v, *p), R("t1", *p), R("r1", *p), p, old, 2.0 ** 31)
-            mm(au, [(R("m256"), R(uo, *p)), (R("idn"), R(v, *p))])
-            act(R("sg", *p), au, AF.Sign, bias=0.5)
+            shear(hu, au, "ae", fq, R(v, *p), R(uo, *p), R("t0", *p), R("r0", *p), p, old, 2.0 ** 23, "f256" if raw else "idf")
+            ahead = AHEAD and hv[0] == "v"
+            if ahead:
+                mm(au, [(R("idb"), R(uo, *p))])
+            shear(hv, av, "be", fq, R(uo, *p), R(v, *p), R("t1", *p), R("r1", *p), p, oldv, 2.0 ** 23)
+            mm(au, [(R("idb"), R(uo, *p))] * (not ahead) + [(R("idn"), R(v, *p))], start=not ahead)
+            act(R("sg", *p), au, AF.Sign, bias=1.0 / 512)
             early("chunk%d" % q)
-        cnt = R("s%d" % h, 0, 32)
+        p, cnt = (64 * h, 64 * h + 64), R("s%d" % h, 0, 32)
         ext(cnt, "z1", R("sg", 512 * h), 32)
-        ts(R("dm", 64 * h, 64 * h + 64, 2), cnt, 1.0, OP.is_ge)
-        scan(R("fs", 64 * h, 64 * h + 64), R("dz", 64 * h, 64 * h + 64), R("dm", 64 * h, 64 * h + 64), 0.0)
+        ts(R("dm", p[0], p[1], 2), cnt, 1.0, OP.is_ge)
+        scan(R("fs", *p), R("dz", *p), R("dm", *p), 0.0)
         early("half%d" % h)
+        if hp == 0:
+            cp(R("fu", 32 * h, 32 * h + 32), fl(32 * h, 32 * h + 32))
 
     def search(h):
         c, bank = (32 * h, 32 * h + 32), "s%d" % h
@@ -369,26 +399,19 @@ def build(costs=COSTS[0]):
         ts(R("on", *c), fl(*c), float(V), OP.is_ge)
         mm(tot, [(R("bo"), R("on", *c))])
         mm(R(bank, 64, 96), [(R("tri"), R("on", *c))])
-        scan(R("ci", *c), R("one"), tot, C("cc", 0) if h else 0.0)
         for e in range(4):
-            if h or not ASIDE:
-                scan(R("cb", 128 * h + 32 * e, 128 * h + 32 * e + 32), R("one"), tot, C("cc", e) if h else -16.0 * e)
-            else:
-                act(R("cb", 32 * e, 32 * e + 32), R("ci", *c), bias=-16.0 * e)
-        if h == 0:
-            act(R("cc"), R("jrow", 0, 4), bias=C("ci", 31), scale=-16.0)
+            scan(R("cb", 128 * h + 32 * e, 128 * h + 32 * e + 32), R("one"), tot, C("cb", 32 * e + 31) if h else -LOW - 16.0 * e)
         for j in range(4):
             o = 512 * h + 128 * j
-            ts(R("flg", o, o + 128), R("cb", 128 * h, 128 * h + 128), C("colb", 0), OP.subtract, float(64 * j), OP.is_le)
+            ts(R("flg", o, o + 128), R("cb", 128 * h, 128 * h + 128), C("colb", 0), OP.subtract, 64 * j - LOW, OP.is_le)
         scan(R("cq", 512 * h, 512 * h + 512), R("rst"), R("flg", 512 * h, 512 * h + 512), 0.0)
-        tt(R("key", *c), R("ci", *c), R(bank, 64, 96), OP.subtract)
+        tt(R("key", *c), R("cb", 128 * h, 128 * h + 32), R(bank, 64, 96), OP.subtract)
         act(R("flm", *c), fl(*c), bias=-1536.0)
 
     def hops(ui, unit, uo, v):
         steps()
         for h in range(2):
             hop(h, 0, ui, unit, uo, v)
-            cp(R("fu", 32 * h, 32 * h + 32), fl(32 * h, 32 * h + 32))
         steps()
         for h in range(2):
             hop(h, 1, uo, "idb", uo, v)
@@ -398,7 +421,7 @@ def build(costs=COSTS[0]):
 
     def leave(t, uo, v):
         sn = "sn%d" % t
-        ts(C("cn", 8 * t + 3), C("ci", 63), float(CAP), OP.min)
+        ts(C("cn", 8 * t + 3), C("cb", 159), LOW, OP.add, float(CAP), OP.min)
         s = send("ct%d" % t, [C("cn", 8 * t + 3)])
         early("count")
         arrive("a_ct%d" % t, [R("cn", 8 * t + 4, 8 * t + 7)], s, T_CNT)
@@ -411,16 +434,19 @@ def build(costs=COSTS[0]):
         arrive("a_fm%d" % t, [LAND["fm%d" % t]], s, T_RELAY)
         ts(R("atu"), R("s0", 256, 272), float(K - 1), OP.min)
         if t == 0:
-            act(R(sn, 0, 256), IND(R(uo, 0, K), R("atu")), AF.Copy)
-            cp(R(sn, 256, 512), IND(R(v, 0, K), R("atu")))
+            cp(R(sn, 0, 256), IND(R(uo, 0, K), R("atu")))
+            act(R(sn, 256, 512), IND(R(v, 0, K), R("atu")), AF.Copy)
         else:
-            act(R(sn, 0, 256), IND(R(uo, 0, K), R("atu")), bias=-1.0, scale=2.0)
-            ts(R(sn, 256, 512), IND(R(v, 0, K), R("atu")), -128.0, OP.add, 1.0 / 64, OP.mult)
-        s = send("uv%d" % t, [R(sn, 0, 512)])
-        arrive("a_u%d" % t, [LAND["u%d" % t]], s, T_RELAY)
-        arrive("a_v%d" % t, [LAND["v%d" % t]], s, T_RELAY + 0.3)
+            ts(R(sn, 0, 256), IND(R(uo, 0, K), R("atu")), 2.0, OP.mult, -1.0, OP.add)
+            act(R("zr"), IND(R("zz"), R("atu")), scale=-4.0)
+        for k, src in enumerate((R(sn, 0, 256), R("zr") if t else R(sn, 256, 512))):
+            if FUSE and t == 0:
+                s = s if k else send("u0", [R(sn, 0, 512)])
+            else:
+                s = send("uv"[k] + str(t), [src])
+            arrive("a_%s%d" % ("uv"[k], t), [LAND["uv"[k] + str(t)]], s, T_RELAY + 0.4 * (k * t + (FUSE and t == 0)))
         act(R("flq"), fl(), bias=-256.0)
-        act(KK, R("key"), bias=2047.0 + LAND["fm%d" % t][1])
+        act(KK, R("key"), bias=2047.0 + LOW + LAND["fm%d" % t][1])
         tt(PK, R("klist", 0, 64), KK, OP.subtract)
 
     def least(t):
@@ -430,50 +456,54 @@ def build(costs=COSTS[0]):
         tt(R("az", 16, 32), R("az", 0, 16), R("klist", 64, 80), OP.mult)
         tt(R("az", 32, 48), R("az", 16, 32), R("s0", 256, 272), OP.max)
         cp(R("a2u"), R("az", 32, 48))
-        ts(NF, R("key"), m, OP.subtract, -2048.0, OP.is_gt)
+        ts(NF, R("key"), m, OP.subtract, -2048.0 - LOW, OP.is_gt)
         tt(PRE, NF, R("flq"), OP.mult)
         tt(L1, NF, PK, OP.mult)
         tt(L2, L1, KK, OP.add)
         cp(R("loc"), L2)
 
     def faces(t):
-        for h in range(2):
-            act(R("gg", 512 * h, 512 * h + 512), IND(R("dd", 0, LAND["fm%d" % t][2]), R("loc", 32 * h, 32 * h + 32)), AF.Copy)
-        ext(R("s0", 416, 480), "z1", R("gg"), 64, [(R("idb"), R("c256"))])
-        tt(fl(), PRE, R("s0", 416, 480), OP.add)
-        cp(R("fu"), fl())
+        if t == 0 and SCAT[0]:
+            zeros("d2")
+            cp(IND(R("d2"), R("a2u")), LAND["fm0"])
+        else:
+            for q in range(4):
+                act(R("gg", 256 * q, 256 * q + 256), IND(R("dd", 0, LAND["fm%d" % t][2]), R("loc", 16 * q, 16 * q + 16)), AF.Copy)
+        ext(R("s0", 416, 480), "z1", R("d2" if t == 0 and SCAT[0] else "gg"), 64, [(R("idb"), R("c256")), (R("idf"), PRE)])
+        cp(R("fu"), R("s0", 416, 480))
+        if t == 0:
+            act(fl(), R("s0", 416, 480))
 
     def followers(w, b, ts_):
         for t in ts_:
             o = 512 * b + 256 * t
-            tt(R("pq", o, o + 256), IND(R(w, BL * (b + 1), W), R("gu", o // 16, o // 16 + 16)), R("ab", o, o + 256), OP.mult)
+            n = 2 * SPAN[b]
+            tt(R("pq", o, o + 16 * n), IND(R(w, BL * (b + 1), W), R("gu", o // 16, o // 16 + n)), R("ab", o, o + 16 * n), OP.mult)
 
     def parts(t, b):
         j0, j1 = jr(t, b)
-        o = 512 * b + 256 * t + j0 - first(t, b)
-        return j0, j1, R("pq", o, o + j1 - j0), R("pq", o + 128, o + 128 + j1 - j0)
+        o, n = 512 * b + 256 * t + j0 - first(t, b), 16 * SPAN[b]
+        return j0, j1, R("pq", o, o + j1 - j0), R("pq", o + n, o + n + j1 - j0)
 
     def heights0():
-        for c in range(2):
-            act(R("xs", 640 * c, 640 * c + 640), IND(R(UA, 0, K), R("so0", 40 * c, 40 * c + 40)), bias=-1.0, scale=2.0)
+        for b in range(4):
+            act(R("xs", BL * b, BL * b + BL), IND(R(UA, 0, K), R("so0", 20 * b, 20 * b + 20)), bias=-1.0, scale=2.0)
         for t in (0, 2, 1):
             n = len(range(t, V, 3))
             acc = R("d%d" % min(t, 1), 0, n)
             mm(acc, [(R("idh"), R("h", t, V, 3)), (R("idb"), R("xs", t, V, 3))])
             if t:
                 act(R("w0", t, V, 3), acc)
-            if t == 0:
-                tt(acc, acc, R("lv", 0, V, 3), OP.mult)
-                act(R("wl", 0, V, 3), acc)
-            elif t == 1:
-                tt(R("wl", 1, V, 3), acc, R("lv", 1, V, 3), OP.mult)
+            if t < 2:
+                tt(R("wl", t, V, 3), acc, R("lv", t, V, 3), OP.mult)
             else:
-                asel(R("wl", 2, V, 3), R("w0", 2, V, 3), [[0, n]], OP.is_ge, 0.0, 0, 0)
+                gcopy(R("wl", 2, V, 3), R("w0", 2, V, 3))
         for b in (3, 2, 1, 0):
             followers("w0", b, [0])
             j0, j1, p1, p2 = parts(0, b)
-            tt(R("d0", j0, j1), R("d0", j0, j1), p1, OP.add)
-            tt(R("w0", 3 * j0, 3 * j1 - 2, 3), R("d0", j0, j1), p2, OP.add)
+            mm(R("d0", j0, j1), [(R("idf"), R("wl", 3 * j0, 3 * j1 - 2, 3))])
+            mm(R("d0", j0, j1), [(R("idf"), p1), (R("idf"), p2)], start=False)
+            act(R("w0", 3 * j0, 3 * j1 - 2, 3), R("d0", j0, j1))
 
     def own(t, b):
         j0, j1 = jr(t, b)
@@ -484,17 +514,16 @@ def build(costs=COSTS[0]):
         return R(name, f[0] - BL * b, f[1] - BL * b, 3)
 
     def halves():
-        for b in (3, 2, 1, 0):
-            mm(R("x%d" % b, 0, BL), [(R("idg"), R("wl", BL * b, BL * b + BL))])
         followers("w1", 3, [0, 1])
-        act(local("c3", 2, 3), local("x3", 2, 3))
-        for t in range(2):
-            tt(local("x3", t, 3), local("x3", t, 3), parts(t, 3)[2], OP.add)
-        for t in range(2):
-            tt(local("c3", t, 3), local("x3", t, 3), parts(t, 3)[3], OP.add)
+        for t in (2, 0, 1):
+            acc = R("x3", 128 * t, 128 * t + _n(R("wl", *own(t, 3))))
+            mm(acc, [(R("idg"), R("wl", *own(t, 3)))] + [(R("idf"), x) for x in (parts(t, 3)[2:] if t < 2 else ())])
+            act(local("c3", t, 3), acc)
+        for b in (2, 1, 0):
+            mm(R("x%d" % b, 0, BL), [(R("idg"), R("wl", BL * b, BL * b + BL))])
 
     def heights1():
-        win = R("up", 0, 16 + K)
+        win = R("up", 0, 16 + (V if REMAP1 else K))
         tt(R("w1", 3 * BL, V), IND(win, R("so1", 60, 80)), R("c3"), OP.add)
         for b in (2, 1, 0):
             blk = (BL * b, BL * b + BL)
@@ -510,7 +539,7 @@ def build(costs=COSTS[0]):
 
     tables(0)
     s = send("hs0", [R("h", 0, GH)])
-    arrive("a_hs0", [R("hg")], s, T_RELAY + 3)
+    arrive("a_hs0", [R("hg")], s, T_RELAY + 20)
     UA = "ua" if REMAP else "u"
     collapse(0, R("u", 0, K), ("su0", 0))
     act(R("sall", 0, 80), R("lf", 0, 80))
@@ -524,20 +553,22 @@ def build(costs=COSTS[0]):
     iota(R("gcol", 2, 8), [[7, 3], [56, 2]], 6, 0)
     iota(R("grow"), [[BL, 4], [0, 32]], BL, 0)
     iota(R("up", 0, 16), [[0, 16]], 0, 0)
-    iota(R("ch"), [[0, 256]], -128, 0)
-    act(C("col", GL), C("under", 8), bias=20.0, scale=-20.0)
-    ts(R("go"), R("gcol"), C("col", GL), OP.add, C("col", LANE), OP.add)
+    iota(R("ch"), [[0, 256]], 128, 0)
+    for n in sorted(set(SPAN)):
+        act(C("col", GL + n), C("under", n), bias=28.0 - n, scale=n - 28.0)
+        act(C("col", GL + n), C("col", GL + n), bias=C("col", LANE))
+    for b in range(4):
+        ts(R("go", 2 * b, 2 * b + 2), R("gcol", 2 * b, 2 * b + 2), C("col", GL + SPAN[b]), OP.add, 111.0, OP.min)
     tt(R("gf"), IND(R("nsb"), R("go")), R("grow"), OP.subtract)
     cp(R("gu"), R("gf"))
-    act(R("w0", V, W), R("hg"), AF.Copy)
+    gcopy(R("w0", V, W), R("hg"))
     least(0)
     ts(R("si"), R("sall"), C("mm", 0), OP.add)
     ts(R("sj"), R("si"), K - 1, OP.bitwise_and)
     cp(R("so0"), R("sj"))
     faces(0)
     if REMAP:
-        for k in range(2):
-            iota(R("lw", 512 * k, 512 * k + 512), [[0, 512]], 0, 0)
+        zeros("lw")
         act(C("col", E1), C("under", 1), bias=C("under", 2), scale=-1.0)
         act(C("col", WR), C("col", E1), bias=C("under", 1), scale=float(K))
         act(R("zk"), R("z1"), scale=C("col", WR))
@@ -549,9 +580,13 @@ def build(costs=COSTS[0]):
         cp(R("su0", 0, 27), R("si", 80, 107))
     else:
         cp(IND(R("u"), R("a2u")), LAND["u0"])
-    for q in range(4):
-        for old, new in (("v", "vb"), ("u", "ua"))[:1 + REMAP]:
-            act(R(new, 256 * q, 256 * q + 256), IND(R(old), R("loc", 16 * q, 16 * q + 16)), AF.Copy)
+    for old, new, scat in (("v", "vb", SCAT[1]), ("u", "ua", SCAT[2]))[:1 + REMAP]:
+        if scat:
+            move(R(new, 0, K), R(old, 0, K))
+            cp(IND(R(new), R("a2u")), LAND[old + "0"])
+        else:
+            for q in range(4):
+                act(R(new, 256 * q, 256 * q + 256), IND(R(old), R("loc", 16 * q, 16 * q + 16)), AF.Copy)
     if REMAP:
         collapse(1, R("u"), ("su0", 0))
     else:
@@ -563,36 +598,50 @@ def build(costs=COSTS[0]):
     arrive("a_hs1", [R("w1", V, W)], s, T_RELAY + 1)
     ext(R("d0", SUB), "z1", R("lv"), 80)
     hops(UA, "idb", "ub", "vb")
-    leave(1, "ub", "vb")
     for c in range(2):
         act(R("up", 16 + 512 * c, 528 + 512 * c), R("ub", 512 * c, 512 * c + 512), bias=-1.0, scale=2.0)
     for q in range(4):
         p, av = (256 * q, 256 * q + 256), R("x%d" % q, 256, 512)
-        mm(av, [(R("idb"), R("ch")), (R("idb"), R("vb", *p))])
+        mm(av, [(R("i256"), R("ch")), (R("idn"), R("vb", *p))])
         tt(R("zz", *p), av, R("up", 16 + p[0], 16 + p[1]), OP.mult)
+    leave(1, "ub", "vb")
     for c in range(2):
-        act(R("sig", 512 * c, 512 * c + 512), R("zz", 512 * c, 512 * c + 512), AF.Sigmoid, scale=1.0 / 64, extra=1.3 if c == 0 else 0.0)
+        act(R("sig", 512 * c, 512 * c + 512), R("zz", 512 * c, 512 * c + 512), AF.Sigmoid, scale=-4.0, extra=1.3 if c == 0 else 0.0)
     halves()
     least(1)
     ts(R("si", 0, 80), R("sall", 0, 80), C("mm", 0), OP.add, C("mm", 1), OP.add)
     ts(R("sj", 0, 80), R("si", 0, 80), K - 1, OP.bitwise_and)
     ts(R("gf", 0, 80), R("sj", 0, 80), 1.0 / 16, OP.mult, 1.0, OP.add)
-    tt(R("gf", 0, 80), R("gf", 0, 80), R("d0", SUB), OP.mult)
-    cp(R("so1"), R("gf", 0, 80))
-    cp(IND(R("up", 16), R("a2u")), LAND["u1"])
-    act(R("s1", 0, 256), LAND["v1"], AF.Copy)
-    tt(R("zr"), R("s1", 0, 256), LAND["u1"], OP.mult)
-    add("s", "act", (IND(R("sig"), R("a2u")), R("zr"), AF.Sigmoid, None, None), [IND(R("sig"), R("a2u"))], [R("zr")],
+    if REMAP1:
+        cp(R("so0", 0, 80), R("sj", 0, 80))
+        for k in range(2):
+            iota(R("lw", 512 * k, 512 * k + 512), [[0, 512]], 0, 0)
+        act(C("col", WR), C("under", 1), scale=1.0 / 16)
+        act(C("col", WR), C("col", E1), bias=C("col", WR), scale=(K + 16) / 16)
+        act(R("zk"), R("z1"), scale=C("col", WR))
+        cp(IND(R("lw"), R("a2u")), R("kw"))
+        for c0, c1 in ((60, 80), (0, 60)):
+            for c in range(c1 - 20, c0 - 1, -20):
+                act(R("xs", 16 * c, 16 * c + BL), IND(R("lw", 0, K), R("so0", c, c + 20)), AF.Copy)
+            ext(R("s1", c0, c1), "zk", R("xs", 16 * c0), c1 - c0)
+            tt(R("gf", c0, c1), R("s1", c0, c1), R("gf", c0, c1), OP.max)
+            tt(R("gf", c0, c1), R("gf", c0, c1), R("d0", SUB + c0, SUB + c1), OP.mult)
+            cp(R("so1", c0, c1), R("gf", c0, c1))
+    else:
+        tt(R("gf", 0, 80), R("gf", 0, 80), R("d0", SUB), OP.mult)
+        cp(R("so1"), R("gf", 0, 80))
+        cp(IND(R("up", 16), R("a2u")), LAND["u1"])
+    add("s", "act", (IND(R("sig"), R("a2u")), LAND["v1"], AF.Sigmoid, None, None), [IND(R("sig"), R("a2u"))], [LAND["v1"]],
         0.065 + CY * SCA * 256)
     faces(1)
     heights1()
     for b in (3, 2, 1, 0):
         mm(R("d0", 0, BL), [(R("idf"), R("w1", BL * b, BL * b + BL))], start=b == 3)
     act(R("d1"), R("sig", 512, K), AF.Copy)
-    for c in range(2):
-        p = (256 * c, 256 * c + 256)
-        tt(R("plo", *p), IND(R("w1"), R("fu", 16 * c, 16 * c + 16)), R("sig", *p), OP.mult)
-        act(R("phi", *p), IND(R("w1"), R("fu", 32 + 16 * c, 48 + 16 * c)), AF.Copy)
+    for c, (c0, c1) in enumerate(LAST):
+        p = (16 * c0, 16 * c1)
+        tt(R("plo", *p), IND(R("w1"), R("fu", c0, c1)), R("sig", *p), OP.mult)
+        act(R("phi", *p), IND(R("w1"), R("fu", 32 + c0, 32 + c1)), AF.Copy)
         tt(R("d1", *p), R("d1", *p), R("phi", *p), OP.mult)
         tt(R("ow", *p), R("d1", *p), R("plo", *p), OP.add)
         store("y", "st%d" % (1 + c), "yw", p[0], p[1], R("ow", *p))
@@ -620,7 +669,8 @@ def schedule(nodes):
             raw = any(_meet(x, y) for x in m["wr"] for y in n["rd"])
             other = any(_meet(x, y) for x in m["wr"] + m["rd"] for y in n["wr"])
             bank = any(_psum(x) and x[0] == y[0] for x in m["wr"] + m["rd"] for y in n["wr"] + n["rd"])
-            if raw or other or (bank and m["eng"] != n["eng"]):
+            group = bank and m["kind"] == n["kind"] == "mm" and not n["args"][2]
+            if not group and (raw or other or (bank and m["eng"] != n["eng"])):
                 dep[m["id"]] = True
             elif bank and n["kind"] == "mm":
                 dep[m["id"]] = False
@@ -629,7 +679,7 @@ def schedule(nodes):
         n["dep"] = dep
     lastq = {}
     for n in nodes:
-        if n["kind"] == "load":
+        if n["kind"] in ("load", "move"):
             if n["eng"] in lastq and lastq[n["eng"]] not in n["dep"]:
                 n["dep"][lastq[n["eng"]]] = False
             lastq[n["eng"]] = n["id"]
@@ -706,40 +756,78 @@ def schedule(nodes):
                     ready.append(i)
         return new
 
-    def spans(at):
-        order, out = sorted(range(len(nodes)), key=lambda i: (at[i], i)), []
-        for same, need in others:
-            t, free = [0.0] * len(nodes), {}
-            for k in order:
-                e = nodes[k]["eng"]
-                t[k] = max([t[i] + d for i, d in need[k]] + [free.get(e, 0.0)])
-                if e != "a":
-                    free[e] = t[k] + same[k]["dur"]
-            out.append(max(t[k] + same[k]["dur"] + same[k]["lat"] for k in order))
-        return out
+    eng = ["vstgy".find(n["eng"]) if n["eng"] != "a" else n["id"] for n in nodes]
+    ends = [k for k in range(len(nodes)) if not after[k]]
+    rows = [([n["dur"] for n in same], [n["dur"] + n["lat"] for n in same], need) for same, need in others]
+
+    def play(order, row, same=0, old=None):
+        dur, tail, need = row
+        t, held = (list(old[1]), list(old[2])) if old else ([0.0] * len(order), [0] * len(order))
+        free, last = [0.0] * len(nodes), [0] * len(nodes)
+        for k in order[max(0, same - 200):same]:
+            free[eng[k]], last[eng[k]] = t[k] + dur[k], k
+        for k in order[same:]:
+            e = eng[k]
+            s, by = free[e], ~last[e]
+            for i, d in need[k]:
+                if t[i] + d >= s:
+                    s, by = t[i] + d, i
+            t[k], held[k], free[e], last[e] = s, by, s + dur[k], k
+        final = max(ends, key=lambda k: t[k] + tail[k])
+        return t[final] + tail[final], t, held, final
 
     at = flow()
     for it in range(PASSES):
         at = pack(pack(at, True), False)
-    best, seed = sum(spans(at)), SEED
+    roots = []
+    for n in nodes:
+        roots.append(sum(1 << i for i in n["dep"]))
+        for i in n["dep"]:
+            roots[-1] |= roots[i]
+    order = best = sorted(range(len(nodes)), key=lambda i: (at[i], i))
+    plays = [play(order, row) for row in rows]
+    least, seed = sum(x[0] for x in plays), SEED
     for it in range(TRIES):
         seed = (seed * 1103515245 + 12345) % 2 ** 31
-        mid, trial = max(at) * seed / 2 ** 31, list(at)
-        for i in range(len(nodes)):
-            if abs(at[i] - mid) < 3:
-                seed = (seed * 1103515245 + 12345) % 2 ** 31
-                if (seed >> 8) % 7 == 0:
-                    trial[i] += (seed / 2 ** 31 - 0.5) * (1.0, 2.0, 4.0)[it % 3]
-        trial = pack(trial, False)
-        if it % 2:
-            trial = pack(pack(trial, True), False)
-        total = sum(spans(trial))
-        if total <= best:
-            best, at = total, trial
-    nodes[0]["spans"] = spans(at)
+        end, t, held, k = plays[(seed >> 8) % len(rows)]
+        pairs = []
+        while t[k] > 0:
+            if held[k] < 0 and not roots[k] >> ~held[k] & 1:
+                pairs.append((~held[k], k))
+            k = max(held[k], ~held[k])
+        a, b = pairs[(seed >> 12) % len(pairs)]
+        pa, pb = order.index(a), order.index(b)
+        if it % 4 < 2:
+            trial = (order[:pa] + [i for i in order[pa:pb] if roots[b] >> i & 1] + [b]
+                     + [i for i in order[pa:pb] if not roots[b] >> i & 1] + order[pb + 1:])
+        elif it % 4 == 2:
+            stop = max([order.index(i) for i, d in before[a]] + [-1]) + 1
+            if stop >= pa:
+                continue
+            to = stop + (seed >> 4) % (pa - stop)
+            trial, pa = order[:to] + [a] + order[to:pa] + order[pa + 1:], to
+        else:
+            stop = min([order.index(i) for i, d in after[a]] + [len(order)])
+            if stop <= pb:
+                continue
+            to = pb + 1 + (seed >> 4) % (stop - pb)
+            trial = order[:pa] + order[pa + 1:to] + [a] + order[to:]
+        seed = (seed * 1103515245 + 12345) % 2 ** 31
+        allowed, got = -(HEAT * (1 - it / TRIES) + 0.01) * math.log((seed + 1) / 2 ** 31), []
+        for row, old in zip(rows, plays):
+            got.append(play(trial, row, pa, old))
+            allowed -= got[-1][0] - old[0]
+            if allowed < -0.3:
+                break
+        if allowed >= 0:
+            order, plays = trial, got
+            if sum(x[0] for x in got) < least:
+                best, least = trial, sum(x[0] for x in got)
+    at = play(best, rows[0])[1]
+    nodes[0]["spans"] = [play(best, row)[0] for row in rows]
     for n in nodes:
         n["t"] = at[n["id"]]
-    return sorted(nodes, key=lambda x: (x["t"], x["id"]))
+    return [nodes[i] for i in best]
 
 
 _ORDER = []
@@ -778,9 +866,12 @@ def routes(T, topo):
             out[r, "ct%d" % t] = ([(None, mine, None, [x]) for x in to if topo.may_write(c, cores[x[0]])]
                                   + [(near[1], mine, C("yf", 128 + 4 * t), [x for x in to if not topo.may_write(c, cores[x[0]])])])
             keep = R("yb", 128 + 256 * t, 384 + 256 * t)
-            out[r, "fm%d" % t] = [(beside(nxt), R("sn%d" % t, 512, 768), keep, [(nxt, LAND["fm%d" % t], "a_fm%d" % t)])]
-            out[r, "uv%d" % t] = [(near[0], R("sn%d" % t, 0, 256), keep, [(nxt, LAND["u%d" % t], "a_u%d" % t)]),
-                                  (far[0], R("sn%d" % t, 256, 512), keep, [(nxt, LAND["v%d" % t], "a_v%d" % t)])]
+            out[r, "fm%d" % t] = [(near[1], R("sn%d" % t, 512, 768), keep, [(nxt, LAND["fm%d" % t], "a_fm%d" % t)])]
+            out[r, "u%d" % t] = [(near[0], R("sn%d" % t, 0, 256), keep, [(nxt, LAND["u%d" % t], "a_u%d" % t)])]
+            src, keep = ((R("sn0", 256, 512), keep), (R("zr"), R("yf", 144)))[t]
+            out[r, "v%d" % t] = [(far[0], src, keep, [(nxt, LAND["v%d" % t], "a_v%d" % t)])]
+        if FUSE:
+            out[r, "u0"] += out.pop((r, "v0"))
     return out
 
 
@@ -868,6 +959,10 @@ def rank_program(g, core, T, topo):
         if kind == "load":
             q.dma_start(ap(a[1]), T[a[0]][:]).then_inc(T.sem["l_" + a[0]], 16)
             mark[n["id"]] = ("l_" + a[0], 16)
+            continue
+        if kind == "move":
+            q.dma_start(ap(a[1]), ap(a[2])).then_inc(T.sem[a[0]], 16)
+            mark[n["id"]] = (a[0], 16)
             continue
         if kind == "store":
             q.dma_start(T[a[1]][:, a[2]:a[3]], ap(a[4])).then_inc(T.sem[a[0]], 16)

import math
from concourse.bass import DstId, RemoteDMATransfer
from concourse.mybir import AluOpType as OP, AxisListType, ActivationFunctionType as AF

NCORES = 256
V, GH, BL, K, CAP = 1280, 512, 320, 1024, 256
W = V + GH
SUB = 432
OFF = 131072.0
LOW = 128.0
BF, F32, I32, U16 = "bfloat16", "float32", "int32", "uint16"

_SB = {
    "li": (I32, 320), "lf": (F32, 252), "sall": (F32, 108), "si": (I32, 108), "sj": (I32, 108),
    "so0": (U16, 108), "so1": (U16, 80), "su0": (U16, 28),
    "du": (U16, 56), "gu": (U16, 128), "go": (U16, 8), "gf": (F32, 128), "grow": (F32, 128), "gcol": (F32, 8),
    "nsb": (F32, 112), "ab": (BF, 2048), "pq": (F32, 2048), "dtmp": (F32, 56), "row48": (F32, 56),
    "jrow": (F32, 256), "krow": (F32, 256), "j3": (F32, 128), "jg": (F32, 128), "pi": (I32, 4), "col": (F32, 32), "colb": (BF, 8),
    "under": (F32, 16), "ca": (BF, 16), "tb7": (F32, 8), "pm": (F32, 768), "bo": (BF, 128), "tri": (BF, 128), "idb": (BF, 128), "idn": (BF, 128),
    "id16": (BF, 128), "idf": (F32, 128), "da": (BF, 128), "db": (BF, 128), "i256": (BF, 128), "m256": (BF, 128),
    "z1": (BF, 144), "zm": (BF, 144), "zd": (BF, 144), "zl": (BF, 144), "c256": (BF, 64), "one": (F32, 32),
    "rst": (BF, 512), "klist": (F32, 80), "coff": (BF, 256), "ch": (BF, 256), "idh": (BF, 128), "idg": (F32, 128),
    "a": (BF, 1296), "b": (BF, 1296), "h": (BF, 1296), "u": (BF, V), "v": (BF, V), "ub": (BF, K), "vb": (BF, V),
    "ua": (BF, V), "d2": (BF, V), "lw": (BF, V), "kw": (BF, 256), "zk": (BF, 144),
    "ae": (BF, W), "be": (BF, W), "ne": (BF, W), "tp": (BF, W), "lv": (BF, 1296),
    "ga": (BF, 2 * SUB), "ns": (BF, 2 * SUB), "ac": (BF, 2 * SUB), "aq": (BF, 2 * SUB), "f256": (F32, 128),
    "cd": (BF, SUB), "c1": (BF, SUB), "c2": (BF, SUB), "xs": (BF, 1296), "zr": (F32, 256),
    "t0": (F32, K), "t1": (F32, K), "r0": (F32, K), "r1": (F32, K), "ki": (I32, K), "gg": (BF, K), "sg": (BF, K),
    "fs": (F32, 128), "dz": (F32, 128), "dm": (F32, 128), "fu": (U16, 64),
    "on": (BF, 64), "ci": (F32, 64), "cc": (F32, 4), "cb": (BF, 256), "key": (F32, 64), "flm": (F32, 64), "flq": (F32, 64),
    "flg": (BF, K), "cq": (BF, K), "cs": (BF, 16), "cu": (U16, 16),
    "oh": (BF, 256), "atu": (U16, 16), "az": (F32, 48), "a2u": (U16, 16),
    "cn": (F32, 16), "mm": (F32, 4), "nf": (F32, 384), "loc": (U16, 64),
    "sn0": (BF, 768), "sn1": (BF, 768), "rc": (BF, 768),
    "dd": (BF, K + 2 * CAP), "up": (BF, 16 + V),
    "hg": (BF, GH), "w0": (F32, W), "w1": (F32, W), "wl": (F32, V), "c3": (F32, BL),
    "zz": (F32, K), "sig": (F32, V), "plo": (F32, 512), "phi": (F32, 512),
    "oh2": (F32, BL), "ow": (F32, 512),
    "yb": (BF, 640), "yf": (F32, 400), "zq": (F32, 256),
}
_AT = {}
for _n, (_d, _w) in list(_SB.items()):
    if _w <= 144 and _n != "yf":
        _used = _SB.get("all_" + _d, (_d, 0))[1]
        _AT[_n] = ("all_" + _d, _used, _w)
        _SB["all_" + _d] = (_d, _used + -(-_w // 32) * 32)
        del _SB[_n]
SCRATCH = {n: ("sbuf", [128, w], d) for n, (d, w) in _SB.items()}
for _n in ("x0", "x1", "x2", "x3", "d0", "d1", "s0", "s1"):
    SCRATCH[_n] = ("psum", [128, 512], F32)

_LOADS = ["sd", "u0", "ta", "th", "pf", "na", "nb", "v0", "tb", "h0"]
_MSGS = ["hs0", "ct0", "fm0", "u0", "v0", "hs1", "ct1", "fm1", "u1", "v1"]
SEMAPHORES = (["ev", "es", "et", "eg", "sent"] + ["l_" + n for n in _LOADS] + ["st0", "st1", "st2"] + ["m%d" % k for k in range(12)]
              + ["y_" + m for m in _MSGS] + ["a_hs0", "a_hs1", "a_ct0", "a_ct1", "a_fm0", "a_fm1", "a_u0", "a_v0", "a_u1", "a_v1"])

COSTS = ((0.001, 0.0005, 1.55, 3.2, 4.0, 3.5, 1.2, 0.12, 0.08, 0.2, 0.6),
         (0.0009, 0.00045, 1.2, 2.2, 5.0, 4.5, 1.6, 0.2, 0.1, 0.45, 1.2),
         (0.0012, 0.0007, 1.9, 4.8, 4.0, 3.5, 1.2, 0.12, 0.08, 0.2, 0.4))
ZV, FUSE, LAST = (4, 1, 2), True, ((0, 20), (20, 32))
TRIES, HEAT, SEED = 160000, 0.7, 22
REMAP, AHEAD, GG = True, True, 16
SCAT, REMAP1 = (True, False, True), False
SHEAR = [[("ts", "vs"), ("ts", "vv"), ("ts", "vs"), ("ts", "vv")]] * 4
EARLY = {"chunk0": 0.5, "chunk2": 0.5, "half0": 2.0, "hs1": 5.0, "count": 4.0, "tp": 6.0}
SLACK, PASSES = 0.1, 2
PARTS = ((0, 14), (14, 27))


def _two(x):
    return _SB.get(x[0], (F32,))[0] in (BF, U16)


def _psum(x):
    return x[0] not in _SB


def _n(x):
    if x[0] == "@":
        return 16 * _n(x[2])
    return len(range(x[1], x[2], x[3]))


def R(name, a=0, b=None, s=1):
    if name in _AT:
        buf, at, w = _AT[name]
        return (buf, at + a, at + (w if b is None else b), s)
    if b is None:
        b = _SB[name][1] if name in _SB else 512
    return (name, a, b, s)


def C(name, c):
    return R(name, c, c + 1)


def IND(win, off):
    return ("@", win, off)


LAND = {"u0": R("u", K, K + CAP) if REMAP else R("rc", 0, CAP), "v0": R("v", K, K + CAP), "fm0": R("dd", K, K + CAP),
        "u1": R("up", 16 + K, 16 + V) if REMAP1 else R("rc", CAP, 2 * CAP), "v1": R("zq"), "fm1": R("dd", K + CAP, K + 2 * CAP)}


def build(costs=COSTS[0]):
    CY, PCY, GAT, SCA, T_RELAY, T_CNT, T_DMA = costs[:7]
    T_ROWS, T_SEND = costs[9:]
    nodes, queued = [], [0.0]

    def regs(xs):
        o = []
        for x in xs:
            if isinstance(x, tuple):
                o += [x[1], x[2]] if x[0] == "@" else [x]
        return o

    def add(eng, kind, args, out, ins, dur, lat=0.0, after=()):
        rd = regs(ins)
        wr = []
        for x in out:
            if x[0] == "@":
                wr.append(x[1]); rd.append(x[2])
            else:
                wr.append(x)
        nodes.append(dict(eng=eng, kind=kind, args=args, rd=rd, wr=wr, dur=dur, lat=lat, after=list(after), id=len(nodes),
                          tag=""))
        return len(nodes) - 1

    def early(name):
        nodes[-1]["tag"] = name

    def vdur(out, ins, per):
        if out[0] == "@":
            return 0.05 + CY * SCA * _n(out)
        if ins[0][0] == "@":
            return 0.05 + CY * GAT * _n(out)
        return 0.02 + CY * max(64, per * _n(out))

    def tt(out, x, y, op):
        return add("v", "tt", (out, x, y, op), [out], [x, y], vdur(out, [x], 1 if x[0] == "@" or _psum(x) or _psum(y) else 2))

    def ts(out, x, s1, op0, s2=None, op1=None):
        wide = [s for s in (s1, s2) if isinstance(s, tuple) and not _two(s)]
        per = 0.5 if x[0] != "@" and _two(x) and _two(out) and not wide else 1
        return add("v", "ts", (out, x, s1, s2, op0, op1), [out], [x, s1, s2], vdur(out, [x], per))

    def cp(out, x):
        per = 0.5 if x[0] != "@" and out[0] != "@" and _two(x) and _two(out) else 1
        return add("v", "cp", (out, x), [out], [x], vdur(out, [x], per))

    def ms(out, c):
        return add("v", "ms", (out, c), [out], [], vdur(out, [out], 0.5 if _two(out) else 1))

    def scan(out, d0, d1, init):
        per = 0.5 if _two(out) and _two(d0) and _two(d1) else 1
        return add("v", "scan", (out, d0, d1, init), [out], [d0, d1, init], vdur(out, [d0], per))

    def rmin(out, x):
        return add("v", "rmin", (out, x), [out], [x], 0.09)

    def act(out, x, f=AF.Identity, bias=0.0, scale=1.0, extra=0.0):
        d = 0.065 + CY * (GAT * _n(out) if x[0] == "@" else max(64, _n(out))) + extra
        return add("s", "act", (out, x, f, bias, scale), [out], [x, bias, scale], d)

    def mm(out, pairs, start=True, stop=True):
        d = sum(PCY * max(64, _n(r)) * (1 if _two(r) else 4) for l, r in pairs) + 0.05
        return add("t", "mm", (out, pairs, start, stop), [out], [x for p in pairs for x in p] + ([] if start else [out]), d)

    def ext(out, z, src, n, more=()):
        if more:
            mm(out, list(more))
        return mm(out, [(R(z, 15 - i, 143 - i), R(src[0], src[1] + i, src[1] + 16 * n, 16)) for i in range(16)], not more)

    def iota(out, pat, base, cm):
        return add("g", "iota", (out, pat, base, cm), [out], [], 0.13 + 2 * CY * _n(out))

    def asel(out, x, pat, op, fill, base, cm):
        return add("g", "asel", (out, x, pat, op, fill, base, cm), [out], [x], 0.17 + 2 * CY * _n(out))

    def move(out, x, us=0.6):
        sem = "m%d" % sum(n["kind"] == "move" for n in nodes)
        return add("y", "move", (sem, out, x), [out], [x], 0.06, lat=T_DMA + us)

    def zeros(name):
        for k in range(2):
            move(R(name, GH * k, GH * k + GH), R("be", V, W))

    def gcopy(out, x):
        return asel(out, x, [[0, _n(out)]], OP.is_ge, 0.0, 0, 0)

    def load(q, name, out, kb):
        queued[0] += kb / 600.0 + T_ROWS
        return add(q, "load", (name, out), [out], [], 0.06, lat=T_DMA + queued[0])

    def store(q, sem, name, a, b, src):
        return add(q, "store", (sem, name, a, b, src), [], [src], 0.06, lat=T_DMA + 0.4)

    def send(msg, ins):
        return add("g", "send", (msg,), [], ins, T_SEND)

    def arrive(sem, out, snd, lat):
        return add("a", "arrive", (sem,), out, [], 0.0, lat=lat, after=[snd])

    def fl(c0=0, c1=64):
        return R("fs", 2 * c0 + 1, 2 * c1, 2)

    load("y", "sd", R("li", 0, 80), 40)
    load("s", "ta", R("a", 0, V), 320)
    load("y", "u0", R("u", 0, K), 256)
    load("s", "th", R("li", 304, 306), 1)
    load("y", "na", R("li", 80, 160), 40)
    load("s", "nb", R("li", 160, 240), 40)
    load("y", "pf", R("li", 240, 304), 32)
    load("y", "v0", R("v", 0, K), 256)
    load("y", "tb", R("b", 0, V), 320)

    LANE, G16, Q3, PF, ODD, EVEN, WM, WD, MA, MB, L3, GL, E0, E1, WR = range(15)
    iota(C("pi", 0), [[0, 1]], 0, 1)
    iota(R("j3"), [[64, 8], [3, 16]], 0, 0)
    iota(R("jg"), [[16, 8], [0, 16]], 0, 0)
    iota(R("jrow"), [[1, 256]], 0, 0)
    iota(R("row48"), [[0, 2], [48, 28]], 0, 0)
    iota(C("col", PF), [[0, 1]], 0, 1)
    ts(C("pi", 1), C("pi", 0), 15, OP.bitwise_and)
    cp(C("col", LANE), C("pi", 1))
    tt(C("col", G16), C("col", PF), C("col", LANE), OP.subtract)
    ts(C("col", Q3), C("col", G16), 4.0, OP.mult, C("col", LANE), OP.add)

    for e in range(3):
        ts(R("pm", 128 * e, 128 * e + 128), R("j3"), C("col", Q3), OP.subtract, float(16 * e), OP.is_equal)
    ts(R("bo"), R("jg"), C("col", G16), OP.is_equal)
    ts(C("pi", 2), C("pi", 0), 1, OP.bitwise_and)
    cp(C("col", ODD), C("pi", 2))
    act(C("col", EVEN), C("col", ODD), bias=256.0, scale=-256.0)
    act(R("tb7"), R("jrow", 0, 8), scale=C("col", EVEN))
    for s in range(7):
        act(R("tp", 256 * s, 256 * s + 256), R("jrow"), bias=C("tb7", s), scale=C("col", ODD))
        early("tp")
    ts(R("under"), R("jrow", 0, 16), C("col", LANE), OP.is_gt)
    act(C("col", MB), C("under", 2), bias=C("under", 4), scale=-1.0)
    act(C("col", WD), C("col", MB), bias=C("under", 2), scale=-1.0)
    act(C("col", MA), C("col", LANE), scale=3.0)
    act(R("row48"), R("row48"), bias=C("col", MA))
    act(C("colb", 0), C("col", LANE))
    ts(R("idb"), R("jrow", 0, 128), C("col", PF), OP.is_equal)
    for name, f in (("da", C("under", 2)), ("db", C("col", MB))):
        act(R(name), R("idb"), scale=f)
    iota(R("z1"), [[0, 144]], 0, 0)
    act(R("z1", 15, 143, 16), R("bo", 0, 128, 16))
    for name, c in (("zm", MB), ("zd", WD), ("zl", LANE)):
        act(R(name), R("z1"), scale=C("col", c))
    for k in range(3):
        iota(R("lf", 84 * k + 80, 84 * k + 84), [[0, 4]], 0, 0)
    iota(R("coff"), [[0, 256]], int(OFF), 0)
    for k in range(4):
        for name, on_vector in zip(("ae", "be", "ne"), ZV):
            if k < on_vector:
                ms(R(name, 448 * k, 448 * k + 448), 0.0)
            else:
                iota(R(name, 448 * k, 448 * k + 448), [[0, 448]], 0, 0)
    load("y", "h0", R("h", 0, V), 320)
    for name, f in (("i256", 1.0 / 256), ("f256", 1.0 / 256), ("idf", 1.0), ("idn", -1.0), ("id16", 16.0), ("idh", 0.5),
                    ("idg", 0.5)):
        asel(R(name), R("be", W - 128, W), [[-1, 128]], OP.not_equal, f, 0, 1)
    iota(R("a", V, 1296), [[0, 16]], 0, 0)
    iota(R("dz"), [[0, 128]], 0, 0)
    for k in range(3):
        iota(R("lv", 432 * k, 432 * k + 432), [[0, 432]], 1, 0)
    asel(R("tri"), R("bo"), [[-1, 128]], OP.is_gt, 0.0, 0, 1)
    asel(R("tri"), R("tri"), [[-1, 128]], OP.not_equal, 2048.0, 0, 1)
    for e in range(3):
        asel(R("pm", 128 * e + 384, 128 * e + 512), R("bo"), [[16, 8], [3, 16]], OP.is_equal, 0.0, 1 - 16 * e, -1)
    iota(R("one"), [[0, 32]], 1, 0)
    iota(R("krow"), [[1, 256]], -2047 - int(LOW), 0)
    iota(R("rst"), [[0, 512]], 1, 0)
    asel(R("rst"), R("rst"), [[0, 16], [1, 32]], OP.is_gt, 0.0, 0, 0)
    iota(R("klist"), [[16, 80]], 0, 0)
    act(R("klist"), R("klist"), bias=C("col", LANE))
    iota(R("c256"), [[0, 64]], 256, 0)
    zeros("dd")

    def perm(out, t, a, b):
        mm(out, [(R("pm", 128 * (3 * t + e), 128 * (3 * t + e + 1)), R("lf", a + e, b, 3)) for e in range(3)])

    cp(R("lf", 0, 80), R("li", 0, 80))
    perm(R("s0", 128, 156), 0, 0, 84)
    cp(R("su0"), R("s0", 128, 156))
    UNIT = (1.0, 1.0 / 256)
    for k in range(2):
        ts(R("colb", 2 + 2 * k, 4 + 2 * k), R("li", 304, 306), 1.0 - 2 * k, OP.mult)
    act(R("colb", 3, 6, 2), R("colb", 3, 6, 2), scale=UNIT[1])
    cp(R("fu"), R("li", 240, 304))
    cp(fl(), R("li", 240, 304))
    cp(R("lf", 84, 164), R("li", 80, 160))
    cp(R("lf", 168, 248), R("li", 160, 240))

    def jr(t, b):
        return -((t - BL * b) // 3), -((t - BL * (b + 1)) // 3)

    def first(t, b):
        return (jr(t, b)[0] // 16) * 16

    SPAN = [max(-(-(jr(t, b)[1] - first(t, b)) // 16) for t in range(2)) for b in range(4)]

    def tables(t):
        mine = (SUB * t, SUB * t + SUB)
        act(R("ac", *mine), R("a", t, 1296, 3), bias=128.0 * UNIT[t], scale=UNIT[t])
        both = R(("s1", "d1")[t], 160, 216)
        perm(both, t, 84, 252)
        tt(R("dtmp"), both, R("row48"), OP.subtract)
        act(R("nsb", 56 * t, 56 * t + 56), both)
        ts(R("du"), R("dtmp"), float(-t), OP.add)
        for k in range(2):
            act(R("ga", SUB * k, SUB * k + SUB), IND(R("tp"), R("du", 28 * k, 28 * k + 27)), AF.Copy)
        both = R(("s0", "d0")[t], 0, SUB)
        mm(both, [(R("da"), R("ga", 0, SUB)), (R("db"), R("ga", SUB))])
        act(R("ns", *mine), both, AF.Copy)

    def collapse(t, win, off):
        for i, (c0, c1) in enumerate(PARTS):
            p, bank = (16 * c0, 16 * c1), "d%d" % (1 - i)
            tt(R("cd", *p), IND(win, R(off[0], off[1] + c0, off[1] + c1)), R("ac", SUB * t + p[0], SUB * t + p[1]), OP.subtract)
            ts(R("c1", *p), R("cd", *p), C("colb", 4 + t), OP.is_ge)
            ts(R("c2", *p), R("cd", *p), C("colb", 2 + t), OP.is_le)
            mm(R(bank, *p), [(R("bo"), R("c1", *p))])
            mm(R(bank, *p), [(R("bo"), R("c2", *p))], start=False)
            ts(R(bank, *p), R(bank, *p), 24.5, OP.is_ge)
        for tab, src in (("ae", "a"), ("be", "b"), ("ne", "ns")):
            for i, (c0, c1) in enumerate(PARTS):
                j0, j1 = 16 * c0, min(16 * c1, 427)
                f = (3 * j0 + t, 3 * (j1 - 1) + t + 1, 3)
                tt(R(tab, *f), R("d%d" % (1 - i), j0, j1), R(src, *f) if src != "ns" else R(src, SUB * t + j0, SUB * t + j1), OP.mult)
        for i, (c0, c1) in enumerate(PARTS):
            j0, j1 = 16 * c0, min(16 * c1, 427)
            act(R("lv", 3 * j0 + t, 3 * (j1 - 1) + t + 1, 3), R("d%d" % (1 - i), j0, j1), bias=1.0, scale=-1.0)

    def factors(t):
        for k in range(2):
            act(R("aq", SUB * k, SUB * k + SUB), R(("ae", "be")[k], t, t + 3 * SUB, 3), scale=1.0 / 256)
        for b in (3, 2, 1, 0):
            o, f, n = 512 * b + 256 * t, first(t, b), 16 * SPAN[b]
            for k in range(2):
                gcopy(R("ab", o + n * k, o + n * k + n), R("aq", SUB * k + f, SUB * k + f + n))

    def shear(how, acc, tab, fq, mul, res, t, r, p, old, big, unit="idf"):
        if old:
            mm(acc, old)
        tt(t, IND(R(tab), fq), mul, OP.mult)
        if how[0] == "t":
            mm(acc, [(R(unit), t)], start=False)
        else:
            tt(acc, t, acc, OP.add)
        if how[1] == "v":
            r = R("ki", *p)
            ts(r, acc, -127.5 / 256, OP.add)
        else:
            act(r, acc, bias=big - big / 2 ** 24, scale=1.0 + 2.0 ** -19)
            act(r, r, bias=-big)
        tt(res, acc, r, OP.subtract)

    def steps():
        for c in range(0, 64, GG):
            act(R("gg", 16 * c, 16 * (c + GG)), IND(R("ne"), R("fu", c, c + GG)), AF.Copy)
        ext(R("s1", 160, 224), "zd", R("gg"), 64)
        ext(R("s1", 224, 288), "zm", R("gg"), 64, [(R("idf"), fl())])
        act(R("dz", 1, 128, 2), R("s1", 160, 224))
        act(R("dm", 1, 128, 2), R("s1", 224, 288))

    def hop(h, hp, ui, unit, uo, v):
        for q in (2 * h, 2 * h + 1):
            n = 2 * (v == "vb") + hp
            p, (hu, hv), raw = (256 * q, 256 * q + 256), SHEAR[n][q], unit == "i256"
            fq, au, av = R("fu", 16 * q, 16 * q + 16), R("x%d" % q, 0, 256), R("x%d" % q, 256, 512)
            off = hv[1] == "s" or (hp == 0 and SHEAR[n + 1][q][1] == "vs")
            oldv = ([(R("i256"), R("coff"))] * off + [(R(unit), R(v, *p))]) * (hv[0] == "t" or hp == 0)
            if oldv and hv[0] == "v":
                mm(av, oldv)
                oldv = []
            old = [(R("i256"), R("coff"))] * (hu[1] == "s") + [(R(unit), R(ui, *p))]
            shear(hu, au, "ae", fq, R(v, *p), R(uo, *p), R("t0", *p), R("r0", *p), p, old, 2.0 ** 23, "f256" if raw else "idf")
            ahead = AHEAD and hv[0] == "v"
            if ahead:
                mm(au, [(R("idb"), R(uo, *p))])
            shear(hv, av, "be", fq, R(uo, *p), R(v, *p), R("t1", *p), R("r1", *p), p, oldv, 2.0 ** 23)
            mm(au, [(R("idb"), R(uo, *p))] * (not ahead) + [(R("idn"), R(v, *p))], start=not ahead)
            act(R("sg", *p), au, AF.Sign, bias=1.0 / 512)
            early("chunk%d" % q)
        p, cnt = (64 * h, 64 * h + 64), R("s%d" % h, 0, 32)
        ext(cnt, "z1", R("sg", 512 * h), 32)
        ts(R("dm", p[0], p[1], 2), cnt, 1.0, OP.is_ge)
        scan(R("fs", *p), R("dz", *p), R("dm", *p), 0.0)
        early("half%d" % h)
        if hp == 0:
            cp(R("fu", 32 * h, 32 * h + 32), fl(32 * h, 32 * h + 32))

    def search(h):
        c, bank = (32 * h, 32 * h + 32), "s%d" % h
        tot = R(bank, 32, 64)
        ts(R("on", *c), fl(*c), float(V), OP.is_ge)
        mm(tot, [(R("bo"), R("on", *c))])
        mm(R(bank, 64, 96), [(R("tri"), R("on", *c))])
        for e in range(4):
            scan(R("cb", 128 * h + 32 * e, 128 * h + 32 * e + 32), R("one"), tot, C("cb", 32 * e + 31) if h else -LOW - 16.0 * e)
        for j in range(4):
            o = 512 * h + 128 * j
            ts(R("flg", o, o + 128), R("cb", 128 * h, 128 * h + 128), C("colb", 0), OP.subtract, 64 * j - LOW, OP.is_le)
        scan(R("cq", 512 * h, 512 * h + 512), R("rst"), R("flg", 512 * h, 512 * h + 512), 0.0)
        tt(R("key", *c), R("cb", 128 * h, 128 * h + 32), R(bank, 64, 96), OP.subtract)
        act(R("flm", *c), fl(*c), bias=-1536.0)

    def hops(ui, unit, uo, v):
        steps()
        for h in range(2):
            hop(h, 0, ui, unit, uo, v)
        steps()
        for h in range(2):
            hop(h, 1, uo, "idb", uo, v)
            search(h)

    NF, KK, PK, PRE, L1, L2 = (R("nf", 64 * k, 64 * k + 64) for k in range(6))

    def leave(t, uo, v):
        sn = "sn%d" % t
        ts(C("cn", 8 * t + 3), C("cb", 159), LOW, OP.add, float(CAP), OP.min)
        s = send("ct%d" % t, [C("cn", 8 * t + 3)])
        early("count")
        arrive("a_ct%d" % t, [R("cn", 8 * t + 4, 8 * t + 7)], s, T_CNT)
        tt(R("cs"), R("cq", 31, 512, 32), R("cq", 543, K, 32), OP.add)
        ts(R("cu"), R("cs"), 63.0, OP.min)
        tt(R("oh"), IND(R("key"), R("cu")), R("krow"), OP.is_equal)
        ext(R("s0", 256, 272), "zl", R("oh"), 16, [(R("id16"), R("cs"))])
        tt(R(sn, 512, 768), IND(R("flm"), R("cu")), R("oh"), OP.mult)
        s = send("fm%d" % t, [R(sn, 512, 768)])
        arrive("a_fm%d" % t, [LAND["fm%d" % t]], s, T_RELAY)
        ts(R("atu"), R("s0", 256, 272), float(K - 1), OP.min)
        if t == 0:
            cp(R(sn, 0, 256), IND(R(uo, 0, K), R("atu")))
            act(R(sn, 256, 512), IND(R(v, 0, K), R("atu")), AF.Copy)
        else:
            ts(R(sn, 0, 256), IND(R(uo, 0, K), R("atu")), 2.0, OP.mult, -1.0, OP.add)
            act(R("zr"), IND(R("zz"), R("atu")), scale=-4.0)
        for k, src in enumerate((R(sn, 0, 256), R("zr") if t else R(sn, 256, 512))):
            if FUSE and t == 0:
                s = s if k else send("u0", [R(sn, 0, 512)])
            else:
                s = send("uv"[k] + str(t), [src])
            arrive("a_%s%d" % ("uv"[k], t), [LAND["uv"[k] + str(t)]], s, T_RELAY + 0.4 * (k * t + (FUSE and t == 0)))
        act(R("flq"), fl(), bias=-256.0)
        act(KK, R("key"), bias=2047.0 + LOW + LAND["fm%d" % t][1])
        tt(PK, R("klist", 0, 64), KK, OP.subtract)

    def least(t):
        m = C("mm", t)
        rmin(m, R("cn", 8 * t + 3, 8 * t + 7))
        ts(R("az", 0, 16), R("klist", 0, 16), m, OP.is_ge)
        tt(R("az", 16, 32), R("az", 0, 16), R("klist", 64, 80), OP.mult)
        tt(R("az", 32, 48), R("az", 16, 32), R("s0", 256, 272), OP.max)
        cp(R("a2u"), R("az", 32, 48))
        ts(NF, R("key"), m, OP.subtract, -2048.0 - LOW, OP.is_gt)
        tt(PRE, NF, R("flq"), OP.mult)
        tt(L1, NF, PK, OP.mult)
        tt(L2, L1, KK, OP.add)
        cp(R("loc"), L2)

    def faces(t):
        if t == 0 and SCAT[0]:
            zeros("d2")
            cp(IND(R("d2"), R("a2u")), LAND["fm0"])
        else:
            for q in range(4):
                act(R("gg", 256 * q, 256 * q + 256), IND(R("dd", 0, LAND["fm%d" % t][2]), R("loc", 16 * q, 16 * q + 16)), AF.Copy)
        ext(R("s0", 416, 480), "z1", R("d2" if t == 0 and SCAT[0] else "gg"), 64, [(R("idb"), R("c256")), (R("idf"), PRE)])
        cp(R("fu"), R("s0", 416, 480))
        if t == 0:
            act(fl(), R("s0", 416, 480))

    def followers(w, b, ts_):
        for t in ts_:
            o = 512 * b + 256 * t
            n = 2 * SPAN[b]
            tt(R("pq", o, o + 16 * n), IND(R(w, BL * (b + 1), W), R("gu", o // 16, o // 16 + n)), R("ab", o, o + 16 * n), OP.mult)

    def parts(t, b):
        j0, j1 = jr(t, b)
        o, n = 512 * b + 256 * t + j0 - first(t, b), 16 * SPAN[b]
        return j0, j1, R("pq", o, o + j1 - j0), R("pq", o + n, o + n + j1 - j0)

    def heights0():
        for b in range(4):
            act(R("xs", BL * b, BL * b + BL), IND(R(UA, 0, K), R("so0", 20 * b, 20 * b + 20)), bias=-1.0, scale=2.0)
        for t in (0, 2, 1):
            n = len(range(t, V, 3))
            acc = R("d%d" % min(t, 1), 0, n)
            mm(acc, [(R("idh"), R("h", t, V, 3)), (R("idb"), R("xs", t, V, 3))])
            if t:
                act(R("w0", t, V, 3), acc)
            if t < 2:
                tt(R("wl", t, V, 3), acc, R("lv", t, V, 3), OP.mult)
            else:
                gcopy(R("wl", 2, V, 3), R("w0", 2, V, 3))
        for b in (3, 2, 1, 0):
            followers("w0", b, [0])
            j0, j1, p1, p2 = parts(0, b)
            mm(R("d0", j0, j1), [(R("idf"), R("wl", 3 * j0, 3 * j1 - 2, 3))])
            mm(R("d0", j0, j1), [(R("idf"), p1), (R("idf"), p2)], start=False)
            act(R("w0", 3 * j0, 3 * j1 - 2, 3), R("d0", j0, j1))

    def own(t, b):
        j0, j1 = jr(t, b)
        return 3 * j0 + t, 3 * (j1 - 1) + t + 1, 3

    def local(name, t, b):
        f = own(t, b)
        return R(name, f[0] - BL * b, f[1] - BL * b, 3)

    def halves():
        followers("w1", 3, [0, 1])
        for t in (2, 0, 1):
            acc = R("x3", 128 * t, 128 * t + _n(R("wl", *own(t, 3))))
            mm(acc, [(R("idg"), R("wl", *own(t, 3)))] + [(R("idf"), x) for x in (parts(t, 3)[2:] if t < 2 else ())])
            act(local("c3", t, 3), acc)
        for b in (2, 1, 0):
            mm(R("x%d" % b, 0, BL), [(R("idg"), R("wl", BL * b, BL * b + BL))])

    def heights1():
        win = R("up", 0, 16 + (V if REMAP1 else K))
        tt(R("w1", 3 * BL, V), IND(win, R("so1", 60, 80)), R("c3"), OP.add)
        for b in (2, 1, 0):
            blk = (BL * b, BL * b + BL)
            act(R("xs", *blk), IND(win, R("so1", 20 * b, 20 * b + 20)), AF.Copy)
            mm(R("x%d" % b, 0, BL), [(R("idb"), R("xs", *blk))], start=False)
            act(R("w1", *own(2, b)), local("x%d" % b, 2, b))
        for b in (2, 1, 0):
            followers("w1", b, [0, 1])
            for t in range(2):
                tt(local("x%d" % b, t, b), local("x%d" % b, t, b), parts(t, b)[2], OP.add)
            for t in range(2):
                tt(R("w1", *own(t, b)), local("x%d" % b, t, b), parts(t, b)[3], OP.add)

    tables(0)
    s = send("hs0", [R("h", 0, GH)])
    arrive("a_hs0", [R("hg")], s, T_RELAY + 20)
    UA = "ua" if REMAP else "u"
    collapse(0, R("u", 0, K), ("su0", 0))
    act(R("sall", 0, 80), R("lf", 0, 80))
    perm(R("d1", 128, 156), 1, 0, 84)
    act(R("sall", 80, 108), R("d1", 128, 156))
    tables(1)
    hops("u", "i256", "u", "v")
    leave(0, "u", "v")
    factors(0)
    iota(R("gcol", 0, 2), [[56, 2]], 0, 0)
    iota(R("gcol", 2, 8), [[7, 3], [56, 2]], 6, 0)
    iota(R("grow"), [[BL, 4], [0, 32]], BL, 0)
    iota(R("up", 0, 16), [[0, 16]], 0, 0)
    iota(R("ch"), [[0, 256]], 128, 0)
    for n in sorted(set(SPAN)):
        act(C("col", GL + n), C("under", n), bias=28.0 - n, scale=n - 28.0)
        act(C("col", GL + n), C("col", GL + n), bias=C("col", LANE))
    for b in range(4):
        ts(R("go", 2 * b, 2 * b + 2), R("gcol", 2 * b, 2 * b + 2), C("col", GL + SPAN[b]), OP.add, 111.0, OP.min)
    tt(R("gf"), IND(R("nsb"), R("go")), R("grow"), OP.subtract)
    cp(R("gu"), R("gf"))
    gcopy(R("w0", V, W), R("hg"))
    least(0)
    ts(R("si"), R("sall"), C("mm", 0), OP.add)
    ts(R("sj"), R("si"), K - 1, OP.bitwise_and)
    cp(R("so0"), R("sj"))
    faces(0)
    if REMAP:
        zeros("lw")
        act(C("col", E1), C("under", 1), bias=C("under", 2), scale=-1.0)
        act(C("col", WR), C("col", E1), bias=C("under", 1), scale=float(K))
        act(R("zk"), R("z1"), scale=C("col", WR))
        act(R("kw"), R("jrow"), bias=C("col", E1), scale=C("under", 1))
        cp(IND(R("lw"), R("a2u")), R("kw"))
        act(R("ga", 0, SUB), IND(R("lw", 0, K), R("so0", 80, 107)), AF.Copy)
        ext(R("s1", 0, 27), "zk", R("ga"), 27)
        tt(R("si", 80, 107), R("s1", 0, 27), R("sj", 80, 107), OP.max)
        cp(R("su0", 0, 27), R("si", 80, 107))
    else:
        cp(IND(R("u"), R("a2u")), LAND["u0"])
    for old, new, scat in (("v", "vb", SCAT[1]), ("u", "ua", SCAT[2]))[:1 + REMAP]:
        if scat:
            move(R(new, 0, K), R(old, 0, K))
            cp(IND(R(new), R("a2u")), LAND[old + "0"])
        else:
            for q in range(4):
                act(R(new, 256 * q, 256 * q + 256), IND(R(old), R("loc", 16 * q, 16 * q + 16)), AF.Copy)
    if REMAP:
        collapse(1, R("u"), ("su0", 0))
    else:
        collapse(1, R("u", 0, K), ("so0", 80))
    factors(1)
    heights0()
    s = send("hs1", [R("w0", 0, GH)])
    early("hs1")
    arrive("a_hs1", [R("w1", V, W)], s, T_RELAY + 1)
    ext(R("d0", SUB), "z1", R("lv"), 80)
    hops(UA, "idb", "ub", "vb")
    for c in range(2):
        act(R("up", 16 + 512 * c, 528 + 512 * c), R("ub", 512 * c, 512 * c + 512), bias=-1.0, scale=2.0)
    for q in range(4):
        p, av = (256 * q, 256 * q + 256), R("x%d" % q, 256, 512)
        mm(av, [(R("i256"), R("ch")), (R("idn"), R("vb", *p))])
        tt(R("zz", *p), av, R("up", 16 + p[0], 16 + p[1]), OP.mult)
    leave(1, "ub", "vb")
    for c in range(2):
        act(R("sig", 512 * c, 512 * c + 512), R("zz", 512 * c, 512 * c + 512), AF.Sigmoid, scale=-4.0, extra=1.3 if c == 0 else 0.0)
    halves()
    least(1)
    ts(R("si", 0, 80), R("sall", 0, 80), C("mm", 0), OP.add, C("mm", 1), OP.add)
    ts(R("sj", 0, 80), R("si", 0, 80), K - 1, OP.bitwise_and)
    ts(R("gf", 0, 80), R("sj", 0, 80), 1.0 / 16, OP.mult, 1.0, OP.add)
    if REMAP1:
        cp(R("so0", 0, 80), R("sj", 0, 80))
        for k in range(2):
            iota(R("lw", 512 * k, 512 * k + 512), [[0, 512]], 0, 0)
        act(C("col", WR), C("under", 1), scale=1.0 / 16)
        act(C("col", WR), C("col", E1), bias=C("col", WR), scale=(K + 16) / 16)
        act(R("zk"), R("z1"), scale=C("col", WR))
        cp(IND(R("lw"), R("a2u")), R("kw"))
        for c0, c1 in ((60, 80), (0, 60)):
            for c in range(c1 - 20, c0 - 1, -20):
                act(R("xs", 16 * c, 16 * c + BL), IND(R("lw", 0, K), R("so0", c, c + 20)), AF.Copy)
            ext(R("s1", c0, c1), "zk", R("xs", 16 * c0), c1 - c0)
            tt(R("gf", c0, c1), R("s1", c0, c1), R("gf", c0, c1), OP.max)
            tt(R("gf", c0, c1), R("gf", c0, c1), R("d0", SUB + c0, SUB + c1), OP.mult)
            cp(R("so1", c0, c1), R("gf", c0, c1))
    else:
        tt(R("gf", 0, 80), R("gf", 0, 80), R("d0", SUB), OP.mult)
        cp(R("so1"), R("gf", 0, 80))
        cp(IND(R("up", 16), R("a2u")), LAND["u1"])
    add("s", "act", (IND(R("sig"), R("a2u")), LAND["v1"], AF.Sigmoid, None, None), [IND(R("sig"), R("a2u"))], [LAND["v1"]],
        0.065 + CY * SCA * 256)
    faces(1)
    heights1()
    for b in (3, 2, 1, 0):
        mm(R("d0", 0, BL), [(R("idf"), R("w1", BL * b, BL * b + BL))], start=b == 3)
    act(R("d1"), R("sig", 512, K), AF.Copy)
    for c, (c0, c1) in enumerate(LAST):
        p = (16 * c0, 16 * c1)
        tt(R("plo", *p), IND(R("w1"), R("fu", c0, c1)), R("sig", *p), OP.mult)
        act(R("phi", *p), IND(R("w1"), R("fu", 32 + c0, 32 + c1)), AF.Copy)
        tt(R("d1", *p), R("d1", *p), R("phi", *p), OP.mult)
        tt(R("ow", *p), R("d1", *p), R("plo", *p), OP.add)
        store("y", "st%d" % (1 + c), "yw", p[0], p[1], R("ow", *p))
    act(R("oh2"), R("d0", 0, BL), AF.Copy)
    store("s", "st0", "yh", 0, BL, R("oh2"))
    goes_on = {}
    for n in reversed(nodes):
        if n["kind"] == "mm":
            out, pairs, start, stop = n["args"]
            n["args"] = (out, pairs, start, not goes_on.get(out[0], False))
            goes_on[out[0]] = not start
    return nodes


def _meet(x, y):
    if x[0] != y[0] or x[1] >= y[2] or y[1] >= x[2]:
        return False
    return x[3] != y[3] or (x[1] - y[1]) % x[3] == 0


def schedule(nodes):
    for n in nodes:
        dep = {}
        for m in nodes[:n["id"]]:
            raw = any(_meet(x, y) for x in m["wr"] for y in n["rd"])
            other = any(_meet(x, y) for x in m["wr"] + m["rd"] for y in n["wr"])
            bank = any(_psum(x) and x[0] == y[0] for x in m["wr"] + m["rd"] for y in n["wr"] + n["rd"])
            group = bank and m["kind"] == n["kind"] == "mm" and not n["args"][2]
            if not group and (raw or other or (bank and m["eng"] != n["eng"])):
                dep[m["id"]] = True
            elif bank and n["kind"] == "mm":
                dep[m["id"]] = False
        for m in n["after"]:
            dep[m] = False
        n["dep"] = dep
    lastq = {}
    for n in nodes:
        if n["kind"] in ("load", "move"):
            if n["eng"] in lastq and lastq[n["eng"]] not in n["dep"]:
                n["dep"][lastq[n["eng"]]] = False
            lastq[n["eng"]] = n["id"]

    above = []
    for n in nodes:
        far = 0
        for i, hard in n["dep"].items():
            if hard and nodes[i]["kind"] != "send":
                far |= above[i]
        n["dep"] = {i: hard for i, hard in n["dep"].items() if not far >> i & 1}
        for i, hard in n["dep"].items():
            if hard and nodes[i]["kind"] != "send":
                far |= 1 << i
        above.append(far)

    def gaps(same, costs):
        return [[(i, same[i]["dur"] + (same[i]["lat"] + costs[7 + (nodes[i]["eng"] == n["eng"])] if hard else 0.0))
                 for i, hard in n["dep"].items()] for n in nodes]

    before = gaps(nodes, COSTS[0])
    others = [(same, gaps(same, costs)) for same, costs in [(nodes, COSTS[0])] + [(build(c), c) for c in COSTS[1:]]]
    after = [[] for n in nodes]
    for n in nodes:
        for i, d in before[n["id"]]:
            after[i].append((n["id"], d))
    chain = [0.0] * len(nodes)
    for n in reversed(nodes):
        k = n["id"]
        chain[k] = max([d + chain[i] for i, d in after[k]] + [n["dur"] + n["lat"]]) + EARLY.get(n["tag"], 0.0)

    def flow():
        at, free, wait = [0.0] * len(nodes), {"a": 0.0}, [len(x) for x in before]
        ready = {i: 0.0 for i, c in enumerate(wait) if not c}
        while ready:
            can = {i: max(t, free.get(nodes[i]["eng"], 0.0)) for i, t in ready.items()}
            k = min(can, key=lambda i: (can[i], -chain[i], i))
            k = max((i for i in can if nodes[i]["eng"] == nodes[k]["eng"] and can[i] <= can[k] + SLACK), key=lambda i: (chain[i], -i))
            at[k] = can[k]
            del ready[k]
            if nodes[k]["eng"] != "a":
                free[nodes[k]["eng"]] = at[k] + nodes[k]["dur"]
            for i, d in after[k]:
                wait[i] -= 1
                if not wait[i]:
                    ready[i] = max(at[j] + d for j, d in before[i])
        return at

    def pack(at, back):
        need, frees = (after, before) if back else (before, after)
        busy, new, wait = {}, [0.0] * len(nodes), [len(x) for x in need]
        ready = [i for i, c in enumerate(wait) if not c]
        while ready:
            k = min(ready, key=lambda i: (-at[i] - nodes[i]["dur"], -i) if back else (at[i], i))
            ready.remove(k)
            dur = nodes[k]["dur"]
            if back:
                t = max([d - new[i] for i, d in need[k]] + [dur + nodes[k]["lat"]]) - dur
            else:
                t = max([new[i] + d for i, d in need[k]] + [0.0])
            if nodes[k]["eng"] != "a":
                q = busy.setdefault(nodes[k]["eng"], [])
                pos = len(q)
                while pos and q[pos - 1][1] > t:
                    pos -= 1
                while pos < len(q) and t + dur > q[pos][0] + 1e-9:
                    t = max(t, q[pos][1])
                    pos += 1
                q.insert(pos, (t, t + dur))
            new[k] = -t - dur if back else t
            for i, d in frees[k]:
                wait[i] -= 1
                if not wait[i]:
                    ready.append(i)
        return new

    eng = ["vstgy".find(n["eng"]) if n["eng"] != "a" else n["id"] for n in nodes]
    ends = [k for k in range(len(nodes)) if not after[k]]
    rows = [([n["dur"] for n in same], [n["dur"] + n["lat"] for n in same], need) for same, need in others]

    def play(order, row, same=0, old=None):
        dur, tail, need = row
        t, held = (list(old[1]), list(old[2])) if old else ([0.0] * len(order), [0] * len(order))
        free, last = [0.0] * len(nodes), [0] * len(nodes)
        for k in order[max(0, same - 200):same]:
            free[eng[k]], last[eng[k]] = t[k] + dur[k], k
        for k in order[same:]:
            e = eng[k]
            s, by = free[e], ~last[e]
            for i, d in need[k]:
                if t[i] + d >= s:
                    s, by = t[i] + d, i
            t[k], held[k], free[e], last[e] = s, by, s + dur[k], k
        final = max(ends, key=lambda k: t[k] + tail[k])
        return t[final] + tail[final], t, held, final

    at = flow()
    for it in range(PASSES):
        at = pack(pack(at, True), False)
    roots = []
    for n in nodes:
        roots.append(sum(1 << i for i in n["dep"]))
        for i in n["dep"]:
            roots[-1] |= roots[i]
    order = best = sorted(range(len(nodes)), key=lambda i: (at[i], i))
    plays = [play(order, row) for row in rows]
    least, seed = sum(x[0] for x in plays), SEED
    for it in range(TRIES):
        seed = (seed * 1103515245 + 12345) % 2 ** 31
        end, t, held, k = plays[(seed >> 8) % len(rows)]
        pairs = []
        while t[k] > 0:
            if held[k] < 0 and not roots[k] >> ~held[k] & 1:
                pairs.append((~held[k], k))
            k = max(held[k], ~held[k])
        a, b = pairs[(seed >> 12) % len(pairs)]
        pa, pb = order.index(a), order.index(b)
        if it % 4 < 2:
            trial = (order[:pa] + [i for i in order[pa:pb] if roots[b] >> i & 1] + [b]
                     + [i for i in order[pa:pb] if not roots[b] >> i & 1] + order[pb + 1:])
        elif it % 4 == 2:
            stop = max([order.index(i) for i, d in before[a]] + [-1]) + 1
            if stop >= pa:
                continue
            to = stop + (seed >> 4) % (pa - stop)
            trial, pa = order[:to] + [a] + order[to:pa] + order[pa + 1:], to
        else:
            stop = min([order.index(i) for i, d in after[a]] + [len(order)])
            if stop <= pb:
                continue
            to = pb + 1 + (seed >> 4) % (stop - pb)
            trial = order[:pa] + order[pa + 1:to] + [a] + order[to:]
        seed = (seed * 1103515245 + 12345) % 2 ** 31
        allowed, got = -(HEAT * (1 - it / TRIES) + 0.01) * math.log((seed + 1) / 2 ** 31), []
        for row, old in zip(rows, plays):
            got.append(play(trial, row, pa, old))
            allowed -= got[-1][0] - old[0]
            if allowed < -0.3:
                break
        if allowed >= 0:
            order, plays = trial, got
            if sum(x[0] for x in got) < least:
                best, least = trial, sum(x[0] for x in got)
    at = play(best, rows[0])[1]
    nodes[0]["spans"] = [play(best, row)[0] for row in rows]
    for n in nodes:
        n["t"] = at[n["id"]]
    return [nodes[i] for i in best]


_ORDER = []


def _order():
    if not _ORDER:
        _ORDER.extend(schedule(build()))
    return _ORDER


def _mask(engines):
    return sum(1 << e for e in engines)


def routes(T, topo):
    cores, n = T.cores, len(T.cores)
    out = {}
    for r, c in enumerate(cores):
        nxt, prv = (r + 1) % n, (r - 1) % n
        own = [x for x in topo.cores_of(c) if x != c and topo.may_write(x, cores[nxt]) and topo.may_write(x, cores[prv])]
        near = [x for x in own if topo.die(x) == topo.die(c)]
        far = [x for x in own if topo.die(x) != topo.die(c)]

        def beside(d):
            return [x for x in range(NCORES) if topo.mates(x, cores[d]) and topo.die(x) == topo.die(c)
                    and topo.may_write(x, cores[d]) and topo.may_write(c, x)][0]

        for t in range(2):
            src, land, buf = (("h", ("hg", 0), "yb"), ("w0", ("w1", V), "yf"))[t]
            out[r, "hs%d" % t] = [(x, R(src, 128 * k, 128 * k + 128), R(buf, 0, 128),
                                   [(prv, R(land[0], land[1] + 128 * k, land[1] + 128 * k + 128), "a_hs%d" % t)])
                                  for k, x in enumerate((beside(prv), near[0], near[1], far[0]))]
            mine = C("cn", 8 * t + 3)
            to = [(d, C("cn", 8 * t + 3 + (d - r) % n), "a_ct%d" % t) for d in range(n) if d != r]
            out[r, "ct%d" % t] = ([(None, mine, None, [x]) for x in to if topo.may_write(c, cores[x[0]])]
                                  + [(near[1], mine, C("yf", 128 + 4 * t), [x for x in to if not topo.may_write(c, cores[x[0]])])])
            keep = R("yb", 128 + 256 * t, 384 + 256 * t)
            out[r, "fm%d" % t] = [(near[1], R("sn%d" % t, 512, 768), keep, [(nxt, LAND["fm%d" % t], "a_fm%d" % t)])]
            out[r, "u%d" % t] = [(near[0], R("sn%d" % t, 0, 256), keep, [(nxt, LAND["u%d" % t], "a_u%d" % t)])]
            src, keep = ((R("sn0", 256, 512), keep), (R("zr"), R("yf", 144)))[t]
            out[r, "v%d" % t] = [(far[0], src, keep, [(nxt, LAND["v%d" % t], "a_v%d" % t)])]
        if FUSE:
            out[r, "u0"] += out.pop((r, "v0"))
    return out


def _deal(src, dsts, topo):
    can = [topo.engines(src, d) for d in dsts]
    every = sorted(set(e for x in can for e in x))
    share = 1
    while share * 2 * len(dsts) <= len(every):
        share *= 2
    used, got = set(), [None] * len(dsts)
    for i in sorted(range(len(dsts)), key=lambda i: len(can[i])):
        got[i] = [e for e in can[i] if e not in used][:share]
        used.update(got[i])
    return got


def _firsts(pieces, T):
    return [x if x is not None else T.cores[to[0][0]] for x, s, k, to in pieces]


def rank_program(g, core, T, topo):
    order = _order()
    msgs = [n["args"][0] for n in order if n["kind"] == "send"]
    way = routes(T, topo)
    cores = T.cores

    def ap(x):
        if not isinstance(x, tuple):
            return x
        if x[0] == "@":
            return ap(x[1]).indirect(ap(x[2]))
        return T[x[0]][:, x[1]:x[2]] if x[3] == 1 else T[x[0]][:, x[1]:x[2]:x[3]]

    def did(dst):
        rid, pid = topo.addr(dst, core)
        return DstId(rid=rid, pnc=pid)

    rank = T.rank_of(core)
    if rank is None:
        sent = 0
        for msg in msgs:
            for r in range(len(cores)):
                pieces = way[r, msg]
                for (x, src, keep, to), eng in zip(pieces, _deal(cores[r], _firsts(pieces, T), topo)):
                    if x != core:
                        continue
                    g.wait_ge(T.sem["y_" + msg], len(eng))
                    on = topo.engines(core, cores[to[0][0]])
                    g.remote_dma_fused([RemoteDMATransfer(dst_ids=[did(cores[d]) for d, l, s in to], dma_engine_mask=_mask(on),
                                                          remote_sem=T.sem[to[0][2]], srcs=[ap(keep)], dsts=[ap(l) for d, l, s in to])],
                                       local_sem=T.sem.sent)
                    sent += len(on)
        if sent:
            g.wait_ge(T.sem.sent, sent)
        return

    due = {}
    for (r, msg), pieces in way.items():
        for (x, src, keep, to), eng in zip(pieces, _deal(cores[r], _firsts(pieces, T), topo)):
            for d, l, s in to:
                if d == rank:
                    due[s] = due.get(s, 0) + (len(eng) if x is None else len(topo.engines(x, core)))

    queue = {"v": g.vector, "s": g.scalar, "t": g.tensor, "g": g, "y": g.sync}
    count = {"v": 0, "s": 0, "t": 0, "g": 0}
    known = {q: {} for q in queue}
    mark, seen = {}, {}
    tail, sent = [], 0
    for n in order:
        kind, a, e = n["kind"], n["args"], n["eng"]
        if kind == "arrive":
            mark[n["id"]] = (a[0], due[a[0]])
            seen[n["id"]] = {}
            continue
        q, kn = queue[e], known[e]
        need = sorted((i for i, hard in n["dep"].items() if hard and i in mark), key=lambda i: -mark[i][1])
        for i in need:
            s, val = mark[i]
            if kn.get(s, 0) < val:
                q.wait_ge(T.sem[s], val)
                kn[s] = val
                for s2, v2 in seen[i].items():
                    kn[s2] = max(kn.get(s2, 0), v2)
        seen[n["id"]] = dict(kn)
        if kind == "load":
            q.dma_start(ap(a[1]), T[a[0]][:]).then_inc(T.sem["l_" + a[0]], 16)
            mark[n["id"]] = ("l_" + a[0], 16)
            continue
        if kind == "move":
            q.dma_start(ap(a[1]), ap(a[2])).then_inc(T.sem[a[0]], 16)
            mark[n["id"]] = (a[0], 16)
            continue
        if kind == "store":
            q.dma_start(T[a[1]][:, a[2]:a[3]], ap(a[4])).then_inc(T.sem[a[0]], 16)
            tail.append(a[0])
            continue
        if kind == "send":
            pieces = way[rank, a[0]]
            firsts = _firsts(pieces, T)
            deal = _deal(core, firsts, topo)
            g.remote_dma_fused([RemoteDMATransfer(dst_ids=[did(f)], dma_engine_mask=_mask(eng),
                                                  remote_sem=T.sem[to[0][2] if x is None else "y_" + a[0]],
                                                  src=ap(src), dst=ap(to[0][1] if x is None else keep))
                                for (x, src, keep, to), f, eng in zip(pieces, firsts, deal)], local_sem=T.sem.sent)
            sent += sum(len(x) for x in deal)
            continue
        if kind == "tt":
            i = q.tensor_tensor(ap(a[0]), ap(a[1]), ap(a[2]), a[3])
        elif kind == "ts":
            if a[5] is None:
                i = q.tensor_scalar(ap(a[0]), ap(a[1]), ap(a[2]), None, a[4])
            else:
                i = q.tensor_scalar(ap(a[0]), ap(a[1]), ap(a[2]), ap(a[3]), a[4], a[5])
        elif kind == "cp":
            i = q.tensor_copy(ap(a[0]), ap(a[1]))
        elif kind == "ms":
            i = q.memset(ap(a[0]), a[1])
        elif kind == "scan":
            i = q.tensor_tensor_scan(ap(a[0]), ap(a[1]), ap(a[2]), ap(a[3]), OP.mult, OP.add)
        elif kind == "rmin":
            i = q.tensor_reduce(ap(a[0]), ap(a[1]), AxisListType.X, OP.min)
        elif kind == "act":
            if a[3] is None:
                i = q.activation(ap(a[0]), ap(a[1]), a[2])
            else:
                i = q.activation(ap(a[0]), ap(a[1]), a[2], bias=ap(a[3]), scale=ap(a[4]))
        elif kind == "mm":
            for k, (l, r) in enumerate(a[1]):
                i = q.matmul(ap(a[0]), ap(l), ap(r), a[2] and k == 0, a[3] and k == len(a[1]) - 1)
        elif kind == "iota":
            if _SB[a[0][0]][0] == I32:
                i = q.iota(ap(a[0]), a[1], a[2], a[3])
            else:
                i = q.iota(ap(a[0]), a[1], a[2], a[3], allow_small_or_imprecise_dtypes=True)
        else:
            i = q.affine_select(ap(a[0]), ap(a[1]), a[2], a[3], a[4], a[5], a[6])
        count[e] += 1
        i.then_inc(T.sem["e" + e], 1)
        mark[n["id"]] = ("e" + e, count[e])
    for s in tail:
        g.sync.wait_ge(T.sem[s], 16)
    for e, c in count.items():
        g.sync.wait_ge(T.sem["e" + e], c)
    g.wait_ge(T.sem.sent, sent)
